import numpy as np
import ml_dtypes


def mxq(x, axis, fmt="e4m3"):
    dtype, down = {"e4m3": (ml_dtypes.float8_e4m3fn, 7), "e5m2": (ml_dtypes.float8_e5m2, 14)}[fmt]
    v = np.moveaxis(np.asarray(x, np.float32).astype(ml_dtypes.bfloat16).astype(np.float64), axis, -1)
    blocks = v.reshape(v.shape[:-1] + (-1, 32))
    amax = np.abs(blocks).max(-1, keepdims=True)
    byte = np.maximum(np.where(amax > 0, np.frexp(amax)[1] - 1 + 127, 0) - down, 1)
    scale = np.exp2(byte - 127.0)
    codes = (blocks / scale).astype(np.float32).astype(dtype).astype(np.float64)
    return np.moveaxis((codes * scale).reshape(v.shape), -1, axis)


WIDE = False


def mx_kscale(k):
    if not WIDE:
        return np.ones(k)
    levels = np.array([10, -10, 5, -5, 0])
    if k % 512:
        return np.exp2(np.random.permutation(np.resize(levels, k // 32))).repeat(32)
    a = np.empty((k // 512, 16))
    for p in range(k // 512):
        a[p, :8] = np.random.permutation(np.resize(levels, 8))
        for g in range(8):
            far = levels[np.abs(levels - a[p, g]) >= 10]
            a[p, g + 8] = far[np.random.randint(len(far))]
    return np.exp2(a.ravel()).repeat(32)


def f64(x):
    return np.asarray(x).astype(np.float64)


def striped(idx):
    return np.tile(idx.reshape(-1, 16).T, (8, 1)).astype(np.uint16)


def unstriped(offs):
    return offs[:16].T.reshape(-1).astype(np.int64)


E2M1 = np.array([0.0, 0.5, 1.0, 1.5, 2.0, 3.0, 4.0, 6.0, -0.0, -0.5, -1.0, -1.5, -2.0, -3.0, -4.0, -6.0])


def pack_fp4(w):
    k, n = w.shape
    w = f64(np.asarray(w, np.float32).astype(ml_dtypes.bfloat16)).reshape(k // 32, 32, n)
    amax = np.abs(w).max(1)
    mant, ex = np.frexp(amax / 6.0)
    byte = np.clip(np.where(amax > 0, np.where(mant > 0.5, ex, ex - 1) + 127, 1), 1, 254)
    scaled = (w * np.exp2(127.0 - byte)[:, None, :]).reshape(k, n).astype(np.float32)
    c = np.ascontiguousarray(scaled.reshape(k // 512, 128, 4, n).transpose(0, 1, 3, 2)).astype(ml_dtypes.float4_e2m1fn).view(np.uint8) & 0xF
    words = (c[..., 0::2] | (c[..., 1::2] << 4)).reshape(k // 512, 128, 2 * n)
    return np.ascontiguousarray(words), np.ascontiguousarray(byte.astype(np.uint8).reshape(k // 512, 16, n))


def unpack_fp4(words, scales):
    g, _, n = scales.shape
    words = np.ascontiguousarray(words).reshape(g, 128, n, 2)
    nib = np.empty((g, 128, n, 4), np.uint8)
    nib[..., 0::2] = words & 0xF
    nib[..., 1::2] = words >> 4
    vals = E2M1[nib] * np.repeat(np.exp2(scales.astype(np.float64) - 127.0), 8, axis=1)[..., None]
    return vals.transpose(0, 1, 3, 2).reshape(g * 512, n)


def silu(v):
    return v / (1.0 + np.exp(-np.maximum(v, -700.0)))


K, T, S, H, N, U = 512, 2048, 1024, 512, 128, 1024


def setup_inputs():
    n = np.random.standard_normal
    s = mx_kscale(K)[:, None]
    u = mx_kscale(H)
    packed_w3 = pack_fp4(n((H, N)) / np.sqrt(H) / u[:, None])
    return {
        "xT": (n((K, T)) * s).astype(np.float32),
        "w1": (n((K, H)) / np.sqrt(2 * K) / s * u).astype(np.float32),
        "w2": (n((K, H)) / np.sqrt(2 * K) / s * u).astype(np.float32),
        "w3_words": packed_w3[0],
        "w3_scales": packed_w3[1],
        "offs": striped(np.random.permutation(T)[:S]),
        "src": striped(np.random.permutation(S)[(S * np.random.uniform(0, 1, U) ** 4).astype(np.int64)]),
        "dst": striped(np.random.permutation(S)),
    }


def reference(xT, w1, w2, w3_words, w3_scales, offs, src, dst):
    xq = mxq(f64(xT)[:, unstriped(offs)], 0, "e4m3")
    y = mxq(f64(w1), 0, "e4m3").T @ xq
    e = mxq(f64(w2), 0, "e4m3").T @ xq
    z = silu(y[:, unstriped(src)] + e[:, unstriped(dst)])
    return unpack_fp4(w3_words, w3_scales).T @ mxq(z, 0, "e4m3")

@@ -1,0 +1,237 @@
+from contextlib import ExitStack
+
+import concourse.mybir as mybir
+
+F32 = mybir.dt.float32
+BF16 = mybir.dt.bfloat16
+U32 = mybir.dt.uint32
+I32 = mybir.dt.int32
+U16 = mybir.dt.uint16
+U8 = mybir.dt.uint8
+FP8X4 = mybir.dt.float8_e4m3fn_x4
+FP4X4 = mybir.dt.float4_e2m1fn_x4
+ADD = mybir.AluOpType.add
+SILU = mybir.ActivationFunctionType.Silu
+
+K, T, S, H, N = 512, 2048, 1024, 512, 128
+P = 128
+PACK = 4
+FLOPS = 2 * K * H * S * 2 + 2 * H * N * S
+
+X_CHUNK = 512
+LAST_SPLIT = 352
+NODE_PIECES = ((0, 512), (512, 256), (768, 256))
+EDGE_CHUNKS = ((0, 640), (640, 256), (896, 128))
+BANK = 512
+
+
+def powers_of_two(n):
+    out = []
+    start = 0
+    for size in (512, 256, 128):
+        if n - start >= size:
+            out.append((start, size))
+            start = start + size
+    return out
+
+
+def tile_picked_hub_silu_e_kernel(tc, xT, w1, w2, w3_words, w3_scales, offs, src, dst, out):
+    nc = tc.nc
+    with ExitStack() as ctx:
+        keep = ctx.enter_context(tc.tile_pool(name="keep", bufs=1))
+        psum = ctx.enter_context(tc.psum_pool(name="psum", bufs=6))
+        psum_out = ctx.enter_context(tc.psum_pool(name="psum_out", bufs=2))
+
+        offs_t = keep.tile([P, S // 16], U16, name="offs_t")
+        src_t = keep.tile([P, S // 16], U16, name="src_t")
+        dst_t = keep.tile([P, S // 16], U16, name="dst_t")
+        w3_codes = keep.tile([P, 2 * N], U8, name="w3_codes", align_bytes=64)
+        w3_plane = keep.tile([P, N], U8, name="w3_plane", align_bytes=64)
+        nc.gpsimd.memset(w3_plane[:], 0)
+
+        x_rows = xT.rearrange("(p j) c -> p j c", j=PACK)
+        x_raw = {}
+        for u in range(2):
+            for c in range(T // X_CHUNK):
+                raw = keep.tile([P, 2, X_CHUNK], F32, name=f"x_raw{u}_{c}")
+                nc.sync.dma_start(out=raw[:], in_=x_rows[:, 2 * u : 2 * u + 2, c * X_CHUNK : (c + 1) * X_CHUNK])
+                x_raw[u, c] = raw
+                if u == 0 and c == 0:
+                    nc.sync.dma_start(offs_t[:], offs)
+        w_raw = []
+        for i, w in enumerate((w1, w2)):
+            raw = keep.tile([P, PACK, H], F32, name=f"w_raw{i}")
+            nc.sync.dma_start(out=raw[:], in_=w.rearrange("(p j) c -> p j c", j=PACK))
+            w_raw.append(raw)
+        nc.sync.dma_start(src_t[:], src)
+        nc.sync.dma_start(dst_t[:], dst)
+        nc.sync.dma_start(out=w3_codes[:].bitcast(I32), in_=w3_words[0].bitcast(I32))
+        for q in range(4):
+            nc.sync.dma_start(
+                out=w3_plane[32 * q : 32 * q + 4, :].bitcast(I32),
+                in_=w3_scales[0, 4 * q : 4 * q + 4, :].bitcast(I32),
+            )
+
+        pairs = [keep.tile([P, T, 2], BF16, name=f"pairs{u}", align_bytes=64) for u in range(2)]
+        picked = [keep.tile([P, n, PACK], BF16, name=f"picked{i}", align_bytes=64) for i, (s0, n) in enumerate(NODE_PIECES)]
+        x_codes = keep.tile([P, S], U32, name="x_codes", align_bytes=64)
+        x_plane = keep.tile([P, S], U8, name="x_plane", align_bytes=64)
+
+        def round_pairs(copy, u, c, lo, hi):
+            copy(out=pairs[u][:, c * X_CHUNK + lo : c * X_CHUNK + hi, :], in_=x_raw[u, c][:, :, lo:hi].rearrange("p e c -> p c e"))
+
+        def gather_pairs(u, i):
+            s0, n = NODE_PIECES[i]
+            window = pairs[u][:].rearrange("p c e -> p (c e)").bitcast(U32)
+            words = picked[i][:].rearrange("p c j -> p (c j)").bitcast(U32)
+            nc.vector.tensor_copy(words[:, u : 2 * n : 2], window.indirect(offs_t[:, s0 // 16 : (s0 + n) // 16]))
+
+        def quantize_nodes(i):
+            s0, n = NODE_PIECES[i]
+            nc.vector.quantize_mx(
+                out=x_codes[:, s0 : s0 + n].bitcast(FP8X4), scales=x_plane[:, s0 : s0 + n], in_=picked[i][:].rearrange("p c j -> p (c j)")
+            )
+
+        n_chunks = T // X_CHUNK
+        for c in range(n_chunks):
+            round_pairs(nc.vector.tensor_copy, 0, c, 0, X_CHUNK)
+        for i in range(len(NODE_PIECES)):
+            gather_pairs(0, i)
+        for c in range(n_chunks - 1):
+            round_pairs(nc.scalar.copy, 1, c, 0, X_CHUNK)
+        round_pairs(nc.vector.tensor_copy, 1, n_chunks - 1, 0, LAST_SPLIT)
+        round_pairs(nc.scalar.copy, 1, n_chunks - 1, LAST_SPLIT, X_CHUNK)
+
+        w_grouped = {}
+        w_codes = {}
+        w_plane = {}
+        for i in range(2):
+            for h in range(2):
+                w_grouped[i, h] = keep.tile([P, 2, P, PACK], BF16, name=f"w_grouped{i}_{h}", align_bytes=64)
+                w_codes[i, h] = keep.tile([P, 2 * P], U32, name=f"w_codes{i}_{h}", align_bytes=64)
+                w_plane[i, h] = keep.tile([P, 2 * P], U8, name=f"w_plane{i}_{h}", align_bytes=64)
+
+        def round_weights(i, h):
+            nc.scalar.copy(
+                out=w_grouped[i, h][:].rearrange("p t m j -> p m j t"),
+                in_=w_raw[i][:].rearrange("p j (m t) -> p m j t", t=PACK)[:, :, :, 2 * h : 2 * h + 2],
+            )
+
+        def quantize_weights(i, h):
+            nc.vector.quantize_mx(
+                out=w_codes[i, h][:].bitcast(FP8X4), scales=w_plane[i, h][:], in_=w_grouped[i, h][:].rearrange("p t m j -> p (t m j)")
+            )
+
+        parts = {}
+        for i in range(2):
+            for t in range(PACK):
+                parts[i, t] = keep.tile([P, S], F32, name=f"part{i}_{t}")
+
+        def first_product(i, t, s0, n):
+            cols = slice((t % 2) * P, (t % 2 + 1) * P)
+            acc = psum.tile([P, n], F32, name="acc")
+            nc.tensor.matmul_mx(
+                out=acc[:],
+                lhsT=w_codes[i, t // 2][:, cols].bitcast(FP8X4),
+                lhsT_scale=w_plane[i, t // 2][:, cols],
+                rhs=x_codes[:, s0 : s0 + n].bitcast(FP8X4),
+                rhs_scale=x_plane[:, s0 : s0 + n],
+                start=True,
+                stop=True,
+            )
+            nc.scalar.copy(out=parts[i, t][:, s0 : s0 + n], in_=acc[:])
+
+        gather_pairs(1, 0)
+        gather_pairs(1, 1)
+        quantize_nodes(0)
+        round_weights(0, 0)
+        gather_pairs(1, 2)
+        quantize_weights(0, 0)
+        quantize_nodes(1)
+        quantize_nodes(2)
+        for s0, n in NODE_PIECES:
+            first_product(0, 0, s0, n)
+        round_weights(1, 0)
+        quantize_weights(1, 0)
+        for i, t in ((1, 0), (0, 1), (1, 1)):
+            for s0 in (0, BANK):
+                first_product(i, t, s0, BANK)
+        for i in range(2):
+            round_weights(i, 1)
+            quantize_weights(i, 1)
+        for t in (2, 3):
+            for s0 in (0, BANK):
+                first_product(0, t, s0, BANK)
+        for s0 in (0, BANK):
+            for t in (2, 3):
+                first_product(1, t, s0, BANK)
+
+        sums_low = keep.tile([P, 2, S], F32, name="sums_low")
+        sums_high = [keep.tile([P, 2, n], F32, name=f"sums_high{ci}") for ci, (r0, n) in enumerate(EDGE_CHUNKS)]
+        zs = [keep.tile([P, n, PACK], BF16, name=f"z{ci}", tag=f"z{ci}", align_bytes=64) for ci, (r0, n) in enumerate(EDGE_CHUNKS)]
+        widest = max(BANK, max(n for r0, n in EDGE_CHUNKS))
+        sources = [keep.tile([P, widest], F32, name=f"source{b}") for b in range(3)]
+
+        items = [(t, r0, BANK, sums_low[:, t, r0 : r0 + BANK]) for t in (0, 1) for r0 in (0, BANK)]
+        for ci, (r0, n) in enumerate(EDGE_CHUNKS):
+            items.extend((t, r0, n, sums_high[ci][:, t - 2, :]) for t in (2, 3))
+        held = {}
+
+        def fetch_source(k, into):
+            t, r0, n, total = items[k]
+            held[k] = into[:, 0:n]
+            nc.vector.tensor_copy(held[k], parts[0, t][:].indirect(src_t[:, r0 // 16 : (r0 + n) // 16]))
+
+        def add_target(k):
+            t, r0, n, total = items[k]
+            nc.vector.tensor_tensor(total, parts[1, t][:].indirect(dst_t[:, r0 // 16 : (r0 + n) // 16]), held[k], ADD)
+
+        def activate(ci, h, sums):
+            nc.scalar.activation(zs[ci][:, :, 2 * h : 2 * h + 2], sums.rearrange("p t c -> p c t"), SILU)
+
+        z_codes = keep.tile([P, S], U32, name="z_codes", align_bytes=64)
+        z_plane = keep.tile([P, S], U8, name="z_plane", align_bytes=64)
+
+        def second_product(ci):
+            r0, n = EDGE_CHUNKS[ci]
+            for s0, size in powers_of_two(n):
+                cols = slice(r0 + s0, r0 + s0 + size)
+                nc.vector.quantize_mx(
+                    out=z_codes[:, cols].bitcast(FP8X4),
+                    scales=z_plane[:, cols],
+                    in_=zs[ci][:, s0 : s0 + size, :].rearrange("p c t -> p (c t)"),
+                )
+            result = keep.tile([P, n], F32, name=f"result{ci}")
+            for s0, size in powers_of_two(n):
+                cols = slice(r0 + s0, r0 + s0 + size)
+                acc = psum_out.tile([P, size], F32, name="acc_out")
+                nc.tensor.matmul_mx(
+                    out=acc[:],
+                    lhsT=w3_codes[:].bitcast(FP4X4),
+                    lhsT_scale=w3_plane[:],
+                    rhs=z_codes[:, cols].bitcast(FP8X4),
+                    rhs_scale=z_plane[:, cols],
+                    start=True,
+                    stop=True,
+                )
+                nc.scalar.copy(out=result[:, s0 : s0 + size], in_=acc[:])
+            nc.sync.dma_start(out=out[:, r0 : r0 + n], in_=result[:])
+
+        last = len(items) - 1
+        fetch_source(0, sources[0])
+        for k in range(len(items)):
+            if k + 1 < last:
+                fetch_source(k + 1, sources[(k + 1) % len(sources)])
+            elif k + 1 == last:
+                second_product(0)
+                late = keep.tile([P, items[last][2]], F32, name="late", tag="z0", align_bytes=64)
+                fetch_source(last, late)
+            add_target(k)
+            if k == 3:
+                for ci, (r0, n) in enumerate(EDGE_CHUNKS):
+                    activate(ci, 0, sums_low[:, :, r0 : r0 + n])
+            if k > 3 and k % 2 == 1:
+                ci = (k - 4) // 2
+                activate(ci, 1, sums_high[ci][:])
+        for ci in range(1, len(EDGE_CHUNKS)):
+            second_product(ci)

@@ -18,10 +18,11 @@ P = 128
 PACK = 4
 FLOPS = 2 * K * H * S * 2 + 2 * H * N * S
 
-X_CHUNK = 512
-LAST_SPLIT = 352
+X_CHUNKS = (((0, 1024), (1024, 512), (1536, 512)), ((0, 512), (512, 512), (1024, 512), (1536, 512)))
+SOURCE_WINDOW = 1408
+TARGET_WINDOW = 1040
 NODE_PIECES = ((0, 512), (512, 256), (768, 256))
-EDGE_CHUNKS = ((0, 640), (640, 256), (896, 128))
+EDGE_CHUNKS = ((0, 384), (384, 256), (640, 256), (896, 128))
 BANK = 512
 
 
@@ -52,17 +53,19 @@ def tile_picked_hub_silu_e_kernel(tc, xT, w1, w2, w3_words, w3_scales, offs, src
         x_rows = xT.rearrange("(p j) c -> p j c", j=PACK)
         x_raw = {}
         for u in range(2):
-            for c in range(T // X_CHUNK):
-                raw = keep.tile([P, 2, X_CHUNK], F32, name=f"x_raw{u}_{c}")
-                nc.sync.dma_start(out=raw[:], in_=x_rows[:, 2 * u : 2 * u + 2, c * X_CHUNK : (c + 1) * X_CHUNK])
+            for c, (c0, width) in enumerate(X_CHUNKS[u]):
+                raw = keep.tile([P, 2, width], F32, name=f"x_raw{u}_{c}")
+                nc.sync.dma_start(out=raw[:], in_=x_rows[:, 2 * u : 2 * u + 2, c0 : c0 + width])
                 x_raw[u, c] = raw
                 if u == 0 and c == 0:
                     nc.sync.dma_start(offs_t[:], offs)
-        w_raw = []
-        for i, w in enumerate((w1, w2)):
-            raw = keep.tile([P, PACK, H], F32, name=f"w_raw{i}")
-            nc.sync.dma_start(out=raw[:], in_=w.rearrange("(p j) c -> p j c", j=PACK))
-            w_raw.append(raw)
+        w1_raw = []
+        for u in range(2):
+            raw = keep.tile([P, 2, H], F32, name=f"w1_raw{u}")
+            nc.sync.dma_start(out=raw[:], in_=w1.rearrange("(p j) c -> p j c", j=PACK)[:, 2 * u : 2 * u + 2, :])
+            w1_raw.append(raw)
+        w2_raw = keep.tile([P, PACK, H], F32, name="w2_raw")
+        nc.sync.dma_start(out=w2_raw[:], in_=w2.rearrange("(p j) c -> p j c", j=PACK))
         nc.sync.dma_start(src_t[:], src)
         nc.sync.dma_start(dst_t[:], dst)
         nc.sync.dma_start(out=w3_codes[:].bitcast(I32), in_=w3_words[0].bitcast(I32))
@@ -74,11 +77,15 @@ def tile_picked_hub_silu_e_kernel(tc, xT, w1, w2, w3_words, w3_scales, offs, src
 
         pairs = [keep.tile([P, T, 2], BF16, name=f"pairs{u}", align_bytes=64) for u in range(2)]
         picked = [keep.tile([P, n, PACK], BF16, name=f"picked{i}", align_bytes=64) for i, (s0, n) in enumerate(NODE_PIECES)]
-        x_codes = keep.tile([P, S], U32, name="x_codes", align_bytes=64)
+        x_codes = {0: keep.tile([P, BANK], U32, name="x_codes0", align_bytes=64)}
         x_plane = keep.tile([P, S], U8, name="x_plane", align_bytes=64)
 
+        def node_codes(s0, n):
+            return x_codes[s0 // BANK][:, s0 % BANK : s0 % BANK + n].bitcast(FP8X4)
+
         def round_pairs(copy, u, c, lo, hi):
-            copy(out=pairs[u][:, c * X_CHUNK + lo : c * X_CHUNK + hi, :], in_=x_raw[u, c][:, :, lo:hi].rearrange("p e c -> p c e"))
+            c0 = X_CHUNKS[u][c][0]
+            copy(out=pairs[u][:, c0 + lo : c0 + hi, :], in_=x_raw[u, c][:, :, lo:hi].rearrange("p e c -> p c e"))
 
         def gather_pairs(u, i):
             s0, n = NODE_PIECES[i]
@@ -89,33 +96,42 @@ def tile_picked_hub_silu_e_kernel(tc, xT, w1, w2, w3_words, w3_scales, offs, src
         def quantize_nodes(i):
             s0, n = NODE_PIECES[i]
             nc.vector.quantize_mx(
-                out=x_codes[:, s0 : s0 + n].bitcast(FP8X4), scales=x_plane[:, s0 : s0 + n], in_=picked[i][:].rearrange("p c j -> p (c j)")
+                out=node_codes(s0, n), scales=x_plane[:, s0 : s0 + n], in_=picked[i][:].rearrange("p c j -> p (c j)")
             )
 
-        n_chunks = T // X_CHUNK
-        for c in range(n_chunks):
-            round_pairs(nc.vector.tensor_copy, 0, c, 0, X_CHUNK)
+        def round_shared(u, c):
+            width = X_CHUNKS[u][c][1]
+            round_pairs(nc.vector.tensor_copy, u, c, 0, width * 11 // 16)
+            round_pairs(nc.scalar.copy, u, c, width * 11 // 16, width)
+
+        for c in range(2):
+            round_pairs(nc.vector.tensor_copy, 0, c, 0, X_CHUNKS[0][c][1])
+        round_shared(0, 2)
         for i in range(len(NODE_PIECES)):
             gather_pairs(0, i)
-        for c in range(n_chunks - 1):
-            round_pairs(nc.scalar.copy, 1, c, 0, X_CHUNK)
-        round_pairs(nc.vector.tensor_copy, 1, n_chunks - 1, 0, LAST_SPLIT)
-        round_pairs(nc.scalar.copy, 1, n_chunks - 1, LAST_SPLIT, X_CHUNK)
+        for c in range(3):
+            round_pairs(nc.scalar.copy, 1, c, 0, X_CHUNKS[1][c][1])
+        round_shared(1, 3)
 
         w_grouped = {}
         w_codes = {}
         w_plane = {}
         for i in range(2):
             for h in range(2):
-                w_grouped[i, h] = keep.tile([P, 2, P, PACK], BF16, name=f"w_grouped{i}_{h}", align_bytes=64)
+                w_grouped[i, h] = keep.tile([P, 2, P, PACK], BF16, name=f"w_grouped{i}_{h}", tag=f"w_grouped{i}_{h}", align_bytes=64)
                 w_codes[i, h] = keep.tile([P, 2 * P], U32, name=f"w_codes{i}_{h}", align_bytes=64)
                 w_plane[i, h] = keep.tile([P, 2 * P], U8, name=f"w_plane{i}_{h}", align_bytes=64)
 
         def round_weights(i, h):
-            nc.scalar.copy(
-                out=w_grouped[i, h][:].rearrange("p t m j -> p m j t"),
-                in_=w_raw[i][:].rearrange("p j (m t) -> p m j t", t=PACK)[:, :, :, 2 * h : 2 * h + 2],
-            )
+            grouped = w_grouped[i, h][:].rearrange("p t m j -> p m j t")
+            if i == 0:
+                for u in range(2):
+                    nc.scalar.copy(
+                        out=grouped[:, :, 2 * u : 2 * u + 2, :],
+                        in_=w1_raw[u][:].rearrange("p j (m t) -> p m j t", t=PACK)[:, :, :, 2 * h : 2 * h + 2],
+                    )
+            else:
+                nc.scalar.copy(out=grouped, in_=w2_raw[:].rearrange("p j (m t) -> p m j t", t=PACK)[:, :, :, 2 * h : 2 * h + 2])
 
         def quantize_weights(i, h):
             nc.vector.quantize_mx(
@@ -125,21 +141,24 @@ def tile_picked_hub_silu_e_kernel(tc, xT, w1, w2, w3_words, w3_scales, offs, src
         parts = {}
         for i in range(2):
             for t in range(PACK):
-                parts[i, t] = keep.tile([P, S], F32, name=f"part{i}_{t}")
+                width = S if t + i >= 3 else (SOURCE_WINDOW, TARGET_WINDOW)[i]
+                parts[i, t] = keep.tile([P, width], F32, name=f"part{i}_{t}")
+                if width > S:
+                    nc.gpsimd.memset(parts[i, t][:, S:width], 0.0)
 
-        def first_product(i, t, s0, n):
+        def first_product(i, t, s0, n, copy):
             cols = slice((t % 2) * P, (t % 2 + 1) * P)
             acc = psum.tile([P, n], F32, name="acc")
             nc.tensor.matmul_mx(
                 out=acc[:],
                 lhsT=w_codes[i, t // 2][:, cols].bitcast(FP8X4),
                 lhsT_scale=w_plane[i, t // 2][:, cols],
-                rhs=x_codes[:, s0 : s0 + n].bitcast(FP8X4),
+                rhs=node_codes(s0, n),
                 rhs_scale=x_plane[:, s0 : s0 + n],
                 start=True,
                 stop=True,
             )
-            nc.scalar.copy(out=parts[i, t][:, s0 : s0 + n], in_=acc[:])
+            copy(out=parts[i, t][:, s0 : s0 + n], in_=acc[:])
 
         gather_pairs(1, 0)
         gather_pairs(1, 1)
@@ -147,44 +166,44 @@ def tile_picked_hub_silu_e_kernel(tc, xT, w1, w2, w3_words, w3_scales, offs, src
         round_weights(0, 0)
         gather_pairs(1, 2)
         quantize_weights(0, 0)
+        x_codes[1] = keep.tile([P, BANK], U32, name="x_codes1", tag="w_grouped0_0", align_bytes=64)
         quantize_nodes(1)
         quantize_nodes(2)
-        for s0, n in NODE_PIECES:
-            first_product(0, 0, s0, n)
+        for i, (s0, n) in enumerate(NODE_PIECES):
+            first_product(0, 0, s0, n, nc.scalar.copy if i == 0 else nc.vector.tensor_copy)
+
+        def whole_product(i, t):
+            for s0 in (0, BANK):
+                first_product(i, t, s0, BANK, nc.scalar.copy)
+
+        round_weights(0, 1)
         round_weights(1, 0)
+        quantize_weights(0, 1)
         quantize_weights(1, 0)
-        for i, t in ((1, 0), (0, 1), (1, 1)):
-            for s0 in (0, BANK):
-                first_product(i, t, s0, BANK)
-        for i in range(2):
-            round_weights(i, 1)
-            quantize_weights(i, 1)
-        for t in (2, 3):
-            for s0 in (0, BANK):
-                first_product(0, t, s0, BANK)
-        for s0 in (0, BANK):
-            for t in (2, 3):
-                first_product(1, t, s0, BANK)
+        whole_product(0, 1)
+        whole_product(1, 0)
+        whole_product(1, 1)
+        whole_product(0, 2)
+        round_weights(1, 1)
+        quantize_weights(1, 1)
+        whole_product(0, 3)
+        whole_product(1, 2)
+        whole_product(1, 3)
 
         sums_low = keep.tile([P, 2, S], F32, name="sums_low")
-        sums_high = [keep.tile([P, 2, n], F32, name=f"sums_high{ci}") for ci, (r0, n) in enumerate(EDGE_CHUNKS)]
         zs = [keep.tile([P, n, PACK], BF16, name=f"z{ci}", tag=f"z{ci}", align_bytes=64) for ci, (r0, n) in enumerate(EDGE_CHUNKS)]
-        widest = max(BANK, max(n for r0, n in EDGE_CHUNKS))
-        sources = [keep.tile([P, widest], F32, name=f"source{b}") for b in range(3)]
+        first_n = EDGE_CHUNKS[0][1]
+        spans = ((0, 0, S, "w_grouped0_1"), (1, 0, S, "w_grouped1_0"), (2, 0, S, "w_grouped1_1"), (3, 0, first_n, "head"), (3, first_n, S - first_n, "rest"))
+        sources = [keep.tile([P, n], F32, name=f"source{k}", tag=tag, align_bytes=64) for k, (t, r0, n, tag) in enumerate(spans)]
 
-        items = [(t, r0, BANK, sums_low[:, t, r0 : r0 + BANK]) for t in (0, 1) for r0 in (0, BANK)]
-        for ci, (r0, n) in enumerate(EDGE_CHUNKS):
-            items.extend((t, r0, n, sums_high[ci][:, t - 2, :]) for t in (2, 3))
-        held = {}
+        def fetch_source(k):
+            t, r0, n, tag = spans[k]
+            nc.vector.tensor_copy(sources[k][:], parts[0, t][:].indirect(src_t[:, r0 // 16 : (r0 + n) // 16]))
 
-        def fetch_source(k, into):
-            t, r0, n, total = items[k]
-            held[k] = into[:, 0:n]
-            nc.vector.tensor_copy(held[k], parts[0, t][:].indirect(src_t[:, r0 // 16 : (r0 + n) // 16]))
-
-        def add_target(k):
-            t, r0, n, total = items[k]
-            nc.vector.tensor_tensor(total, parts[1, t][:].indirect(dst_t[:, r0 // 16 : (r0 + n) // 16]), held[k], ADD)
+        def add_target(t, r0, n, total):
+            k = 4 if t == 3 and r0 >= first_n else t
+            lo = r0 - spans[k][1]
+            nc.vector.tensor_tensor(total, parts[1, t][:].indirect(dst_t[:, r0 // 16 : (r0 + n) // 16]), sources[k][:, lo : lo + n], ADD)
 
         def activate(ci, h, sums):
             nc.scalar.activation(zs[ci][:, :, 2 * h : 2 * h + 2], sums.rearrange("p t c -> p c t"), SILU)
@@ -214,24 +233,25 @@ def tile_picked_hub_silu_e_kernel(tc, xT, w1, w2, w3_words, w3_scales, offs, src
                     start=True,
                     stop=True,
                 )
-                nc.scalar.copy(out=result[:, s0 : s0 + size], in_=acc[:])
+                copy = nc.vector.tensor_copy if ci >= len(EDGE_CHUNKS) - 2 else nc.scalar.copy
+                copy(out=result[:, s0 : s0 + size], in_=acc[:])
             nc.sync.dma_start(out=out[:, r0 : r0 + n], in_=result[:])
 
-        last = len(items) - 1
-        fetch_source(0, sources[0])
-        for k in range(len(items)):
-            if k + 1 < last:
-                fetch_source(k + 1, sources[(k + 1) % len(sources)])
-            elif k + 1 == last:
-                second_product(0)
-                late = keep.tile([P, items[last][2]], F32, name="late", tag="z0", align_bytes=64)
-                fetch_source(last, late)
-            add_target(k)
-            if k == 3:
-                for ci, (r0, n) in enumerate(EDGE_CHUNKS):
-                    activate(ci, 0, sums_low[:, :, r0 : r0 + n])
-            if k > 3 and k % 2 == 1:
-                ci = (k - 4) // 2
-                activate(ci, 1, sums_high[ci][:])
-        for ci in range(1, len(EDGE_CHUNKS)):
+        for t in range(2):
+            fetch_source(t)
+        for t in range(2):
+            add_target(t, 0, S, sums_low[:, t, :])
+        for ci, (r0, n) in enumerate(EDGE_CHUNKS):
+            activate(ci, 0, sums_low[:, :, r0 : r0 + n])
+        for k in (2, 3, 4):
+            fetch_source(k)
+        sums_tags = ("sums_high", "head", "z0", "z1")
+        for ci, (r0, n) in enumerate(EDGE_CHUNKS):
+            if ci >= 2:
+                second_product(ci - 2)
+            sums_high = keep.tile([P, 2, n], F32, name=f"sums_high{ci}", tag=sums_tags[ci], align_bytes=64)
+            for t in (2, 3):
+                add_target(t, r0, n, sums_high[:, t - 2, :])
+            activate(ci, 1, sums_high[:])
+        for ci in range(len(EDGE_CHUNKS) - 2, len(EDGE_CHUNKS)):
             second_product(ci)

@@ -16,24 +16,26 @@ SILU = mybir.ActivationFunctionType.Silu
 K, T, S, H, N = 512, 2048, 1024, 512, 128
 P = 128
 PACK = 4
+BANK = 512
+GROUP = 16
 FLOPS = 2 * K * H * S * 2 + 2 * H * N * S
 
 X_CHUNKS = (((0, 1024), (1024, 512), (1536, 512)), ((0, 512), (512, 512), (1024, 512), (1536, 512)))
-SOURCE_WINDOW = 1408
-TARGET_WINDOW = 1040
+VECTOR_SHARE = 352
 NODE_PIECES = ((0, 512), (512, 256), (768, 256))
-EDGE_CHUNKS = ((0, 384), (384, 256), (640, 256), (896, 128))
-BANK = 512
+EDGE_CHUNKS = ((0, 256), (256, 384), (640, 256), (896, 128))
+SOURCE_WINDOW = 1408
+TARGET_WINDOW = S + GROUP
 
 
 def powers_of_two(n):
-    out = []
+    pieces = []
     start = 0
-    for size in (512, 256, 128):
-        if n - start >= size:
-            out.append((start, size))
-            start = start + size
-    return out
+    for width in (256, 128):
+        if n - start >= width:
+            pieces.append((start, width))
+            start = start + width
+    return pieces
 
 
 def tile_picked_hub_silu_e_kernel(tc, xT, w1, w2, w3_words, w3_scales, offs, src, dst, out):
@@ -43,27 +45,27 @@ def tile_picked_hub_silu_e_kernel(tc, xT, w1, w2, w3_words, w3_scales, offs, src
         psum = ctx.enter_context(tc.psum_pool(name="psum", bufs=6))
         psum_out = ctx.enter_context(tc.psum_pool(name="psum_out", bufs=2))
 
-        offs_t = keep.tile([P, S // 16], U16, name="offs_t")
-        src_t = keep.tile([P, S // 16], U16, name="src_t")
-        dst_t = keep.tile([P, S // 16], U16, name="dst_t")
+        def entries(list_tile, start, n):
+            return list_tile[:, start // GROUP : (start + n) // GROUP]
+
+        offs_t = keep.tile([P, S // GROUP], U16, name="offs_t")
+        src_t = keep.tile([P, S // GROUP], U16, name="src_t")
+        dst_t = keep.tile([P, S // GROUP], U16, name="dst_t")
         w3_codes = keep.tile([P, 2 * N], U8, name="w3_codes", align_bytes=64)
-        w3_plane = keep.tile([P, N], U8, name="w3_plane", align_bytes=64)
-        nc.gpsimd.memset(w3_plane[:], 0)
+        w3_bytes = keep.tile([P, N], U8, name="w3_bytes", align_bytes=64)
+        nc.gpsimd.memset(w3_bytes[:], 0)
 
         x_rows = xT.rearrange("(p j) c -> p j c", j=PACK)
         x_raw = {}
         for u in range(2):
             for c, (c0, width) in enumerate(X_CHUNKS[u]):
-                raw = keep.tile([P, 2, width], F32, name=f"x_raw{u}_{c}")
-                nc.sync.dma_start(out=raw[:], in_=x_rows[:, 2 * u : 2 * u + 2, c0 : c0 + width])
-                x_raw[u, c] = raw
+                x_raw[u, c] = keep.tile([P, 2, width], F32, name=f"x_raw{u}_{c}")
+                nc.sync.dma_start(out=x_raw[u, c][:], in_=x_rows[:, 2 * u : 2 * u + 2, c0 : c0 + width])
                 if u == 0 and c == 0:
                     nc.sync.dma_start(offs_t[:], offs)
-        w1_raw = []
+        w1_raw = [keep.tile([P, 2, H], F32, name=f"w1_raw{u}") for u in range(2)]
         for u in range(2):
-            raw = keep.tile([P, 2, H], F32, name=f"w1_raw{u}")
-            nc.sync.dma_start(out=raw[:], in_=w1.rearrange("(p j) c -> p j c", j=PACK)[:, 2 * u : 2 * u + 2, :])
-            w1_raw.append(raw)
+            nc.sync.dma_start(out=w1_raw[u][:], in_=w1.rearrange("(p j) c -> p j c", j=PACK)[:, 2 * u : 2 * u + 2, :])
         w2_raw = keep.tile([P, PACK, H], F32, name="w2_raw")
         nc.sync.dma_start(out=w2_raw[:], in_=w2.rearrange("(p j) c -> p j c", j=PACK))
         nc.sync.dma_start(src_t[:], src)
@@ -71,14 +73,14 @@ def tile_picked_hub_silu_e_kernel(tc, xT, w1, w2, w3_words, w3_scales, offs, src
         nc.sync.dma_start(out=w3_codes[:].bitcast(I32), in_=w3_words[0].bitcast(I32))
         for q in range(4):
             nc.sync.dma_start(
-                out=w3_plane[32 * q : 32 * q + 4, :].bitcast(I32),
+                out=w3_bytes[32 * q : 32 * q + 4, :].bitcast(I32),
                 in_=w3_scales[0, 4 * q : 4 * q + 4, :].bitcast(I32),
             )
 
         pairs = [keep.tile([P, T, 2], BF16, name=f"pairs{u}", align_bytes=64) for u in range(2)]
         picked = [keep.tile([P, n, PACK], BF16, name=f"picked{i}", align_bytes=64) for i, (s0, n) in enumerate(NODE_PIECES)]
         x_codes = {0: keep.tile([P, BANK], U32, name="x_codes0", align_bytes=64)}
-        x_plane = keep.tile([P, S], U8, name="x_plane", align_bytes=64)
+        x_bytes = keep.tile([P, S], U8, name="x_bytes", align_bytes=64)
 
         def node_codes(s0, n):
             return x_codes[s0 // BANK][:, s0 % BANK : s0 % BANK + n].bitcast(FP8X4)
@@ -87,78 +89,78 @@ def tile_picked_hub_silu_e_kernel(tc, xT, w1, w2, w3_words, w3_scales, offs, src
             c0 = X_CHUNKS[u][c][0]
             copy(out=pairs[u][:, c0 + lo : c0 + hi, :], in_=x_raw[u, c][:, :, lo:hi].rearrange("p e c -> p c e"))
 
+        def round_pair(copy, u):
+            last = len(X_CHUNKS[u]) - 1
+            for c in range(last):
+                round_pairs(copy, u, c, 0, X_CHUNKS[u][c][1])
+            round_pairs(nc.vector.tensor_copy, u, last, 0, VECTOR_SHARE)
+            round_pairs(nc.scalar.copy, u, last, VECTOR_SHARE, X_CHUNKS[u][last][1])
+
         def gather_pairs(u, i):
             s0, n = NODE_PIECES[i]
             window = pairs[u][:].rearrange("p c e -> p (c e)").bitcast(U32)
             words = picked[i][:].rearrange("p c j -> p (c j)").bitcast(U32)
-            nc.vector.tensor_copy(words[:, u : 2 * n : 2], window.indirect(offs_t[:, s0 // 16 : (s0 + n) // 16]))
+            nc.vector.tensor_copy(words[:, u : 2 * n : 2], window.indirect(entries(offs_t, s0, n)))
 
         def quantize_nodes(i):
             s0, n = NODE_PIECES[i]
             nc.vector.quantize_mx(
-                out=node_codes(s0, n), scales=x_plane[:, s0 : s0 + n], in_=picked[i][:].rearrange("p c j -> p (c j)")
+                out=node_codes(s0, n), scales=x_bytes[:, s0 : s0 + n], in_=picked[i][:].rearrange("p c j -> p (c j)")
             )
 
-        def round_shared(u, c):
-            width = X_CHUNKS[u][c][1]
-            round_pairs(nc.vector.tensor_copy, u, c, 0, width * 11 // 16)
-            round_pairs(nc.scalar.copy, u, c, width * 11 // 16, width)
-
-        for c in range(2):
-            round_pairs(nc.vector.tensor_copy, 0, c, 0, X_CHUNKS[0][c][1])
-        round_shared(0, 2)
+        round_pair(nc.vector.tensor_copy, 0)
         for i in range(len(NODE_PIECES)):
             gather_pairs(0, i)
-        for c in range(3):
-            round_pairs(nc.scalar.copy, 1, c, 0, X_CHUNKS[1][c][1])
-        round_shared(1, 3)
+        round_pair(nc.scalar.copy, 1)
 
-        w_grouped = {}
+        w_rounded = {}
         w_codes = {}
-        w_plane = {}
-        for i in range(2):
+        w_bytes = {}
+        for w in range(2):
             for h in range(2):
-                w_grouped[i, h] = keep.tile([P, 2, P, PACK], BF16, name=f"w_grouped{i}_{h}", tag=f"w_grouped{i}_{h}", align_bytes=64)
-                w_codes[i, h] = keep.tile([P, 2 * P], U32, name=f"w_codes{i}_{h}", align_bytes=64)
-                w_plane[i, h] = keep.tile([P, 2 * P], U8, name=f"w_plane{i}_{h}", align_bytes=64)
+                w_rounded[w, h] = keep.tile([P, 2, P, PACK], BF16, name=f"w_rounded{w}_{h}", tag=f"w_rounded{w}_{h}", align_bytes=64)
+                w_codes[w, h] = keep.tile([P, 2 * P], U32, name=f"w_codes{w}_{h}", align_bytes=64)
+                w_bytes[w, h] = keep.tile([P, 2 * P], U8, name=f"w_bytes{w}_{h}", align_bytes=64)
 
-        def round_weights(i, h):
-            grouped = w_grouped[i, h][:].rearrange("p t m j -> p m j t")
-            if i == 0:
-                for u in range(2):
-                    nc.scalar.copy(
-                        out=grouped[:, :, 2 * u : 2 * u + 2, :],
-                        in_=w1_raw[u][:].rearrange("p j (m t) -> p m j t", t=PACK)[:, :, :, 2 * h : 2 * h + 2],
-                    )
-            else:
-                nc.scalar.copy(out=grouped, in_=w2_raw[:].rearrange("p j (m t) -> p m j t", t=PACK)[:, :, :, 2 * h : 2 * h + 2])
+        def round_weights(w, h):
+            rounded = w_rounded[w, h][:].rearrange("p t m j -> p m j t")
+            loads = ((w1_raw[0], 0, 2), (w1_raw[1], 2, PACK)) if w == 0 else ((w2_raw, 0, PACK),)
+            for raw, j0, j1 in loads:
+                nc.scalar.copy(
+                    out=rounded[:, :, j0:j1, :],
+                    in_=raw[:].rearrange("p j (m t) -> p m j t", t=PACK)[:, :, :, 2 * h : 2 * h + 2],
+                )
 
-        def quantize_weights(i, h):
+        def quantize_weights(w, h):
             nc.vector.quantize_mx(
-                out=w_codes[i, h][:].bitcast(FP8X4), scales=w_plane[i, h][:], in_=w_grouped[i, h][:].rearrange("p t m j -> p (t m j)")
+                out=w_codes[w, h][:].bitcast(FP8X4), scales=w_bytes[w, h][:], in_=w_rounded[w, h][:].rearrange("p t m j -> p (t m j)")
             )
 
-        parts = {}
-        for i in range(2):
+        planes = {}
+        for w in range(2):
             for t in range(PACK):
-                width = S if t + i >= 3 else (SOURCE_WINDOW, TARGET_WINDOW)[i]
-                parts[i, t] = keep.tile([P, width], F32, name=f"part{i}_{t}")
+                width = (SOURCE_WINDOW, TARGET_WINDOW)[w] if t < 2 else S
+                planes[w, t] = keep.tile([P, width], F32, name=f"plane{w}_{t}")
                 if width > S:
-                    nc.gpsimd.memset(parts[i, t][:, S:width], 0.0)
+                    nc.gpsimd.memset(planes[w, t][:, S:width], 0.0)
 
-        def first_product(i, t, s0, n, copy):
+        def first_product(w, t, s0, n, copy):
             cols = slice((t % 2) * P, (t % 2 + 1) * P)
             acc = psum.tile([P, n], F32, name="acc")
             nc.tensor.matmul_mx(
                 out=acc[:],
-                lhsT=w_codes[i, t // 2][:, cols].bitcast(FP8X4),
-                lhsT_scale=w_plane[i, t // 2][:, cols],
+                lhsT=w_codes[w, t // 2][:, cols].bitcast(FP8X4),
+                lhsT_scale=w_bytes[w, t // 2][:, cols],
                 rhs=node_codes(s0, n),
-                rhs_scale=x_plane[:, s0 : s0 + n],
+                rhs_scale=x_bytes[:, s0 : s0 + n],
                 start=True,
                 stop=True,
             )
-            copy(out=parts[i, t][:, s0 : s0 + n], in_=acc[:])
+            copy(out=planes[w, t][:, s0 : s0 + n], in_=acc[:])
+
+        def whole_product(w, t):
+            for s0 in (0, BANK):
+                first_product(w, t, s0, BANK, nc.scalar.copy)
 
         gather_pairs(1, 0)
         gather_pairs(1, 1)
@@ -166,16 +168,11 @@ def tile_picked_hub_silu_e_kernel(tc, xT, w1, w2, w3_words, w3_scales, offs, src
         round_weights(0, 0)
         gather_pairs(1, 2)
         quantize_weights(0, 0)
-        x_codes[1] = keep.tile([P, BANK], U32, name="x_codes1", tag="w_grouped0_0", align_bytes=64)
+        x_codes[1] = keep.tile([P, BANK], U32, name="x_codes1", tag="w_rounded0_0", align_bytes=64)
         quantize_nodes(1)
         quantize_nodes(2)
         for i, (s0, n) in enumerate(NODE_PIECES):
             first_product(0, 0, s0, n, nc.scalar.copy if i == 0 else nc.vector.tensor_copy)
-
-        def whole_product(i, t):
-            for s0 in (0, BANK):
-                first_product(i, t, s0, BANK, nc.scalar.copy)
-
         round_weights(0, 1)
         round_weights(1, 0)
         quantize_weights(0, 1)
@@ -190,68 +187,63 @@ def tile_picked_hub_silu_e_kernel(tc, xT, w1, w2, w3_words, w3_scales, offs, src
         whole_product(1, 2)
         whole_product(1, 3)
 
-        sums_low = keep.tile([P, 2, S], F32, name="sums_low")
-        zs = [keep.tile([P, n, PACK], BF16, name=f"z{ci}", tag=f"z{ci}", align_bytes=64) for ci, (r0, n) in enumerate(EDGE_CHUNKS)]
-        first_n = EDGE_CHUNKS[0][1]
-        spans = ((0, 0, S, "w_grouped0_1"), (1, 0, S, "w_grouped1_0"), (2, 0, S, "w_grouped1_1"), (3, 0, first_n, "head"), (3, first_n, S - first_n, "rest"))
-        sources = [keep.tile([P, n], F32, name=f"source{k}", tag=tag, align_bytes=64) for k, (t, r0, n, tag) in enumerate(spans)]
-
-        def fetch_source(k):
-            t, r0, n, tag = spans[k]
-            nc.vector.tensor_copy(sources[k][:], parts[0, t][:].indirect(src_t[:, r0 // 16 : (r0 + n) // 16]))
-
-        def add_target(t, r0, n, total):
-            k = 4 if t == 3 and r0 >= first_n else t
-            lo = r0 - spans[k][1]
-            nc.vector.tensor_tensor(total, parts[1, t][:].indirect(dst_t[:, r0 // 16 : (r0 + n) // 16]), sources[k][:, lo : lo + n], ADD)
-
-        def activate(ci, h, sums):
-            nc.scalar.activation(zs[ci][:, :, 2 * h : 2 * h + 2], sums.rearrange("p t c -> p c t"), SILU)
-
+        sums = keep.tile([P, PACK, S], F32, name="sums")
+        z = [keep.tile([P, n, PACK], BF16, name=f"z{c}", tag=f"z{c}", align_bytes=64) for c, (r0, n) in enumerate(EDGE_CHUNKS)]
         z_codes = keep.tile([P, S], U32, name="z_codes", align_bytes=64)
-        z_plane = keep.tile([P, S], U8, name="z_plane", align_bytes=64)
+        z_bytes = keep.tile([P, S], U8, name="z_bytes", align_bytes=64)
 
-        def second_product(ci):
-            r0, n = EDGE_CHUNKS[ci]
-            for s0, size in powers_of_two(n):
-                cols = slice(r0 + s0, r0 + s0 + size)
+        def fetch_source(t, r0, n, fetched):
+            nc.vector.tensor_copy(fetched, planes[0, t][:].indirect(entries(src_t, r0, n)))
+
+        def add_target(t, r0, n, fetched):
+            nc.vector.tensor_tensor(sums[:, t, r0 : r0 + n], planes[1, t][:].indirect(entries(dst_t, r0, n)), fetched, ADD)
+
+        def activate(c):
+            r0, n = EDGE_CHUNKS[c]
+            nc.scalar.activation(
+                z[c][:].rearrange("p (g i) t -> p g t i", i=4), sums[:, :, r0 : r0 + n].rearrange("p t (g i) -> p g t i", i=4), SILU
+            )
+
+        def second_product(c, copy):
+            r0, n = EDGE_CHUNKS[c]
+            for s0, width in powers_of_two(n):
+                cols = slice(r0 + s0, r0 + s0 + width)
                 nc.vector.quantize_mx(
                     out=z_codes[:, cols].bitcast(FP8X4),
-                    scales=z_plane[:, cols],
-                    in_=zs[ci][:, s0 : s0 + size, :].rearrange("p c t -> p (c t)"),
+                    scales=z_bytes[:, cols],
+                    in_=z[c][:, s0 : s0 + width, :].rearrange("p r t -> p (r t)"),
                 )
-            result = keep.tile([P, n], F32, name=f"result{ci}")
-            for s0, size in powers_of_two(n):
-                cols = slice(r0 + s0, r0 + s0 + size)
-                acc = psum_out.tile([P, size], F32, name="acc_out")
+            result = keep.tile([P, n], F32, name=f"result{c}")
+            for s0, width in powers_of_two(n):
+                cols = slice(r0 + s0, r0 + s0 + width)
+                acc_out = psum_out.tile([P, width], F32, name="acc_out")
                 nc.tensor.matmul_mx(
-                    out=acc[:],
+                    out=acc_out[:],
                     lhsT=w3_codes[:].bitcast(FP4X4),
-                    lhsT_scale=w3_plane[:],
+                    lhsT_scale=w3_bytes[:],
                     rhs=z_codes[:, cols].bitcast(FP8X4),
-                    rhs_scale=z_plane[:, cols],
+                    rhs_scale=z_bytes[:, cols],
                     start=True,
                     stop=True,
                 )
-                copy = nc.vector.tensor_copy if ci >= len(EDGE_CHUNKS) - 2 else nc.scalar.copy
-                copy(out=result[:, s0 : s0 + size], in_=acc[:])
+                copy(out=result[:, s0 : s0 + width], in_=acc_out[:])
             nc.sync.dma_start(out=out[:, r0 : r0 + n], in_=result[:])
 
+        low_tags = ("w_rounded0_1", "w_rounded1_0")
+        low = [keep.tile([P, S], F32, name=f"low{t}", tag=low_tags[t], align_bytes=64) for t in range(2)]
         for t in range(2):
-            fetch_source(t)
+            fetch_source(t, 0, S, low[t][:])
         for t in range(2):
-            add_target(t, 0, S, sums_low[:, t, :])
-        for ci, (r0, n) in enumerate(EDGE_CHUNKS):
-            activate(ci, 0, sums_low[:, :, r0 : r0 + n])
-        for k in (2, 3, 4):
-            fetch_source(k)
-        sums_tags = ("sums_high", "head", "z0", "z1")
-        for ci, (r0, n) in enumerate(EDGE_CHUNKS):
-            if ci >= 2:
-                second_product(ci - 2)
-            sums_high = keep.tile([P, 2, n], F32, name=f"sums_high{ci}", tag=sums_tags[ci], align_bytes=64)
+            add_target(t, 0, S, low[t][:])
+
+        for c, (r0, n) in enumerate(EDGE_CHUNKS):
+            if c >= 2:
+                second_product(c - 2, nc.scalar.copy)
+            high = keep.tile([P, 2, n], F32, name=f"high{c}", tag=f"z{c - 2}" if c >= 2 else "w_rounded1_1", align_bytes=64)
             for t in (2, 3):
-                add_target(t, r0, n, sums_high[:, t - 2, :])
-            activate(ci, 1, sums_high[:])
-        for ci in range(len(EDGE_CHUNKS) - 2, len(EDGE_CHUNKS)):
-            second_product(ci)
+                fetch_source(t, r0, n, high[:, t - 2, :])
+            for t in (2, 3):
+                add_target(t, r0, n, high[:, t - 2, :])
+            activate(c)
+        for c in range(len(EDGE_CHUNKS) - 2, len(EDGE_CHUNKS)):
+            second_product(c, nc.vector.tensor_copy)

@@ -11,6 +11,8 @@ U8 = mybir.dt.uint8
 FP8X4 = mybir.dt.float8_e4m3fn_x4
 FP4X4 = mybir.dt.float4_e2m1fn_x4
 ADD = mybir.AluOpType.add
+MULT = mybir.AluOpType.mult
+COPY = mybir.ActivationFunctionType.Copy
 SILU = mybir.ActivationFunctionType.Silu
 
 K, T, S, H, N = 512, 2048, 1024, 512, 128
@@ -20,9 +22,12 @@ BANK = 512
 GROUP = 16
 FLOPS = 2 * K * H * S * 2 + 2 * H * N * S
 
-X_CHUNKS = (((0, 1024), (1024, 512), (1536, 512)), ((0, 512), (512, 512), (1024, 512), (1536, 512)))
+PAIR_CHUNKS = ((0, 1024), (1024, 512), (1536, 512))
 VECTOR_SHARE = 352
-NODE_PIECES = ((0, 512), (512, 256), (768, 256))
+ROW2_CHUNKS = ((0, 1024), (1024, 768), (1792, 256))
+ROW2_SCALAR = (512, 320, 256)
+ROW3_CHUNKS = ((0, 704), (704, 704), (1408, 640))
+PIECE = 256
 EDGE_CHUNKS = ((0, 256), (256, 384), (640, 256), (896, 128))
 SOURCE_WINDOW = 1408
 TARGET_WINDOW = S + GROUP
@@ -56,18 +61,20 @@ def tile_picked_hub_silu_e_kernel(tc, xT, w1, w2, w3_words, w3_scales, offs, src
         nc.gpsimd.memset(w3_bytes[:], 0)
 
         x_rows = xT.rearrange("(p j) c -> p j c", j=PACK)
-        x_raw = {}
-        for u in range(2):
-            for c, (c0, width) in enumerate(X_CHUNKS[u]):
-                x_raw[u, c] = keep.tile([P, 2, width], F32, name=f"x_raw{u}_{c}")
-                nc.sync.dma_start(out=x_raw[u, c][:], in_=x_rows[:, 2 * u : 2 * u + 2, c0 : c0 + width])
-                if u == 0 and c == 0:
-                    nc.sync.dma_start(offs_t[:], offs)
-        w1_raw = [keep.tile([P, 2, H], F32, name=f"w1_raw{u}") for u in range(2)]
-        for u in range(2):
-            nc.sync.dma_start(out=w1_raw[u][:], in_=w1.rearrange("(p j) c -> p j c", j=PACK)[:, 2 * u : 2 * u + 2, :])
-        w2_raw = keep.tile([P, PACK, H], F32, name="w2_raw")
-        nc.sync.dma_start(out=w2_raw[:], in_=w2.rearrange("(p j) c -> p j c", j=PACK))
+        pair_raw = []
+        for c, (c0, width) in enumerate(PAIR_CHUNKS):
+            pair_raw.append(keep.tile([P, 2, width], F32, name=f"pair_raw{c}"))
+            nc.sync.dma_start(out=pair_raw[c][:], in_=x_rows[:, 0:2, c0 : c0 + width])
+            if c == 0:
+                nc.sync.dma_start(offs_t[:], offs)
+        row_raw = {}
+        for j, chunks in ((2, ROW2_CHUNKS), (3, ROW3_CHUNKS)):
+            row_raw[j] = keep.tile([P, T], F32, name=f"row_raw{j}")
+            for c0, width in chunks:
+                nc.sync.dma_start(out=row_raw[j][:, c0 : c0 + width], in_=x_rows[:, j, c0 : c0 + width])
+        w_raw = [keep.tile([P, PACK, H], F32, name=f"w_raw{w}") for w in range(2)]
+        for w, weights in enumerate((w1, w2)):
+            nc.sync.dma_start(out=w_raw[w][:], in_=weights.rearrange("(p j) c -> p j c", j=PACK))
         nc.sync.dma_start(src_t[:], src)
         nc.sync.dma_start(dst_t[:], dst)
         nc.sync.dma_start(out=w3_codes[:].bitcast(I32), in_=w3_words[0].bitcast(I32))
@@ -77,59 +84,77 @@ def tile_picked_hub_silu_e_kernel(tc, xT, w1, w2, w3_words, w3_scales, offs, src
                 in_=w3_scales[0, 4 * q : 4 * q + 4, :].bitcast(I32),
             )
 
-        pairs = [keep.tile([P, T, 2], BF16, name=f"pairs{u}", align_bytes=64) for u in range(2)]
-        picked = [keep.tile([P, n, PACK], BF16, name=f"picked{i}", align_bytes=64) for i, (s0, n) in enumerate(NODE_PIECES)]
+        pairs = keep.tile([P, T, 2], BF16, name="pairs", align_bytes=64)
+        rows = {j: keep.tile([P, T], BF16, name=f"row{j}", align_bytes=64) for j in (2, 3)}
+        pieces = S // PIECE
+        picked = [keep.tile([P, PIECE, PACK], BF16, name=f"picked{i}", tag=f"picked{i}", align_bytes=64) for i in range(pieces)]
         x_codes = {0: keep.tile([P, BANK], U32, name="x_codes0", align_bytes=64)}
         x_bytes = keep.tile([P, S], U8, name="x_bytes", align_bytes=64)
 
         def node_codes(s0, n):
             return x_codes[s0 // BANK][:, s0 % BANK : s0 % BANK + n].bitcast(FP8X4)
 
-        def round_pairs(copy, u, c, lo, hi):
-            c0 = X_CHUNKS[u][c][0]
-            copy(out=pairs[u][:, c0 + lo : c0 + hi, :], in_=x_raw[u, c][:, :, lo:hi].rearrange("p e c -> p c e"))
+        def round_pairs(copy, c, lo, hi):
+            c0 = PAIR_CHUNKS[c][0]
+            copy(out=pairs[:, c0 + lo : c0 + hi, :], in_=pair_raw[c][:, :, lo:hi].rearrange("p e c -> p c e"))
 
-        def round_pair(copy, u):
-            last = len(X_CHUNKS[u]) - 1
-            for c in range(last):
-                round_pairs(copy, u, c, 0, X_CHUNKS[u][c][1])
-            round_pairs(nc.vector.tensor_copy, u, last, 0, VECTOR_SHARE)
-            round_pairs(nc.scalar.copy, u, last, VECTOR_SHARE, X_CHUNKS[u][last][1])
+        def gpsimd_round(out, in_):
+            nc.gpsimd.tensor_scalar(out, in_, 1.0, 0.0, MULT, ADD)
 
-        def gather_pairs(u, i):
-            s0, n = NODE_PIECES[i]
-            window = pairs[u][:].rearrange("p c e -> p (c e)").bitcast(U32)
+        def round_row(copy, j, lo, hi):
+            copy(out=rows[j][:, lo:hi], in_=row_raw[j][:, lo:hi])
+
+        def gather_pairs(i):
+            window = pairs[:].rearrange("p c e -> p (c e)").bitcast(U32)
             words = picked[i][:].rearrange("p c j -> p (c j)").bitcast(U32)
-            nc.vector.tensor_copy(words[:, u : 2 * n : 2], window.indirect(entries(offs_t, s0, n)))
+            nc.vector.tensor_copy(words[:, 0 : 2 * PIECE : 2], window.indirect(entries(offs_t, i * PIECE, PIECE)))
+
+        def gather_row(j, i):
+            chosen = entries(offs_t, i * PIECE, PIECE)
+            if i == 0:
+                nc.vector.tensor_copy(picked[i][:, :, j], row_raw[j][:].indirect(chosen))
+            else:
+                nc.scalar.activation(picked[i][:, :, j], rows[j][:].indirect(chosen), COPY)
 
         def quantize_nodes(i):
-            s0, n = NODE_PIECES[i]
+            s0 = i * PIECE
             nc.vector.quantize_mx(
-                out=node_codes(s0, n), scales=x_bytes[:, s0 : s0 + n], in_=picked[i][:].rearrange("p c j -> p (c j)")
+                out=node_codes(s0, PIECE), scales=x_bytes[:, s0 : s0 + PIECE], in_=picked[i][:].rearrange("p c j -> p (c j)")
             )
 
-        round_pair(nc.vector.tensor_copy, 0)
-        for i in range(len(NODE_PIECES)):
-            gather_pairs(0, i)
-        round_pair(nc.scalar.copy, 1)
+        last = len(PAIR_CHUNKS) - 1
+        for c in range(last):
+            round_pairs(nc.vector.tensor_copy, c, 0, PAIR_CHUNKS[c][1])
+        round_pairs(nc.vector.tensor_copy, last, 0, VECTOR_SHARE)
+        round_pairs(nc.scalar.copy, last, VECTOR_SHARE, PAIR_CHUNKS[last][1])
+        for i in (1, 2, 3, 0):
+            gather_pairs(i)
+        for (c0, width), share in zip(ROW2_CHUNKS, ROW2_SCALAR):
+            round_row(nc.scalar.copy, 2, c0, c0 + share)
+            if share < width:
+                round_row(gpsimd_round, 2, c0 + share, c0 + width)
+        for i in range(pieces):
+            gather_row(2, i)
+        for c0, width in ROW3_CHUNKS[:-1]:
+            round_row(gpsimd_round, 3, c0, c0 + width)
+        round_row(nc.vector.tensor_copy, 3, ROW3_CHUNKS[-1][0], T)
+        for i in range(pieces):
+            gather_row(3, i)
 
         w_rounded = {}
         w_codes = {}
         w_bytes = {}
         for w in range(2):
             for h in range(2):
-                w_rounded[w, h] = keep.tile([P, 2, P, PACK], BF16, name=f"w_rounded{w}_{h}", tag=f"w_rounded{w}_{h}", align_bytes=64)
                 w_codes[w, h] = keep.tile([P, 2 * P], U32, name=f"w_codes{w}_{h}", align_bytes=64)
                 w_bytes[w, h] = keep.tile([P, 2 * P], U8, name=f"w_bytes{w}_{h}", align_bytes=64)
 
-        def round_weights(w, h):
-            rounded = w_rounded[w, h][:].rearrange("p t m j -> p m j t")
-            loads = ((w1_raw[0], 0, 2), (w1_raw[1], 2, PACK)) if w == 0 else ((w2_raw, 0, PACK),)
-            for raw, j0, j1 in loads:
-                nc.scalar.copy(
-                    out=rounded[:, :, j0:j1, :],
-                    in_=raw[:].rearrange("p j (m t) -> p m j t", t=PACK)[:, :, :, 2 * h : 2 * h + 2],
-                )
+        def round_weights(w, h, copy, tag):
+            w_rounded[w, h] = keep.tile([P, 2, P, PACK], BF16, name=f"w_rounded{w}_{h}", tag=tag, align_bytes=64)
+            copy(
+                out=w_rounded[w, h][:].rearrange("p t m j -> p m j t"),
+                in_=w_raw[w][:].rearrange("p j (m t) -> p m j t", t=PACK)[:, :, :, 2 * h : 2 * h + 2],
+            )
 
         def quantize_weights(w, h):
             nc.vector.quantize_mx(
@@ -139,7 +164,7 @@ def tile_picked_hub_silu_e_kernel(tc, xT, w1, w2, w3_words, w3_scales, offs, src
         planes = {}
         for w in range(2):
             for t in range(PACK):
-                width = (SOURCE_WINDOW, TARGET_WINDOW)[w] if t < 2 else S
+                width = SOURCE_WINDOW if w == 0 else (TARGET_WINDOW if t < 2 else S)
                 planes[w, t] = keep.tile([P, width], F32, name=f"plane{w}_{t}")
                 if width > S:
                     nc.gpsimd.memset(planes[w, t][:, S:width], 0.0)
@@ -162,47 +187,41 @@ def tile_picked_hub_silu_e_kernel(tc, xT, w1, w2, w3_words, w3_scales, offs, src
             for s0 in (0, BANK):
                 first_product(w, t, s0, BANK, nc.scalar.copy)
 
-        gather_pairs(1, 0)
-        gather_pairs(1, 1)
         quantize_nodes(0)
-        round_weights(0, 0)
-        gather_pairs(1, 2)
-        quantize_weights(0, 0)
-        x_codes[1] = keep.tile([P, BANK], U32, name="x_codes1", tag="w_rounded0_0", align_bytes=64)
         quantize_nodes(1)
+        round_weights(0, 0, nc.vector.tensor_copy, "first")
+        quantize_weights(0, 0)
+        x_codes[1] = keep.tile([P, BANK], U32, name="x_codes1", tag="first", align_bytes=64)
         quantize_nodes(2)
-        for i, (s0, n) in enumerate(NODE_PIECES):
-            first_product(0, 0, s0, n, nc.scalar.copy if i == 0 else nc.vector.tensor_copy)
-        round_weights(0, 1)
-        round_weights(1, 0)
-        quantize_weights(0, 1)
-        quantize_weights(1, 0)
+        quantize_nodes(3)
+        first_product(0, 0, 0, BANK, nc.scalar.copy)
+        first_product(0, 0, BANK, PIECE, nc.vector.tensor_copy)
+        first_product(0, 0, BANK + PIECE, PIECE, nc.vector.tensor_copy)
         whole_product(0, 1)
+        round_weights(1, 0, nc.scalar.copy, "picked3")
+        quantize_weights(1, 0)
+        round_weights(0, 1, nc.scalar.copy, "picked2")
         whole_product(1, 0)
         whole_product(1, 1)
+        quantize_weights(0, 1)
+        round_weights(1, 1, nc.scalar.copy, "picked1")
         whole_product(0, 2)
-        round_weights(1, 1)
-        quantize_weights(1, 1)
         whole_product(0, 3)
+        quantize_weights(1, 1)
         whole_product(1, 2)
         whole_product(1, 3)
 
-        sums = keep.tile([P, PACK, S], F32, name="sums")
         z = [keep.tile([P, n, PACK], BF16, name=f"z{c}", tag=f"z{c}", align_bytes=64) for c, (r0, n) in enumerate(EDGE_CHUNKS)]
         z_codes = keep.tile([P, S], U32, name="z_codes", align_bytes=64)
         z_bytes = keep.tile([P, S], U8, name="z_bytes", align_bytes=64)
 
-        def fetch_source(t, r0, n, fetched):
-            nc.vector.tensor_copy(fetched, planes[0, t][:].indirect(entries(src_t, r0, n)))
+        def fetch(t, tag):
+            fetched = keep.tile([P, S], F32, name=f"fetched{t}", tag=tag, align_bytes=64)
+            nc.vector.tensor_copy(fetched[:], planes[0, t][:].indirect(src_t[:]))
+            return fetched
 
-        def add_target(t, r0, n, fetched):
-            nc.vector.tensor_tensor(sums[:, t, r0 : r0 + n], planes[1, t][:].indirect(entries(dst_t, r0, n)), fetched, ADD)
-
-        def activate(c):
-            r0, n = EDGE_CHUNKS[c]
-            nc.scalar.activation(
-                z[c][:].rearrange("p (g i) t -> p g t i", i=4), sums[:, :, r0 : r0 + n].rearrange("p t (g i) -> p g t i", i=4), SILU
-            )
+        def activate(c, h, sums):
+            nc.scalar.activation(z[c][:, :, 2 * h : 2 * h + 2], sums.rearrange("p t r -> p r t"), SILU)
 
         def second_product(c, copy):
             r0, n = EDGE_CHUNKS[c]
@@ -229,21 +248,21 @@ def tile_picked_hub_silu_e_kernel(tc, xT, w1, w2, w3_words, w3_scales, offs, src
                 copy(out=result[:, s0 : s0 + width], in_=acc_out[:])
             nc.sync.dma_start(out=out[:, r0 : r0 + n], in_=result[:])
 
-        low_tags = ("w_rounded0_1", "w_rounded1_0")
-        low = [keep.tile([P, S], F32, name=f"low{t}", tag=low_tags[t], align_bytes=64) for t in range(2)]
+        sources = [fetch(0, "source0"), fetch(1, "picked3")]
+        low_sums = keep.tile([P, 2, S], F32, name="low_sums", tag="picked2", align_bytes=64)
         for t in range(2):
-            fetch_source(t, 0, S, low[t][:])
-        for t in range(2):
-            add_target(t, 0, S, low[t][:])
+            nc.vector.tensor_tensor(low_sums[:, t, :], planes[1, t][:].indirect(dst_t[:]), sources[t][:], ADD)
+        sources.append(fetch(2, "picked1"))
+        sources.append(fetch(3, "source3"))
+        for c, (r0, n) in enumerate(EDGE_CHUNKS):
+            activate(c, 0, low_sums[:, :, r0 : r0 + n])
 
         for c, (r0, n) in enumerate(EDGE_CHUNKS):
             if c >= 2:
                 second_product(c - 2, nc.scalar.copy)
-            high = keep.tile([P, 2, n], F32, name=f"high{c}", tag=f"z{c - 2}" if c >= 2 else "w_rounded1_1", align_bytes=64)
+            high = keep.tile([P, 2, n], F32, name=f"high{c}", tag=f"z{c - 2}" if c >= 2 else f"high{c}", align_bytes=64)
             for t in (2, 3):
-                fetch_source(t, r0, n, high[:, t - 2, :])
-            for t in (2, 3):
-                add_target(t, r0, n, high[:, t - 2, :])
-            activate(c)
+                nc.vector.tensor_tensor(high[:, t - 2, :], planes[1, t][:].indirect(entries(dst_t, r0, n)), sources[t][:, r0 : r0 + n], ADD)
+            activate(c, 1, high[:])
         for c in range(len(EDGE_CHUNKS) - 2, len(EDGE_CHUNKS)):
             second_product(c, nc.vector.tensor_copy)

@@ -47,7 +47,8 @@ def tile_picked_hub_silu_e_kernel(tc, xT, w1, w2, w3_words, w3_scales, offs, src
     nc = tc.nc
     with ExitStack() as ctx:
         keep = ctx.enter_context(tc.tile_pool(name="keep", bufs=1))
-        psum = ctx.enter_context(tc.psum_pool(name="psum", bufs=6))
+        placed = ctx.enter_context(tc.tile_pool(name="placed", bufs=1))
+        psum = ctx.enter_context(tc.psum_pool(name="psum", bufs=1))
         psum_out = ctx.enter_context(tc.psum_pool(name="psum_out", bufs=2))
 
         def entries(list_tile, start, n):
@@ -72,9 +73,12 @@ def tile_picked_hub_silu_e_kernel(tc, xT, w1, w2, w3_words, w3_scales, offs, src
             row_raw[j] = keep.tile([P, T], F32, name=f"row_raw{j}")
             for c0, width in chunks:
                 nc.sync.dma_start(out=row_raw[j][:, c0 : c0 + width], in_=x_rows[:, j, c0 : c0 + width])
-        w_raw = [keep.tile([P, PACK, H], F32, name=f"w_raw{w}") for w in range(2)]
-        for w, weights in enumerate((w1, w2)):
-            nc.sync.dma_start(out=w_raw[w][:], in_=weights.rearrange("(p j) c -> p j c", j=PACK))
+        half = H // 2
+        w1_raw = [keep.tile([P, PACK, half], F32, name="w1_raw0"), placed.tile([P, PACK, half], F32, name="w1_raw1", offset=0, align_bytes=64)]
+        for a in range(2):
+            nc.sync.dma_start(out=w1_raw[a][:], in_=w1.rearrange("(p j) c -> p j c", j=PACK)[:, :, a * half : (a + 1) * half])
+        w2_raw = keep.tile([P, PACK, H], F32, name="w2_raw")
+        nc.sync.dma_start(out=w2_raw[:], in_=w2.rearrange("(p j) c -> p j c", j=PACK))
         nc.sync.dma_start(src_t[:], src)
         nc.sync.dma_start(dst_t[:], dst)
         nc.sync.dma_start(out=w3_codes[:].bitcast(I32), in_=w3_words[0].bitcast(I32))
@@ -88,11 +92,8 @@ def tile_picked_hub_silu_e_kernel(tc, xT, w1, w2, w3_words, w3_scales, offs, src
         rows = {j: keep.tile([P, T], BF16, name=f"row{j}", align_bytes=64) for j in (2, 3)}
         pieces = S // PIECE
         picked = [keep.tile([P, PIECE, PACK], BF16, name=f"picked{i}", tag=f"picked{i}", align_bytes=64) for i in range(pieces)]
-        x_codes = {0: keep.tile([P, BANK], U32, name="x_codes0", align_bytes=64)}
-        x_bytes = keep.tile([P, S], U8, name="x_bytes", align_bytes=64)
-
-        def node_codes(s0, n):
-            return x_codes[s0 // BANK][:, s0 % BANK : s0 % BANK + n].bitcast(FP8X4)
+        x_codes = {}
+        x_bytes = {}
 
         def round_pairs(copy, c, lo, hi):
             c0 = PAIR_CHUNKS[c][0]
@@ -117,9 +118,8 @@ def tile_picked_hub_silu_e_kernel(tc, xT, w1, w2, w3_words, w3_scales, offs, src
                 nc.scalar.activation(picked[i][:, :, j], rows[j][:].indirect(chosen), COPY)
 
         def quantize_nodes(i):
-            s0 = i * PIECE
             nc.vector.quantize_mx(
-                out=node_codes(s0, PIECE), scales=x_bytes[:, s0 : s0 + PIECE], in_=picked[i][:].rearrange("p c j -> p (c j)")
+                out=x_codes[i][:].bitcast(FP8X4), scales=x_bytes[i][:], in_=picked[i][:].rearrange("p c j -> p (c j)")
             )
 
         last = len(PAIR_CHUNKS) - 1
@@ -149,11 +149,10 @@ def tile_picked_hub_silu_e_kernel(tc, xT, w1, w2, w3_words, w3_scales, offs, src
                 w_codes[w, h] = keep.tile([P, 2 * P], U32, name=f"w_codes{w}_{h}", align_bytes=64)
                 w_bytes[w, h] = keep.tile([P, 2 * P], U8, name=f"w_bytes{w}_{h}", align_bytes=64)
 
-        def round_weights(w, h, copy, tag):
-            w_rounded[w, h] = keep.tile([P, 2, P, PACK], BF16, name=f"w_rounded{w}_{h}", tag=tag, align_bytes=64)
+        def round_weights(copy, w, h, raw, m0, m1):
             copy(
-                out=w_rounded[w, h][:].rearrange("p t m j -> p m j t"),
-                in_=w_raw[w][:].rearrange("p j (m t) -> p m j t", t=PACK)[:, :, :, 2 * h : 2 * h + 2],
+                out=w_rounded[w, h][:, :, m0:m1, :].rearrange("p t m j -> p m j t"),
+                in_=raw[:].rearrange("p j (m t) -> p m j t", t=PACK)[:, :, :, 2 * h : 2 * h + 2],
             )
 
         def quantize_weights(w, h):
@@ -165,51 +164,58 @@ def tile_picked_hub_silu_e_kernel(tc, xT, w1, w2, w3_words, w3_scales, offs, src
         for w in range(2):
             for t in range(PACK):
                 width = SOURCE_WINDOW if w == 0 else (TARGET_WINDOW if t < 2 else S)
-                planes[w, t] = keep.tile([P, width], F32, name=f"plane{w}_{t}")
+                planes[w, t] = keep.tile([P, width], F32, name=f"plane{w}_{t}", tag=f"plane{w}_{t}", align_bytes=64)
                 if width > S:
                     nc.gpsimd.memset(planes[w, t][:, S:width], 0.0)
 
-        def first_product(w, t, s0, n, copy):
+        def first_product(w, t, first, count, bank):
             cols = slice((t % 2) * P, (t % 2 + 1) * P)
-            acc = psum.tile([P, n], F32, name="acc")
-            nc.tensor.matmul_mx(
-                out=acc[:],
-                lhsT=w_codes[w, t // 2][:, cols].bitcast(FP8X4),
-                lhsT_scale=w_bytes[w, t // 2][:, cols],
-                rhs=node_codes(s0, n),
-                rhs_scale=x_bytes[:, s0 : s0 + n],
-                start=True,
-                stop=True,
-            )
-            copy(out=planes[w, t][:, s0 : s0 + n], in_=acc[:])
+            acc = psum.tile([P, count * PIECE], F32, name="acc", tag=f"bank{bank}")
+            for i in range(count):
+                nc.tensor.matmul_mx(
+                    out=acc[:, i * PIECE : (i + 1) * PIECE],
+                    lhsT=w_codes[w, t // 2][:, cols].bitcast(FP8X4),
+                    lhsT_scale=w_bytes[w, t // 2][:, cols],
+                    rhs=x_codes[first + i][:].bitcast(FP8X4),
+                    rhs_scale=x_bytes[first + i][:],
+                    start=True,
+                    stop=True,
+                )
+            nc.scalar.copy(out=planes[w, t][:, first * PIECE : (first + count) * PIECE], in_=acc[:])
 
-        def whole_product(w, t):
-            for s0 in (0, BANK):
-                first_product(w, t, s0, BANK, nc.scalar.copy)
+        def whole_product(w, t, bank):
+            first_product(w, t, 0, 2, bank)
+            first_product(w, t, 2, 2, bank + 1)
 
+        def weights_tile(w, h, tag):
+            return keep.tile([P, 2, P, PACK], BF16, name=f"w_rounded{w}_{h}", tag=tag, align_bytes=64)
+
+        def bytes_tile(i):
+            return keep.tile([P, PIECE], U8, name=f"x_bytes{i}", align_bytes=64)
+
+        x_codes[0] = keep.tile([P, PIECE], U32, name="x_codes0", align_bytes=64)
+        x_bytes[0] = bytes_tile(0)
         quantize_nodes(0)
-        quantize_nodes(1)
-        round_weights(0, 0, nc.vector.tensor_copy, "first")
+        for h in range(2):
+            w_rounded[0, h] = weights_tile(0, h, f"w1_rounded{h}")
+        for a in range(2):
+            for h in range(2):
+                round_weights(nc.vector.tensor_copy, 0, h, w1_raw[a], a * P // 2, (a + 1) * P // 2)
         quantize_weights(0, 0)
-        x_codes[1] = keep.tile([P, BANK], U32, name="x_codes1", tag="first", align_bytes=64)
-        quantize_nodes(2)
-        quantize_nodes(3)
-        first_product(0, 0, 0, BANK, nc.scalar.copy)
-        first_product(0, 0, BANK, PIECE, nc.vector.tensor_copy)
-        first_product(0, 0, BANK + PIECE, PIECE, nc.vector.tensor_copy)
-        whole_product(0, 1)
-        round_weights(1, 0, nc.scalar.copy, "picked3")
-        quantize_weights(1, 0)
-        round_weights(0, 1, nc.scalar.copy, "picked2")
-        whole_product(1, 0)
-        whole_product(1, 1)
+        for i in range(1, pieces):
+            x_codes[i] = placed.tile([P, PIECE], U32, name=f"x_codes{i}", offset=4 * PIECE * i, align_bytes=64)
+            x_bytes[i] = bytes_tile(i)
+            quantize_nodes(i)
+        for i in range(pieces):
+            first_product(0, 0, i, 1, i)
+        w_rounded[1, 0] = weights_tile(1, 0, "w2_rounded0")
+        round_weights(nc.vector.tensor_copy, 1, 0, w2_raw, 0, P)
         quantize_weights(0, 1)
-        round_weights(1, 1, nc.scalar.copy, "picked1")
-        whole_product(0, 2)
-        whole_product(0, 3)
-        quantize_weights(1, 1)
-        whole_product(1, 2)
-        whole_product(1, 3)
+        quantize_weights(1, 0)
+        first_product(0, 1, 0, 2, 2)
+        first_product(0, 1, 2, 2, 3)
+        whole_product(1, 0, 4)
+        whole_product(1, 1, 0)
 
         z = [keep.tile([P, n, PACK], BF16, name=f"z{c}", tag=f"z{c}", align_bytes=64) for c, (r0, n) in enumerate(EDGE_CHUNKS)]
         z_codes = keep.tile([P, S], U32, name="z_codes", align_bytes=64)
@@ -248,11 +254,18 @@ def tile_picked_hub_silu_e_kernel(tc, xT, w1, w2, w3_words, w3_scales, offs, src
                 copy(out=result[:, s0 : s0 + width], in_=acc_out[:])
             nc.sync.dma_start(out=out[:, r0 : r0 + n], in_=result[:])
 
-        sources = [fetch(0, "source0"), fetch(1, "picked3")]
-        low_sums = keep.tile([P, 2, S], F32, name="low_sums", tag="picked2", align_bytes=64)
+        sources = [fetch(0, "source0"), fetch(1, "source1")]
+        w_rounded[1, 1] = weights_tile(1, 1, "plane0_0")
+        round_weights(nc.scalar.copy, 1, 1, w2_raw, 0, P)
+        whole_product(0, 2, 2)
+        whole_product(0, 3, 4)
+        quantize_weights(1, 1)
+        whole_product(1, 2, 0)
+        whole_product(1, 3, 2)
+        low_sums = keep.tile([P, 2, S], F32, name="low_sums")
         for t in range(2):
             nc.vector.tensor_tensor(low_sums[:, t, :], planes[1, t][:].indirect(dst_t[:]), sources[t][:], ADD)
-        sources.append(fetch(2, "picked1"))
+        sources.append(fetch(2, "source2"))
         sources.append(fetch(3, "source3"))
         for c, (r0, n) in enumerate(EDGE_CHUNKS):
             activate(c, 0, low_sums[:, :, r0 : r0 + n])
@@ -260,7 +273,7 @@ def tile_picked_hub_silu_e_kernel(tc, xT, w1, w2, w3_words, w3_scales, offs, src
         for c, (r0, n) in enumerate(EDGE_CHUNKS):
             if c >= 2:
                 second_product(c - 2, nc.scalar.copy)
-            high = keep.tile([P, 2, n], F32, name=f"high{c}", tag=f"z{c - 2}" if c >= 2 else f"high{c}", align_bytes=64)
+            high = keep.tile([P, 2, n], F32, name=f"high{c}", tag=f"high{c % 2}", align_bytes=64)
             for t in (2, 3):
                 nc.vector.tensor_tensor(high[:, t - 2, :], planes[1, t][:].indirect(entries(dst_t, r0, n)), sources[t][:, r0 : r0 + n], ADD)
             activate(c, 1, high[:])

@@ -18,15 +18,14 @@ SILU = mybir.ActivationFunctionType.Silu
 K, T, S, H, N = 512, 2048, 1024, 512, 128
 P = 128
 PACK = 4
-BANK = 512
 GROUP = 16
 FLOPS = 2 * K * H * S * 2 + 2 * H * N * S
 
 PAIR_CHUNKS = ((0, 1024), (1024, 512), (1536, 512))
-VECTOR_SHARE = 352
 ROW2_CHUNKS = ((0, 1024), (1024, 768), (1792, 256))
+ROW3_CHUNKS = ((0, 768), (768, 768), (1536, 512))
+VECTOR_SHARE = 352
 ROW2_SCALAR = (512, 320, 256)
-ROW3_CHUNKS = ((0, 704), (704, 704), (1408, 640))
 PIECE = 256
 EDGE_CHUNKS = ((0, 256), (256, 384), (640, 256), (896, 128))
 SOURCE_WINDOW = 1408
@@ -74,7 +73,10 @@ def tile_picked_hub_silu_e_kernel(tc, xT, w1, w2, w3_words, w3_scales, offs, src
             for c0, width in chunks:
                 nc.sync.dma_start(out=row_raw[j][:, c0 : c0 + width], in_=x_rows[:, j, c0 : c0 + width])
         half = H // 2
-        w1_raw = [keep.tile([P, PACK, half], F32, name="w1_raw0"), placed.tile([P, PACK, half], F32, name="w1_raw1", offset=0, align_bytes=64)]
+        w1_raw = [
+            keep.tile([P, PACK, half], F32, name="w1_raw0"),
+            placed.tile([P, PACK, half], F32, name="w1_raw1", offset=0, align_bytes=64),
+        ]
         for a in range(2):
             nc.sync.dma_start(out=w1_raw[a][:], in_=w1.rearrange("(p j) c -> p j c", j=PACK)[:, :, a * half : (a + 1) * half])
         w2_raw = keep.tile([P, PACK, H], F32, name="w2_raw")
@@ -91,7 +93,7 @@ def tile_picked_hub_silu_e_kernel(tc, xT, w1, w2, w3_words, w3_scales, offs, src
         pairs = keep.tile([P, T, 2], BF16, name="pairs", align_bytes=64)
         rows = {j: keep.tile([P, T], BF16, name=f"row{j}", align_bytes=64) for j in (2, 3)}
         pieces = S // PIECE
-        picked = [keep.tile([P, PIECE, PACK], BF16, name=f"picked{i}", tag=f"picked{i}", align_bytes=64) for i in range(pieces)]
+        picked = [keep.tile([P, PIECE, PACK], BF16, name=f"picked{i}", align_bytes=64) for i in range(pieces)]
         x_codes = {}
         x_bytes = {}
 
@@ -135,9 +137,8 @@ def tile_picked_hub_silu_e_kernel(tc, xT, w1, w2, w3_words, w3_scales, offs, src
                 round_row(gpsimd_round, 2, c0 + share, c0 + width)
         for i in range(pieces):
             gather_row(2, i)
-        for c0, width in ROW3_CHUNKS[:-1]:
+        for c0, width in ROW3_CHUNKS:
             round_row(gpsimd_round, 3, c0, c0 + width)
-        round_row(nc.vector.tensor_copy, 3, ROW3_CHUNKS[-1][0], T)
         for i in range(pieces):
             gather_row(3, i)
 
@@ -164,7 +165,7 @@ def tile_picked_hub_silu_e_kernel(tc, xT, w1, w2, w3_words, w3_scales, offs, src
         for w in range(2):
             for t in range(PACK):
                 width = SOURCE_WINDOW if w == 0 else (TARGET_WINDOW if t < 2 else S)
-                planes[w, t] = keep.tile([P, width], F32, name=f"plane{w}_{t}", tag=f"plane{w}_{t}", align_bytes=64)
+                planes[w, t] = keep.tile([P, width], F32, name=f"plane{w}_{t}", align_bytes=64)
                 if width > S:
                     nc.gpsimd.memset(planes[w, t][:, S:width], 0.0)
 
@@ -187,8 +188,8 @@ def tile_picked_hub_silu_e_kernel(tc, xT, w1, w2, w3_words, w3_scales, offs, src
             first_product(w, t, 0, 2, bank)
             first_product(w, t, 2, 2, bank + 1)
 
-        def weights_tile(w, h, tag):
-            return keep.tile([P, 2, P, PACK], BF16, name=f"w_rounded{w}_{h}", tag=tag, align_bytes=64)
+        def weights_tile(name):
+            return keep.tile([P, 2, P, PACK], BF16, name=name, align_bytes=64)
 
         def bytes_tile(i):
             return keep.tile([P, PIECE], U8, name=f"x_bytes{i}", align_bytes=64)
@@ -197,7 +198,7 @@ def tile_picked_hub_silu_e_kernel(tc, xT, w1, w2, w3_words, w3_scales, offs, src
         x_bytes[0] = bytes_tile(0)
         quantize_nodes(0)
         for h in range(2):
-            w_rounded[0, h] = weights_tile(0, h, f"w1_rounded{h}")
+            w_rounded[0, h] = weights_tile(f"w1_rounded{h}")
         for a in range(2):
             for h in range(2):
                 round_weights(nc.vector.tensor_copy, 0, h, w1_raw[a], a * P // 2, (a + 1) * P // 2)
@@ -208,21 +209,20 @@ def tile_picked_hub_silu_e_kernel(tc, xT, w1, w2, w3_words, w3_scales, offs, src
             quantize_nodes(i)
         for i in range(pieces):
             first_product(0, 0, i, 1, i)
-        w_rounded[1, 0] = weights_tile(1, 0, "w2_rounded0")
+        w_rounded[1, 0] = weights_tile("w2_rounded0")
         round_weights(nc.vector.tensor_copy, 1, 0, w2_raw, 0, P)
         quantize_weights(0, 1)
         quantize_weights(1, 0)
-        first_product(0, 1, 0, 2, 2)
-        first_product(0, 1, 2, 2, 3)
+        whole_product(0, 1, 2)
         whole_product(1, 0, 4)
         whole_product(1, 1, 0)
 
-        z = [keep.tile([P, n, PACK], BF16, name=f"z{c}", tag=f"z{c}", align_bytes=64) for c, (r0, n) in enumerate(EDGE_CHUNKS)]
+        z = [keep.tile([P, n, PACK], BF16, name=f"z{c}", align_bytes=64) for c, (r0, n) in enumerate(EDGE_CHUNKS)]
         z_codes = keep.tile([P, S], U32, name="z_codes", align_bytes=64)
         z_bytes = keep.tile([P, S], U8, name="z_bytes", align_bytes=64)
 
-        def fetch(t, tag):
-            fetched = keep.tile([P, S], F32, name=f"fetched{t}", tag=tag, align_bytes=64)
+        def fetch(t):
+            fetched = keep.tile([P, S], F32, name=f"source{t}", align_bytes=64)
             nc.vector.tensor_copy(fetched[:], planes[0, t][:].indirect(src_t[:]))
             return fetched
 
@@ -254,8 +254,8 @@ def tile_picked_hub_silu_e_kernel(tc, xT, w1, w2, w3_words, w3_scales, offs, src
                 copy(out=result[:, s0 : s0 + width], in_=acc_out[:])
             nc.sync.dma_start(out=out[:, r0 : r0 + n], in_=result[:])
 
-        sources = [fetch(0, "source0"), fetch(1, "source1")]
-        w_rounded[1, 1] = weights_tile(1, 1, "plane0_0")
+        sources = [fetch(0), fetch(1)]
+        w_rounded[1, 1] = keep.tile([P, 2, P, PACK], BF16, name="w2_rounded1", tag="plane0_0", align_bytes=64)
         round_weights(nc.scalar.copy, 1, 1, w2_raw, 0, P)
         whole_product(0, 2, 2)
         whole_product(0, 3, 4)
@@ -265,8 +265,8 @@ def tile_picked_hub_silu_e_kernel(tc, xT, w1, w2, w3_words, w3_scales, offs, src
         low_sums = keep.tile([P, 2, S], F32, name="low_sums")
         for t in range(2):
             nc.vector.tensor_tensor(low_sums[:, t, :], planes[1, t][:].indirect(dst_t[:]), sources[t][:], ADD)
-        sources.append(fetch(2, "source2"))
-        sources.append(fetch(3, "source3"))
+        sources.append(fetch(2))
+        sources.append(fetch(3))
         for c, (r0, n) in enumerate(EDGE_CHUNKS):
             activate(c, 0, low_sums[:, :, r0 : r0 + n])
 

@@ -21,15 +21,12 @@ PACK = 4
 GROUP = 16
 FLOPS = 2 * K * H * S * 2 + 2 * H * N * S
 
-PAIR_CHUNKS = ((0, 1024), (1024, 512), (1536, 512))
-ROW2_CHUNKS = ((0, 1024), (1024, 768), (1792, 256))
-ROW3_CHUNKS = ((0, 768), (768, 768), (1536, 512))
-VECTOR_SHARE = 352
-ROW2_SCALAR = (512, 320, 256)
+ROW_CHUNKS = ((0, 1024), (1024, 1024))
+ROW3_CHUNKS = ((0, 768), (768, 896), (1664, 384))
+VECTOR_NODES = 448
 PIECE = 256
 EDGE_CHUNKS = ((0, 256), (256, 384), (640, 256), (896, 128))
 SOURCE_WINDOW = 1408
-TARGET_WINDOW = S + GROUP
 
 
 def powers_of_two(n):
@@ -61,27 +58,23 @@ def tile_picked_hub_silu_e_kernel(tc, xT, w1, w2, w3_words, w3_scales, offs, src
         nc.gpsimd.memset(w3_bytes[:], 0)
 
         x_rows = xT.rearrange("(p j) c -> p j c", j=PACK)
-        pair_raw = []
-        for c, (c0, width) in enumerate(PAIR_CHUNKS):
-            pair_raw.append(keep.tile([P, 2, width], F32, name=f"pair_raw{c}"))
-            nc.sync.dma_start(out=pair_raw[c][:], in_=x_rows[:, 0:2, c0 : c0 + width])
-            if c == 0:
-                nc.sync.dma_start(offs_t[:], offs)
-        row_raw = {}
-        for j, chunks in ((2, ROW2_CHUNKS), (3, ROW3_CHUNKS)):
-            row_raw[j] = keep.tile([P, T], F32, name=f"row_raw{j}")
-            for c0, width in chunks:
+        row_raw = []
+        for j in range(PACK):
+            row_raw.append(keep.tile([P, T], F32, name=f"row_raw{j}"))
+            for c, (c0, width) in enumerate(ROW3_CHUNKS if j == PACK - 1 else ROW_CHUNKS):
                 nc.sync.dma_start(out=row_raw[j][:, c0 : c0 + width], in_=x_rows[:, j, c0 : c0 + width])
+                if j == 0 and c == 0:
+                    nc.sync.dma_start(offs_t[:], offs)
         half = H // 2
         w1_raw = [
-            keep.tile([P, PACK, half], F32, name="w1_raw0"),
+            placed.tile([P, PACK, half], F32, name="w1_raw0", offset=24576, align_bytes=64),
             placed.tile([P, PACK, half], F32, name="w1_raw1", offset=0, align_bytes=64),
         ]
         for a in range(2):
             nc.sync.dma_start(out=w1_raw[a][:], in_=w1.rearrange("(p j) c -> p j c", j=PACK)[:, :, a * half : (a + 1) * half])
+        nc.sync.dma_start(src_t[:], src)
         w2_raw = keep.tile([P, PACK, H], F32, name="w2_raw")
         nc.sync.dma_start(out=w2_raw[:], in_=w2.rearrange("(p j) c -> p j c", j=PACK))
-        nc.sync.dma_start(src_t[:], src)
         nc.sync.dma_start(dst_t[:], dst)
         nc.sync.dma_start(out=w3_codes[:].bitcast(I32), in_=w3_words[0].bitcast(I32))
         for q in range(4):
@@ -90,16 +83,11 @@ def tile_picked_hub_silu_e_kernel(tc, xT, w1, w2, w3_words, w3_scales, offs, src
                 in_=w3_scales[0, 4 * q : 4 * q + 4, :].bitcast(I32),
             )
 
-        pairs = keep.tile([P, T, 2], BF16, name="pairs", align_bytes=64)
-        rows = {j: keep.tile([P, T], BF16, name=f"row{j}", align_bytes=64) for j in (2, 3)}
+        rows = [keep.tile([P, T], BF16, name=f"row{j}", align_bytes=64) for j in range(PACK)]
         pieces = S // PIECE
-        picked = [keep.tile([P, PIECE, PACK], BF16, name=f"picked{i}", align_bytes=64) for i in range(pieces)]
+        picked = keep.tile([P, S, PACK], BF16, name="picked", align_bytes=64)
         x_codes = {}
         x_bytes = {}
-
-        def round_pairs(copy, c, lo, hi):
-            c0 = PAIR_CHUNKS[c][0]
-            copy(out=pairs[:, c0 + lo : c0 + hi, :], in_=pair_raw[c][:, :, lo:hi].rearrange("p e c -> p c e"))
 
         def gpsimd_round(out, in_):
             nc.gpsimd.tensor_scalar(out, in_, 1.0, 0.0, MULT, ADD)
@@ -107,53 +95,41 @@ def tile_picked_hub_silu_e_kernel(tc, xT, w1, w2, w3_words, w3_scales, offs, src
         def round_row(copy, j, lo, hi):
             copy(out=rows[j][:, lo:hi], in_=row_raw[j][:, lo:hi])
 
-        def gather_pairs(i):
-            window = pairs[:].rearrange("p c e -> p (c e)").bitcast(U32)
-            words = picked[i][:].rearrange("p c j -> p (c j)").bitcast(U32)
-            nc.vector.tensor_copy(words[:, 0 : 2 * PIECE : 2], window.indirect(entries(offs_t, i * PIECE, PIECE)))
-
-        def gather_row(j, i):
-            chosen = entries(offs_t, i * PIECE, PIECE)
-            if i == 0:
-                nc.vector.tensor_copy(picked[i][:, :, j], row_raw[j][:].indirect(chosen))
-            else:
-                nc.scalar.activation(picked[i][:, :, j], rows[j][:].indirect(chosen), COPY)
-
         def quantize_nodes(i):
             nc.vector.quantize_mx(
-                out=x_codes[i][:].bitcast(FP8X4), scales=x_bytes[i][:], in_=picked[i][:].rearrange("p c j -> p (c j)")
+                out=x_codes[i][:].bitcast(FP8X4), scales=x_bytes[i][:], in_=picked[:, i * PIECE : (i + 1) * PIECE, :].rearrange("p c j -> p (c j)")
             )
 
-        last = len(PAIR_CHUNKS) - 1
-        for c in range(last):
-            round_pairs(nc.vector.tensor_copy, c, 0, PAIR_CHUNKS[c][1])
-        round_pairs(nc.vector.tensor_copy, last, 0, VECTOR_SHARE)
-        round_pairs(nc.scalar.copy, last, VECTOR_SHARE, PAIR_CHUNKS[last][1])
-        for i in (1, 2, 3, 0):
-            gather_pairs(i)
-        for (c0, width), share in zip(ROW2_CHUNKS, ROW2_SCALAR):
-            round_row(nc.scalar.copy, 2, c0, c0 + share)
-            if share < width:
-                round_row(gpsimd_round, 2, c0 + share, c0 + width)
-        for i in range(pieces):
-            gather_row(2, i)
-        for c0, width in ROW3_CHUNKS:
-            round_row(gpsimd_round, 3, c0, c0 + width)
-        for i in range(pieces):
-            gather_row(3, i)
+        for j in range(PACK):
+            if j < PACK - 1:
+                round_row(gpsimd_round if j else nc.scalar.copy, j, 0, ROW_CHUNKS[1][0])
+                round_row(nc.vector.tensor_copy, j, ROW_CHUNKS[1][0], T)
+            else:
+                for (c0, width), copy in zip(ROW3_CHUNKS, (gpsimd_round, nc.vector.tensor_copy, gpsimd_round)):
+                    round_row(copy, j, c0, c0 + width)
+            n = VECTOR_NODES if j < 2 else PIECE
+            nc.vector.tensor_copy(picked[:, 0:n, j], row_raw[j][:].indirect(entries(offs_t, 0, n)))
+            cuts = range(n, S + 1, PIECE) if j == PACK - 1 else (n, S)
+            for lo, hi in zip(cuts, cuts[1:]):
+                nc.scalar.activation(picked[:, lo:hi, j], rows[j][:].indirect(entries(offs_t, lo, hi - lo)), COPY)
 
         w_rounded = {}
         w_codes = {}
         w_bytes = {}
-        for w in range(2):
-            for h in range(2):
-                w_codes[w, h] = keep.tile([P, 2 * P], U32, name=f"w_codes{w}_{h}", align_bytes=64)
-                w_bytes[w, h] = keep.tile([P, 2 * P], U8, name=f"w_bytes{w}_{h}", align_bytes=64)
+        w_codes[0, 0] = placed.tile([P, 2 * P], U32, name="w_codes0_0", offset=8192, align_bytes=64)
+        w_codes[0, 1] = placed.tile([P, 2 * P], U32, name="w_codes0_1", offset=16384, align_bytes=64)
+        for h in range(2):
+            w_bytes[0, h] = keep.tile([P, 2 * P], U8, name=f"w_bytes0_{h}", align_bytes=64)
+        w2_codes = keep.tile([P, H], U32, name="w2_codes", align_bytes=64)
+        w2_bytes = keep.tile([P, H], U8, name="w2_bytes", align_bytes=64)
+        for h in range(2):
+            w_codes[1, h] = w2_codes[:, h * 2 * P : (h + 1) * 2 * P]
+            w_bytes[1, h] = w2_bytes[:, h * 2 * P : (h + 1) * 2 * P]
 
-        def round_weights(copy, w, h, raw, m0, m1):
+        def round_weights(copy, w, h, raw, m0, m1, walk="m j t"):
             copy(
-                out=w_rounded[w, h][:, :, m0:m1, :].rearrange("p t m j -> p m j t"),
-                in_=raw[:].rearrange("p j (m t) -> p m j t", t=PACK)[:, :, :, 2 * h : 2 * h + 2],
+                out=w_rounded[w, h][:, :, m0:m1, :].rearrange("p t m j -> p " + walk),
+                in_=raw[:].rearrange("p j (m t) -> p j m t", t=PACK)[:, :, :, 2 * h : 2 * h + 2].rearrange("p j m t -> p " + walk),
             )
 
         def quantize_weights(w, h):
@@ -164,7 +140,7 @@ def tile_picked_hub_silu_e_kernel(tc, xT, w1, w2, w3_words, w3_scales, offs, src
         planes = {}
         for w in range(2):
             for t in range(PACK):
-                width = SOURCE_WINDOW if w == 0 else (TARGET_WINDOW if t < 2 else S)
+                width = SOURCE_WINDOW if w == 0 else S
                 planes[w, t] = keep.tile([P, width], F32, name=f"plane{w}_{t}", align_bytes=64)
                 if width > S:
                     nc.gpsimd.memset(planes[w, t][:, S:width], 0.0)
@@ -202,20 +178,26 @@ def tile_picked_hub_silu_e_kernel(tc, xT, w1, w2, w3_words, w3_scales, offs, src
         for a in range(2):
             for h in range(2):
                 round_weights(nc.vector.tensor_copy, 0, h, w1_raw[a], a * P // 2, (a + 1) * P // 2)
+            if a == 0:
+                x_codes[1] = placed.tile([P, PIECE], U32, name="x_codes1", offset=24576, align_bytes=64)
+                x_bytes[1] = bytes_tile(1)
+                quantize_nodes(1)
         quantize_weights(0, 0)
-        for i in range(1, pieces):
+        for i in range(2, pieces):
             x_codes[i] = placed.tile([P, PIECE], U32, name=f"x_codes{i}", offset=4 * PIECE * i, align_bytes=64)
             x_bytes[i] = bytes_tile(i)
             quantize_nodes(i)
         for i in range(pieces):
             first_product(0, 0, i, 1, i)
-        w_rounded[1, 0] = weights_tile("w2_rounded0")
-        round_weights(nc.vector.tensor_copy, 1, 0, w2_raw, 0, P)
         quantize_weights(0, 1)
-        quantize_weights(1, 0)
         whole_product(0, 1, 2)
-        whole_product(1, 0, 4)
-        whole_product(1, 1, 0)
+        w2_rounded = placed.tile([P, PACK, P, PACK], BF16, name="w2_rounded", offset=8192, align_bytes=64)
+        for h in range(2):
+            w_rounded[1, h] = w2_rounded[:, 2 * h : 2 * h + 2, :, :]
+        round_weights(gpsimd_round, 1, 0, w2_raw, 0, P, "m t j")
+        round_weights(nc.scalar.copy, 1, 1, w2_raw, 0, P)
+        first_product(0, 2, 0, 2, 4)
+        first_product(0, 2, 2, 2, 3)
 
         z = [keep.tile([P, n, PACK], BF16, name=f"z{c}", align_bytes=64) for c, (r0, n) in enumerate(EDGE_CHUNKS)]
         z_codes = keep.tile([P, S], U32, name="z_codes", align_bytes=64)
@@ -255,20 +237,29 @@ def tile_picked_hub_silu_e_kernel(tc, xT, w1, w2, w3_words, w3_scales, offs, src
             nc.sync.dma_start(out=out[:, r0 : r0 + n], in_=result[:])
 
         sources = [fetch(0), fetch(1)]
-        w_rounded[1, 1] = keep.tile([P, 2, P, PACK], BF16, name="w2_rounded1", tag="plane0_0", align_bytes=64)
-        round_weights(nc.scalar.copy, 1, 1, w2_raw, 0, P)
-        whole_product(0, 2, 2)
-        whole_product(0, 3, 4)
-        quantize_weights(1, 1)
+        nc.vector.quantize_mx(
+            out=w2_codes[:].bitcast(FP8X4), scales=w2_bytes[:], in_=w2_rounded[:].rearrange("p t m j -> p (t m j)")
+        )
+        whole_product(1, 0, 0)
+        whole_product(1, 1, 4)
+        sources.append(fetch(2))
+        first_product(0, 3, 0, 2, 2)
+        first_product(0, 3, 2, 2, 5)
         whole_product(1, 2, 0)
         whole_product(1, 3, 2)
-        low_sums = keep.tile([P, 2, S], F32, name="low_sums")
-        for t in range(2):
-            nc.vector.tensor_tensor(low_sums[:, t, :], planes[1, t][:].indirect(dst_t[:]), sources[t][:], ADD)
-        sources.append(fetch(2))
+        for first, last in ((0, 2), (2, 4)):
+            r0 = EDGE_CHUNKS[first][0]
+            n = sum(width for start, width in EDGE_CHUNKS[first:last])
+            if first == 0:
+                low = keep.tile([P, 2, n], F32, name="low0")
+            else:
+                low = placed.tile([P, 2, n], F32, name="low1", offset=16384, align_bytes=64)
+            for t in range(2):
+                nc.vector.tensor_tensor(low[:, t, :], planes[1, t][:].indirect(entries(dst_t, r0, n)), sources[t][:, r0 : r0 + n], ADD)
+            for c in range(first, last):
+                lo = EDGE_CHUNKS[c][0] - r0
+                activate(c, 0, low[:, :, lo : lo + EDGE_CHUNKS[c][1]])
         sources.append(fetch(3))
-        for c, (r0, n) in enumerate(EDGE_CHUNKS):
-            activate(c, 0, low_sums[:, :, r0 : r0 + n])
 
         for c, (r0, n) in enumerate(EDGE_CHUNKS):
             if c >= 2:

@@ -23,7 +23,7 @@ FLOPS = 2 * K * H * S * 2 + 2 * H * N * S
 
 ROW_CHUNKS = ((0, 1024), (1024, 1024))
 ROW3_CHUNKS = ((0, 768), (768, 896), (1664, 384))
-VECTOR_NODES = 448
+VECTOR_NODES = (448, 448, 416, 256)
 PIECE = 256
 EDGE_CHUNKS = ((0, 256), (256, 384), (640, 256), (896, 128))
 SOURCE_WINDOW = 1408
@@ -45,7 +45,6 @@ def tile_picked_hub_silu_e_kernel(tc, xT, w1, w2, w3_words, w3_scales, offs, src
         keep = ctx.enter_context(tc.tile_pool(name="keep", bufs=1))
         placed = ctx.enter_context(tc.tile_pool(name="placed", bufs=1))
         psum = ctx.enter_context(tc.psum_pool(name="psum", bufs=1))
-        psum_out = ctx.enter_context(tc.psum_pool(name="psum_out", bufs=2))
 
         def entries(list_tile, start, n):
             return list_tile[:, start // GROUP : (start + n) // GROUP]
@@ -107,7 +106,7 @@ def tile_picked_hub_silu_e_kernel(tc, xT, w1, w2, w3_words, w3_scales, offs, src
             else:
                 for (c0, width), copy in zip(ROW3_CHUNKS, (gpsimd_round, nc.vector.tensor_copy, gpsimd_round)):
                     round_row(copy, j, c0, c0 + width)
-            n = VECTOR_NODES if j < 2 else PIECE
+            n = VECTOR_NODES[j]
             nc.vector.tensor_copy(picked[:, 0:n, j], row_raw[j][:].indirect(entries(offs_t, 0, n)))
             cuts = range(n, S + 1, PIECE) if j == PACK - 1 else (n, S)
             for lo, hi in zip(cuts, cuts[1:]):
@@ -221,11 +220,11 @@ def tile_picked_hub_silu_e_kernel(tc, xT, w1, w2, w3_words, w3_scales, offs, src
                     in_=z[c][:, s0 : s0 + width, :].rearrange("p r t -> p (r t)"),
                 )
             result = keep.tile([P, n], F32, name=f"result{c}")
+            acc_out = psum.tile([P, n], F32, name="acc_out", tag=f"bank{c}")
             for s0, width in powers_of_two(n):
                 cols = slice(r0 + s0, r0 + s0 + width)
-                acc_out = psum_out.tile([P, width], F32, name="acc_out")
                 nc.tensor.matmul_mx(
-                    out=acc_out[:],
+                    out=acc_out[:, s0 : s0 + width],
                     lhsT=w3_codes[:].bitcast(FP4X4),
                     lhsT_scale=w3_bytes[:],
                     rhs=z_codes[:, cols].bitcast(FP8X4),
@@ -233,7 +232,7 @@ def tile_picked_hub_silu_e_kernel(tc, xT, w1, w2, w3_words, w3_scales, offs, src
                     start=True,
                     stop=True,
                 )
-                copy(out=result[:, s0 : s0 + width], in_=acc_out[:])
+            copy(out=result[:], in_=acc_out[:])
             nc.sync.dma_start(out=out[:, r0 : r0 + n], in_=result[:])
 
         sources = [fetch(0), fetch(1)]
@@ -262,11 +261,11 @@ def tile_picked_hub_silu_e_kernel(tc, xT, w1, w2, w3_words, w3_scales, offs, src
         sources.append(fetch(3))
 
         for c, (r0, n) in enumerate(EDGE_CHUNKS):
-            if c >= 2:
-                second_product(c - 2, nc.scalar.copy)
+            if c == 2:
+                second_product(0, nc.scalar.copy)
             high = keep.tile([P, 2, n], F32, name=f"high{c}", tag=f"high{c % 2}", align_bytes=64)
             for t in (2, 3):
                 nc.vector.tensor_tensor(high[:, t - 2, :], planes[1, t][:].indirect(entries(dst_t, r0, n)), sources[t][:, r0 : r0 + n], ADD)
             activate(c, 1, high[:])
-        for c in range(len(EDGE_CHUNKS) - 2, len(EDGE_CHUNKS)):
-            second_product(c, nc.vector.tensor_copy)
+        for c in range(1, len(EDGE_CHUNKS)):
+            second_product(c, nc.vector.tensor_copy if c > 1 else nc.scalar.copy)

@@ -144,7 +144,7 @@ def tile_picked_hub_silu_e_kernel(tc, xT, w1, w2, w3_words, w3_scales, offs, src
                 if width > S:
                     nc.gpsimd.memset(planes[w, t][:, S:width], 0.0)
 
-        def first_product(w, t, first, count, bank):
+        def first_product(w, t, first, count, bank, copy=nc.scalar.copy):
             cols = slice((t % 2) * P, (t % 2 + 1) * P)
             acc = psum.tile([P, count * PIECE], F32, name="acc", tag=f"bank{bank}")
             for i in range(count):
@@ -157,7 +157,7 @@ def tile_picked_hub_silu_e_kernel(tc, xT, w1, w2, w3_words, w3_scales, offs, src
                     start=True,
                     stop=True,
                 )
-            nc.scalar.copy(out=planes[w, t][:, first * PIECE : (first + count) * PIECE], in_=acc[:])
+            copy(out=planes[w, t][:, first * PIECE : (first + count) * PIECE], in_=acc[:])
 
         def whole_product(w, t, bank):
             first_product(w, t, 0, 2, bank)
@@ -187,16 +187,13 @@ def tile_picked_hub_silu_e_kernel(tc, xT, w1, w2, w3_words, w3_scales, offs, src
             x_bytes[i] = bytes_tile(i)
             quantize_nodes(i)
         for i in range(pieces):
-            first_product(0, 0, i, 1, i)
+            first_product(0, 0, i, 1, i, nc.vector.tensor_copy if i == 2 else nc.scalar.copy)
         quantize_weights(0, 1)
-        whole_product(0, 1, 2)
+        whole_product(0, 1, 0)
         w2_rounded = placed.tile([P, PACK, P, PACK], BF16, name="w2_rounded", offset=8192, align_bytes=64)
-        for h in range(2):
-            w_rounded[1, h] = w2_rounded[:, 2 * h : 2 * h + 2, :, :]
-        round_weights(gpsimd_round, 1, 0, w2_raw, 0, P, "m t j")
-        round_weights(nc.scalar.copy, 1, 1, w2_raw, 0, P)
+        nc.scalar.copy(out=w2_rounded[:].rearrange("p t m j -> p m j t"), in_=w2_raw[:].rearrange("p j (m t) -> p m j t", t=PACK))
         first_product(0, 2, 0, 2, 4)
-        first_product(0, 2, 2, 2, 3)
+        first_product(0, 2, 2, 2, 1)
 
         z = [keep.tile([P, n, PACK], BF16, name=f"z{c}", align_bytes=64) for c, (r0, n) in enumerate(EDGE_CHUNKS)]
         z_codes = keep.tile([P, S], U32, name="z_codes", align_bytes=64)
@@ -239,13 +236,13 @@ def tile_picked_hub_silu_e_kernel(tc, xT, w1, w2, w3_words, w3_scales, offs, src
         nc.vector.quantize_mx(
             out=w2_codes[:].bitcast(FP8X4), scales=w2_bytes[:], in_=w2_rounded[:].rearrange("p t m j -> p (t m j)")
         )
-        whole_product(1, 0, 0)
+        whole_product(1, 0, 2)
         whole_product(1, 1, 4)
         sources.append(fetch(2))
-        first_product(0, 3, 0, 2, 2)
+        first_product(0, 3, 0, 2, 0)
         first_product(0, 3, 2, 2, 5)
-        whole_product(1, 2, 0)
-        whole_product(1, 3, 2)
+        whole_product(1, 2, 2)
+        whole_product(1, 3, 0)
         for first, last in ((0, 2), (2, 4)):
             r0 = EDGE_CHUNKS[first][0]
             n = sum(width for start, width in EDGE_CHUNKS[first:last])

@@ -84,7 +84,7 @@ def tile_picked_hub_silu_e_kernel(tc, xT, w1, w2, w3_words, w3_scales, offs, src
 
         rows = [keep.tile([P, T], BF16, name=f"row{j}", align_bytes=64) for j in range(PACK)]
         pieces = S // PIECE
-        picked = keep.tile([P, S, PACK], BF16, name="picked", align_bytes=64)
+        picked = placed.tile([P, S, PACK], BF16, name="picked", offset=32768, align_bytes=64)
         x_codes = {}
         x_bytes = {}
 
@@ -115,8 +115,11 @@ def tile_picked_hub_silu_e_kernel(tc, xT, w1, w2, w3_words, w3_scales, offs, src
         w_rounded = {}
         w_codes = {}
         w_bytes = {}
-        w_codes[0, 0] = placed.tile([P, 2 * P], U32, name="w_codes0_0", offset=8192, align_bytes=64)
-        w_codes[0, 1] = placed.tile([P, 2 * P], U32, name="w_codes0_1", offset=16384, align_bytes=64)
+        plane_codes = [
+            keep.tile([P, P], U32, name="plane_codes0", align_bytes=64),
+            placed.tile([P, P], U32, name="plane_codes1", offset=32768, align_bytes=64),
+        ]
+        w_codes[0, 1] = placed.tile([P, 2 * P], U32, name="w_codes0_1", offset=36864, align_bytes=64)
         for h in range(2):
             w_bytes[0, h] = keep.tile([P, 2 * P], U8, name=f"w_bytes0_{h}", align_bytes=64)
         w2_codes = keep.tile([P, H], U32, name="w2_codes", align_bytes=64)
@@ -150,7 +153,7 @@ def tile_picked_hub_silu_e_kernel(tc, xT, w1, w2, w3_words, w3_scales, offs, src
             for i in range(count):
                 nc.tensor.matmul_mx(
                     out=acc[:, i * PIECE : (i + 1) * PIECE],
-                    lhsT=w_codes[w, t // 2][:, cols].bitcast(FP8X4),
+                    lhsT=(plane_codes[t][:] if w == 0 and t < 2 else w_codes[w, t // 2][:, cols]).bitcast(FP8X4),
                     lhsT_scale=w_bytes[w, t // 2][:, cols],
                     rhs=x_codes[first + i][:].bitcast(FP8X4),
                     rhs_scale=x_bytes[first + i][:],
@@ -177,20 +180,23 @@ def tile_picked_hub_silu_e_kernel(tc, xT, w1, w2, w3_words, w3_scales, offs, src
         for a in range(2):
             for h in range(2):
                 round_weights(nc.vector.tensor_copy, 0, h, w1_raw[a], a * P // 2, (a + 1) * P // 2)
-            if a == 0:
-                x_codes[1] = placed.tile([P, PIECE], U32, name="x_codes1", offset=24576, align_bytes=64)
-                x_bytes[1] = bytes_tile(1)
-                quantize_nodes(1)
-        quantize_weights(0, 0)
-        for i in range(2, pieces):
+        def quantize_plane(t):
+            cols = slice(t * P, (t + 1) * P)
+            nc.vector.quantize_mx(
+                out=plane_codes[t][:].bitcast(FP8X4), scales=w_bytes[0, 0][:, cols], in_=w_rounded[0, 0][:, t].rearrange("p m j -> p (m j)")
+            )
+
+        quantize_plane(0)
+        for i in range(1, pieces):
             x_codes[i] = placed.tile([P, PIECE], U32, name=f"x_codes{i}", offset=4 * PIECE * i, align_bytes=64)
             x_bytes[i] = bytes_tile(i)
             quantize_nodes(i)
+        quantize_plane(1)
         for i in range(pieces):
-            first_product(0, 0, i, 1, i, nc.vector.tensor_copy if i == 2 else nc.scalar.copy)
+            first_product(0, 0, i, 1, i)
         quantize_weights(0, 1)
         whole_product(0, 1, 0)
-        w2_rounded = placed.tile([P, PACK, P, PACK], BF16, name="w2_rounded", offset=8192, align_bytes=64)
+        w2_rounded = placed.tile([P, PACK, P, PACK], BF16, name="w2_rounded", offset=32768, align_bytes=64)
         nc.scalar.copy(out=w2_rounded[:].rearrange("p t m j -> p m j t"), in_=w2_raw[:].rearrange("p j (m t) -> p m j t", t=PACK))
         first_product(0, 2, 0, 2, 4)
         first_product(0, 2, 2, 2, 1)
@@ -249,7 +255,7 @@ def tile_picked_hub_silu_e_kernel(tc, xT, w1, w2, w3_words, w3_scales, offs, src
             if first == 0:
                 low = keep.tile([P, 2, n], F32, name="low0")
             else:
-                low = placed.tile([P, 2, n], F32, name="low1", offset=16384, align_bytes=64)
+                low = placed.tile([P, 2, n], F32, name="low1", offset=36864, align_bytes=64)
             for t in range(2):
                 nc.vector.tensor_tensor(low[:, t, :], planes[1, t][:].indirect(entries(dst_t, r0, n)), sources[t][:, r0 : r0 + n], ADD)
             for c in range(first, last):

@@ -23,7 +23,8 @@ FLOPS = 2 * K * H * S * 2 + 2 * H * N * S
 
 ROW_CHUNKS = ((0, 1024), (1024, 1024))
 ROW3_CHUNKS = ((0, 768), (768, 896), (1664, 384))
-VECTOR_NODES = (448, 448, 416, 256)
+VECTOR_NODES = (448, 448, 320, 256)
+W1_FIRST = 320
 PIECE = 256
 EDGE_CHUNKS = ((0, 256), (256, 384), (640, 256), (896, 128))
 SOURCE_WINDOW = 1408
@@ -64,13 +65,13 @@ def tile_picked_hub_silu_e_kernel(tc, xT, w1, w2, w3_words, w3_scales, offs, src
                 nc.sync.dma_start(out=row_raw[j][:, c0 : c0 + width], in_=x_rows[:, j, c0 : c0 + width])
                 if j == 0 and c == 0:
                     nc.sync.dma_start(offs_t[:], offs)
-        half = H // 2
+        w1_cuts = (0, W1_FIRST, H)
         w1_raw = [
-            placed.tile([P, PACK, half], F32, name="w1_raw0", offset=24576, align_bytes=64),
-            placed.tile([P, PACK, half], F32, name="w1_raw1", offset=0, align_bytes=64),
+            keep.tile([P, PACK, W1_FIRST], F32, name="w1_raw0", align_bytes=64),
+            placed.tile([P, PACK, H - W1_FIRST], F32, name="w1_raw1", offset=0, align_bytes=64),
         ]
         for a in range(2):
-            nc.sync.dma_start(out=w1_raw[a][:], in_=w1.rearrange("(p j) c -> p j c", j=PACK)[:, :, a * half : (a + 1) * half])
+            nc.sync.dma_start(out=w1_raw[a][:], in_=w1.rearrange("(p j) c -> p j c", j=PACK)[:, :, w1_cuts[a] : w1_cuts[a + 1]])
         nc.sync.dma_start(src_t[:], src)
         w2_raw = keep.tile([P, PACK, H], F32, name="w2_raw")
         nc.sync.dma_start(out=w2_raw[:], in_=w2.rearrange("(p j) c -> p j c", j=PACK))
@@ -179,7 +180,7 @@ def tile_picked_hub_silu_e_kernel(tc, xT, w1, w2, w3_words, w3_scales, offs, src
             w_rounded[0, h] = weights_tile(f"w1_rounded{h}")
         for a in range(2):
             for h in range(2):
-                round_weights(nc.vector.tensor_copy, 0, h, w1_raw[a], a * P // 2, (a + 1) * P // 2)
+                round_weights(nc.vector.tensor_copy, 0, h, w1_raw[a], w1_cuts[a] // PACK, w1_cuts[a + 1] // PACK)
         def quantize_plane(t):
             cols = slice(t * P, (t + 1) * P)
             nc.vector.quantize_mx(
@@ -188,7 +189,7 @@ def tile_picked_hub_silu_e_kernel(tc, xT, w1, w2, w3_words, w3_scales, offs, src
 
         quantize_plane(0)
         for i in range(1, pieces):
-            x_codes[i] = placed.tile([P, PIECE], U32, name=f"x_codes{i}", offset=4 * PIECE * i, align_bytes=64)
+            x_codes[i] = placed.tile([P, PIECE], U32, name=f"x_codes{i}", offset=4 * PIECE * (i - 1), align_bytes=64)
             x_bytes[i] = bytes_tile(i)
             quantize_nodes(i)
         quantize_plane(1)

@@ -23,8 +23,8 @@ FLOPS = 2 * K * H * S * 2 + 2 * H * N * S
 
 ROW_CHUNKS = ((0, 1024), (1024, 1024))
 ROW3_CHUNKS = ((0, 768), (768, 896), (1664, 384))
-VECTOR_NODES = (448, 448, 320, 256)
-W1_FIRST = 320
+VECTOR_NODES = (448, 448, 416, 256)
+W1_CUTS = (0, 192, 384, 512)
 PIECE = 256
 EDGE_CHUNKS = ((0, 256), (256, 384), (640, 256), (896, 128))
 SOURCE_WINDOW = 1408
@@ -61,16 +61,19 @@ def tile_picked_hub_silu_e_kernel(tc, xT, w1, w2, w3_words, w3_scales, offs, src
         row_raw = []
         for j in range(PACK):
             row_raw.append(keep.tile([P, T], F32, name=f"row_raw{j}"))
-            for c, (c0, width) in enumerate(ROW3_CHUNKS if j == PACK - 1 else ROW_CHUNKS):
+            for c, (c0, width) in enumerate(((0, T),) if j == 0 else ROW3_CHUNKS if j == PACK - 1 else ROW_CHUNKS):
                 nc.sync.dma_start(out=row_raw[j][:, c0 : c0 + width], in_=x_rows[:, j, c0 : c0 + width])
                 if j == 0 and c == 0:
                     nc.sync.dma_start(offs_t[:], offs)
-        w1_cuts = (0, W1_FIRST, H)
-        w1_raw = [
-            keep.tile([P, PACK, W1_FIRST], F32, name="w1_raw0", align_bytes=64),
-            placed.tile([P, PACK, H - W1_FIRST], F32, name="w1_raw1", offset=0, align_bytes=64),
-        ]
-        for a in range(2):
+        w1_cuts = W1_CUTS
+        parts = len(w1_cuts) - 1
+        w1_raw = []
+        for a in range(parts):
+            shape = [P, PACK, w1_cuts[a + 1] - w1_cuts[a]]
+            if a < parts - 1:
+                w1_raw.append(keep.tile(shape, F32, name=f"w1_raw{a}", align_bytes=64))
+            else:
+                w1_raw.append(placed.tile(shape, F32, name=f"w1_raw{a}", offset=0, align_bytes=64))
             nc.sync.dma_start(out=w1_raw[a][:], in_=w1.rearrange("(p j) c -> p j c", j=PACK)[:, :, w1_cuts[a] : w1_cuts[a + 1]])
         nc.sync.dma_start(src_t[:], src)
         w2_raw = keep.tile([P, PACK, H], F32, name="w2_raw")
@@ -178,7 +181,7 @@ def tile_picked_hub_silu_e_kernel(tc, xT, w1, w2, w3_words, w3_scales, offs, src
         quantize_nodes(0)
         for h in range(2):
             w_rounded[0, h] = weights_tile(f"w1_rounded{h}")
-        for a in range(2):
+        for a in range(parts):
             for h in range(2):
                 round_weights(nc.vector.tensor_copy, 0, h, w1_raw[a], w1_cuts[a] // PACK, w1_cuts[a + 1] // PACK)
         def quantize_plane(t):
@@ -189,8 +192,8 @@ def tile_picked_hub_silu_e_kernel(tc, xT, w1, w2, w3_words, w3_scales, offs, src
 
         quantize_plane(0)
         for i in range(1, pieces):
-            x_codes[i] = placed.tile([P, PIECE], U32, name=f"x_codes{i}", offset=4 * PIECE * (i - 1), align_bytes=64)
-            x_bytes[i] = bytes_tile(i)
+            x_codes[i] = keep.tile([P, PIECE], U32, name=f"x_codes{i}", align_bytes=64)
+            x_bytes[i] = placed.tile([P, PIECE], U8, name=f"x_bytes{i}", offset=PIECE * i, align_bytes=64)
             quantize_nodes(i)
         quantize_plane(1)
         for i in range(pieces):

@@ -21,23 +21,28 @@ PACK = 4
 GROUP = 16
 FLOPS = 2 * K * H * S * 2 + 2 * H * N * S
 
-ROW_CHUNKS = ((0, 1024), (1024, 1024))
-ROW3_CHUNKS = ((0, 768), (768, 896), (1664, 384))
-VECTOR_NODES = (448, 448, 416, 256)
-W1_CUTS = (0, 192, 384, 512)
+LOAD_CUTS = ((0, T), (0, T // 2, T), (0, T // 2, T), (0, 896, 1664, T))
+VECTOR_NODES = (416, 416, 352, 256)
+W1_CUTS = (0, 192, 384, H)
 PIECE = 256
-EDGE_CHUNKS = ((0, 256), (256, 384), (640, 256), (896, 128))
+EDGE_RANGES = ((0, 256), (256, 384), (640, 256), (896, 128))
 SOURCE_WINDOW = 1408
+
+AT_W1_LAST = 0
+AT_W2_CODES = 8192
+AT_NODE_CODES = 16384
+AT_PICKED = 32768
+AT_SUMS = (AT_W2_CODES + 256 - 3072, AT_W2_CODES + 1792, AT_NODE_CODES + 3 * 4096, AT_W2_CODES + 256)
 
 
 def powers_of_two(n):
-    pieces = []
+    parts = []
     start = 0
     for width in (256, 128):
         if n - start >= width:
-            pieces.append((start, width))
+            parts.append((start, width))
             start = start + width
-    return pieces
+    return parts
 
 
 def tile_picked_hub_silu_e_kernel(tc, xT, w1, w2, w3_words, w3_scales, offs, src, dst, out):
@@ -61,20 +66,18 @@ def tile_picked_hub_silu_e_kernel(tc, xT, w1, w2, w3_words, w3_scales, offs, src
         row_raw = []
         for j in range(PACK):
             row_raw.append(keep.tile([P, T], F32, name=f"row_raw{j}"))
-            for c, (c0, width) in enumerate(((0, T),) if j == 0 else ROW3_CHUNKS if j == PACK - 1 else ROW_CHUNKS):
-                nc.sync.dma_start(out=row_raw[j][:, c0 : c0 + width], in_=x_rows[:, j, c0 : c0 + width])
-                if j == 0 and c == 0:
-                    nc.sync.dma_start(offs_t[:], offs)
-        w1_cuts = W1_CUTS
-        parts = len(w1_cuts) - 1
+            for lo, hi in zip(LOAD_CUTS[j], LOAD_CUTS[j][1:]):
+                nc.sync.dma_start(out=row_raw[j][:, lo:hi], in_=x_rows[:, j, lo:hi])
+            if j == 0:
+                nc.sync.dma_start(offs_t[:], offs)
+        w1_parts = list(zip(W1_CUTS, W1_CUTS[1:]))
         w1_raw = []
-        for a in range(parts):
-            shape = [P, PACK, w1_cuts[a + 1] - w1_cuts[a]]
-            if a < parts - 1:
-                w1_raw.append(keep.tile(shape, F32, name=f"w1_raw{a}", align_bytes=64))
+        for a, (lo, hi) in enumerate(w1_parts):
+            if hi < H:
+                w1_raw.append(keep.tile([P, PACK, hi - lo], F32, name=f"w1_raw{a}", align_bytes=64))
             else:
-                w1_raw.append(placed.tile(shape, F32, name=f"w1_raw{a}", offset=0, align_bytes=64))
-            nc.sync.dma_start(out=w1_raw[a][:], in_=w1.rearrange("(p j) c -> p j c", j=PACK)[:, :, w1_cuts[a] : w1_cuts[a + 1]])
+                w1_raw.append(placed.tile([P, PACK, hi - lo], F32, name=f"w1_raw{a}", offset=AT_W1_LAST, align_bytes=64))
+            nc.sync.dma_start(out=w1_raw[a][:], in_=w1.rearrange("(p j) c -> p j c", j=PACK)[:, :, lo:hi])
         nc.sync.dma_start(src_t[:], src)
         w2_raw = keep.tile([P, PACK, H], F32, name="w2_raw")
         nc.sync.dma_start(out=w2_raw[:], in_=w2.rearrange("(p j) c -> p j c", j=PACK))
@@ -86,139 +89,121 @@ def tile_picked_hub_silu_e_kernel(tc, xT, w1, w2, w3_words, w3_scales, offs, src
                 in_=w3_scales[0, 4 * q : 4 * q + 4, :].bitcast(I32),
             )
 
-        rows = [keep.tile([P, T], BF16, name=f"row{j}", align_bytes=64) for j in range(PACK)]
+        row_rounded = [keep.tile([P, T], BF16, name=f"row_rounded{j}", align_bytes=64) for j in range(PACK)]
         pieces = S // PIECE
-        picked = placed.tile([P, S, PACK], BF16, name="picked", offset=32768, align_bytes=64)
+        picked = placed.tile([P, S, PACK], BF16, name="picked", offset=AT_PICKED, align_bytes=64)
         x_codes = {}
         x_bytes = {}
 
         def gpsimd_round(out, in_):
             nc.gpsimd.tensor_scalar(out, in_, 1.0, 0.0, MULT, ADD)
 
-        def round_row(copy, j, lo, hi):
-            copy(out=rows[j][:, lo:hi], in_=row_raw[j][:, lo:hi])
-
         def quantize_nodes(i):
             nc.vector.quantize_mx(
-                out=x_codes[i][:].bitcast(FP8X4), scales=x_bytes[i][:], in_=picked[:, i * PIECE : (i + 1) * PIECE, :].rearrange("p c j -> p (c j)")
+                out=x_codes[i][:].bitcast(FP8X4),
+                scales=x_bytes[i][:],
+                in_=picked[:, i * PIECE : (i + 1) * PIECE, :].rearrange("p c j -> p (c j)"),
             )
 
+        rounders = (
+            (nc.scalar.copy, nc.vector.tensor_copy),
+            (gpsimd_round, nc.vector.tensor_copy),
+            (gpsimd_round, nc.vector.tensor_copy),
+            (gpsimd_round, nc.vector.tensor_copy, gpsimd_round),
+        )
         for j in range(PACK):
-            if j < PACK - 1:
-                round_row(gpsimd_round if j else nc.scalar.copy, j, 0, ROW_CHUNKS[1][0])
-                round_row(nc.vector.tensor_copy, j, ROW_CHUNKS[1][0], T)
-            else:
-                for (c0, width), copy in zip(ROW3_CHUNKS, (gpsimd_round, nc.vector.tensor_copy, gpsimd_round)):
-                    round_row(copy, j, c0, c0 + width)
+            round_cuts = LOAD_CUTS[max(j, 1)]
+            for lo, hi, copy in zip(round_cuts, round_cuts[1:], rounders[j]):
+                copy(out=row_rounded[j][:, lo:hi], in_=row_raw[j][:, lo:hi])
             n = VECTOR_NODES[j]
             nc.vector.tensor_copy(picked[:, 0:n, j], row_raw[j][:].indirect(entries(offs_t, 0, n)))
-            cuts = range(n, S + 1, PIECE) if j == PACK - 1 else (n, S)
-            for lo, hi in zip(cuts, cuts[1:]):
-                nc.scalar.activation(picked[:, lo:hi, j], rows[j][:].indirect(entries(offs_t, lo, hi - lo)), COPY)
+            gather_cuts = range(n, S + 1, PIECE) if j == PACK - 1 else (n, S)
+            for lo, hi in zip(gather_cuts, gather_cuts[1:]):
+                nc.scalar.activation(picked[:, lo:hi, j], row_rounded[j][:].indirect(entries(offs_t, lo, hi - lo)), COPY)
 
-        w_rounded = {}
-        w_codes = {}
-        w_bytes = {}
-        plane_codes = [
-            keep.tile([P, P], U32, name="plane_codes0", align_bytes=64),
-            placed.tile([P, P], U32, name="plane_codes1", offset=32768, align_bytes=64),
-        ]
-        w_codes[0, 1] = placed.tile([P, 2 * P], U32, name="w_codes0_1", offset=36864, align_bytes=64)
-        for h in range(2):
-            w_bytes[0, h] = keep.tile([P, 2 * P], U8, name=f"w_bytes0_{h}", align_bytes=64)
-        w2_codes = keep.tile([P, H], U32, name="w2_codes", align_bytes=64)
+        w1_codes0 = keep.tile([P, P], U32, name="w1_codes0", align_bytes=64)
+        w1_codes1 = placed.tile([P, P], U32, name="w1_codes1", offset=AT_PICKED, align_bytes=64)
+        w1_codes23 = placed.tile([P, 2 * P], U32, name="w1_codes23", offset=AT_PICKED + 4096, align_bytes=64)
+        w1_bytes01 = keep.tile([P, 2 * P], U8, name="w1_bytes01", align_bytes=64)
+        w1_bytes23 = keep.tile([P, 2 * P], U8, name="w1_bytes23", align_bytes=64)
+        w2_codes = placed.tile([P, H], U32, name="w2_codes", offset=AT_W2_CODES, align_bytes=64)
         w2_bytes = keep.tile([P, H], U8, name="w2_bytes", align_bytes=64)
-        for h in range(2):
-            w_codes[1, h] = w2_codes[:, h * 2 * P : (h + 1) * 2 * P]
-            w_bytes[1, h] = w2_bytes[:, h * 2 * P : (h + 1) * 2 * P]
-
-        def round_weights(copy, w, h, raw, m0, m1, walk="m j t"):
-            copy(
-                out=w_rounded[w, h][:, :, m0:m1, :].rearrange("p t m j -> p " + walk),
-                in_=raw[:].rearrange("p j (m t) -> p j m t", t=PACK)[:, :, :, 2 * h : 2 * h + 2].rearrange("p j m t -> p " + walk),
-            )
-
-        def quantize_weights(w, h):
-            nc.vector.quantize_mx(
-                out=w_codes[w, h][:].bitcast(FP8X4), scales=w_bytes[w, h][:], in_=w_rounded[w, h][:].rearrange("p t m j -> p (t m j)")
-            )
+        w_codes = {(0, 0): w1_codes0[:], (0, 1): w1_codes1[:], (0, 2): w1_codes23[:, 0:P], (0, 3): w1_codes23[:, P : 2 * P]}
+        w_bytes = {}
+        for t in range(PACK):
+            w_bytes[0, t] = (w1_bytes01 if t < 2 else w1_bytes23)[:, (t % 2) * P : (t % 2 + 1) * P]
+            w_codes[1, t] = w2_codes[:, t * P : (t + 1) * P]
+            w_bytes[1, t] = w2_bytes[:, t * P : (t + 1) * P]
 
         planes = {}
         for w in range(2):
             for t in range(PACK):
-                width = SOURCE_WINDOW if w == 0 else S
+                width = SOURCE_WINDOW if w == 0 else (S + GROUP if t == 0 else S)
                 planes[w, t] = keep.tile([P, width], F32, name=f"plane{w}_{t}", align_bytes=64)
                 if width > S:
                     nc.gpsimd.memset(planes[w, t][:, S:width], 0.0)
 
-        def first_product(w, t, first, count, bank, copy=nc.scalar.copy):
-            cols = slice((t % 2) * P, (t % 2 + 1) * P)
+        def first_product(w, t, first, count, bank):
             acc = psum.tile([P, count * PIECE], F32, name="acc", tag=f"bank{bank}")
             for i in range(count):
                 nc.tensor.matmul_mx(
                     out=acc[:, i * PIECE : (i + 1) * PIECE],
-                    lhsT=(plane_codes[t][:] if w == 0 and t < 2 else w_codes[w, t // 2][:, cols]).bitcast(FP8X4),
-                    lhsT_scale=w_bytes[w, t // 2][:, cols],
+                    lhsT=w_codes[w, t].bitcast(FP8X4),
+                    lhsT_scale=w_bytes[w, t],
                     rhs=x_codes[first + i][:].bitcast(FP8X4),
                     rhs_scale=x_bytes[first + i][:],
                     start=True,
                     stop=True,
                 )
-            copy(out=planes[w, t][:, first * PIECE : (first + count) * PIECE], in_=acc[:])
+            nc.scalar.copy(out=planes[w, t][:, first * PIECE : (first + count) * PIECE], in_=acc[:])
 
-        def whole_product(w, t, bank):
-            first_product(w, t, 0, 2, bank)
-            first_product(w, t, 2, 2, bank + 1)
-
-        def weights_tile(name):
-            return keep.tile([P, 2, P, PACK], BF16, name=name, align_bytes=64)
-
-        def bytes_tile(i):
-            return keep.tile([P, PIECE], U8, name=f"x_bytes{i}", align_bytes=64)
+        def whole_product(w, t, banks):
+            for half, bank in enumerate(banks):
+                first_product(w, t, 2 * half, 2, bank)
 
         x_codes[0] = keep.tile([P, PIECE], U32, name="x_codes0", align_bytes=64)
-        x_bytes[0] = bytes_tile(0)
+        x_bytes[0] = keep.tile([P, PIECE], U8, name="x_bytes0", align_bytes=64)
         quantize_nodes(0)
-        for h in range(2):
-            w_rounded[0, h] = weights_tile(f"w1_rounded{h}")
-        for a in range(parts):
+        w1_rounded = [keep.tile([P, 2, P, PACK], BF16, name=f"w1_rounded{h}", align_bytes=64) for h in range(2)]
+        for a, (lo, hi) in enumerate(w1_parts):
             for h in range(2):
-                round_weights(nc.vector.tensor_copy, 0, h, w1_raw[a], w1_cuts[a] // PACK, w1_cuts[a + 1] // PACK)
-        def quantize_plane(t):
-            cols = slice(t * P, (t + 1) * P)
+                nc.vector.tensor_copy(
+                    out=w1_rounded[h][:, :, lo // PACK : hi // PACK, :].rearrange("p u m j -> p m j u"),
+                    in_=w1_raw[a][:].rearrange("p j (m t) -> p j m t", t=PACK)[:, :, :, 2 * h : 2 * h + 2].rearrange("p j m u -> p m j u"),
+                )
+
+        def quantize_w1_plane(t):
             nc.vector.quantize_mx(
-                out=plane_codes[t][:].bitcast(FP8X4), scales=w_bytes[0, 0][:, cols], in_=w_rounded[0, 0][:, t].rearrange("p m j -> p (m j)")
+                out=w_codes[0, t].bitcast(FP8X4), scales=w_bytes[0, t], in_=w1_rounded[0][:, t].rearrange("p m j -> p (m j)")
             )
 
-        quantize_plane(0)
+        quantize_w1_plane(0)
         for i in range(1, pieces):
-            x_codes[i] = keep.tile([P, PIECE], U32, name=f"x_codes{i}", align_bytes=64)
-            x_bytes[i] = placed.tile([P, PIECE], U8, name=f"x_bytes{i}", offset=PIECE * i, align_bytes=64)
+            x_codes[i] = placed.tile([P, PIECE], U32, name=f"x_codes{i}", offset=AT_NODE_CODES + 4096 * i, align_bytes=64)
+            x_bytes[i] = placed.tile([P, PIECE], U8, name=f"x_bytes{i}", offset=AT_W1_LAST + PIECE * i, align_bytes=64)
             quantize_nodes(i)
-        quantize_plane(1)
+        quantize_w1_plane(1)
         for i in range(pieces):
             first_product(0, 0, i, 1, i)
-        quantize_weights(0, 1)
-        whole_product(0, 1, 0)
-        w2_rounded = placed.tile([P, PACK, P, PACK], BF16, name="w2_rounded", offset=32768, align_bytes=64)
+        nc.vector.quantize_mx(
+            out=w1_codes23[:].bitcast(FP8X4), scales=w1_bytes23[:], in_=w1_rounded[1][:].rearrange("p u m j -> p (u m j)")
+        )
+        whole_product(0, 1, (0, 1))
+        w2_rounded = placed.tile([P, PACK, P, PACK], BF16, name="w2_rounded", offset=AT_PICKED, align_bytes=64)
         nc.scalar.copy(out=w2_rounded[:].rearrange("p t m j -> p m j t"), in_=w2_raw[:].rearrange("p j (m t) -> p m j t", t=PACK))
-        first_product(0, 2, 0, 2, 4)
-        first_product(0, 2, 2, 2, 1)
+        whole_product(0, 2, (4, 1))
 
-        z = [keep.tile([P, n, PACK], BF16, name=f"z{c}", align_bytes=64) for c, (r0, n) in enumerate(EDGE_CHUNKS)]
+        z = [keep.tile([P, n, PACK], BF16, name=f"z{c}", align_bytes=64) for c, (r0, n) in enumerate(EDGE_RANGES)]
         z_codes = keep.tile([P, S], U32, name="z_codes", align_bytes=64)
         z_bytes = keep.tile([P, S], U8, name="z_bytes", align_bytes=64)
 
-        def fetch(t):
+        def fetch_sources(t):
             fetched = keep.tile([P, S], F32, name=f"source{t}", align_bytes=64)
             nc.vector.tensor_copy(fetched[:], planes[0, t][:].indirect(src_t[:]))
             return fetched
 
-        def activate(c, h, sums):
-            nc.scalar.activation(z[c][:, :, 2 * h : 2 * h + 2], sums.rearrange("p t r -> p r t"), SILU)
-
         def second_product(c, copy):
-            r0, n = EDGE_CHUNKS[c]
+            r0, n = EDGE_RANGES[c]
             for s0, width in powers_of_two(n):
                 cols = slice(r0 + s0, r0 + s0 + width)
                 nc.vector.quantize_mx(
@@ -242,37 +227,32 @@ def tile_picked_hub_silu_e_kernel(tc, xT, w1, w2, w3_words, w3_scales, offs, src
             copy(out=result[:], in_=acc_out[:])
             nc.sync.dma_start(out=out[:, r0 : r0 + n], in_=result[:])
 
-        sources = [fetch(0), fetch(1)]
+        sources = [fetch_sources(0), fetch_sources(1)]
         nc.vector.quantize_mx(
             out=w2_codes[:].bitcast(FP8X4), scales=w2_bytes[:], in_=w2_rounded[:].rearrange("p t m j -> p (t m j)")
         )
-        whole_product(1, 0, 2)
-        whole_product(1, 1, 4)
-        sources.append(fetch(2))
-        first_product(0, 3, 0, 2, 0)
-        first_product(0, 3, 2, 2, 5)
-        whole_product(1, 2, 2)
-        whole_product(1, 3, 0)
-        for first, last in ((0, 2), (2, 4)):
-            r0 = EDGE_CHUNKS[first][0]
-            n = sum(width for start, width in EDGE_CHUNKS[first:last])
-            if first == 0:
-                low = keep.tile([P, 2, n], F32, name="low0")
-            else:
-                low = placed.tile([P, 2, n], F32, name="low1", offset=36864, align_bytes=64)
-            for t in range(2):
-                nc.vector.tensor_tensor(low[:, t, :], planes[1, t][:].indirect(entries(dst_t, r0, n)), sources[t][:, r0 : r0 + n], ADD)
-            for c in range(first, last):
-                lo = EDGE_CHUNKS[c][0] - r0
-                activate(c, 0, low[:, :, lo : lo + EDGE_CHUNKS[c][1]])
-        sources.append(fetch(3))
+        whole_product(1, 0, (2, 3))
+        sources.append(fetch_sources(2))
+        whole_product(0, 3, (0, 5))
+        whole_product(1, 1, (2, 3))
+        whole_product(1, 2, (4, 5))
+        whole_product(1, 3, (4, 5))
 
-        for c, (r0, n) in enumerate(EDGE_CHUNKS):
+        sums0 = keep.tile([P, S], F32, name="sums0", align_bytes=64)
+        nc.vector.tensor_tensor(sums0[:], planes[1, 0][:].indirect(dst_t[:]), sources[0][:], ADD)
+        for c, (r0, n) in enumerate(EDGE_RANGES):
+            nc.scalar.activation(z[c][:, :, 0], sums0[:, r0 : r0 + n], SILU)
+        sources.append(fetch_sources(3))
+
+        for c, (r0, n) in enumerate(EDGE_RANGES):
             if c == 2:
                 second_product(0, nc.scalar.copy)
-            high = keep.tile([P, 2, n], F32, name=f"high{c}", tag=f"high{c % 2}", align_bytes=64)
-            for t in (2, 3):
-                nc.vector.tensor_tensor(high[:, t - 2, :], planes[1, t][:].indirect(entries(dst_t, r0, n)), sources[t][:, r0 : r0 + n], ADD)
-            activate(c, 1, high[:])
-        for c in range(1, len(EDGE_CHUNKS)):
-            second_product(c, nc.vector.tensor_copy if c > 1 else nc.scalar.copy)
+            sums = placed.tile([P, PACK - 1, n], F32, name=f"sums_range{c}", offset=AT_SUMS[c], align_bytes=64)
+            for t in range(1, PACK):
+                nc.vector.tensor_tensor(sums[:, t - 1, :], planes[1, t][:].indirect(entries(dst_t, r0, n)), sources[t][:, r0 : r0 + n], ADD)
+            nc.scalar.activation(
+                z[c][:, :, 1:PACK].rearrange("p (r i) t -> p r t i", i=2), sums[:].rearrange("p t (r i) -> p r t i", i=2), SILU
+            )
+        second_product(1, nc.scalar.copy)
+        for c in range(2, len(EDGE_RANGES)):
+            second_product(c, nc.vector.tensor_copy)

@@ -143,7 +143,7 @@ def tile_picked_hub_silu_e_kernel(tc, xT, w1, w2, w3_words, w3_scales, offs, src
                 if width > S:
                     nc.gpsimd.memset(planes[w, t][:, S:width], 0.0)
 
-        def first_product(w, t, first, count, bank):
+        def first_product(w, t, first, count, bank, copy=nc.scalar.copy):
             acc = psum.tile([P, count * PIECE], F32, name="acc", tag=f"bank{bank}")
             for i in range(count):
                 nc.tensor.matmul_mx(
@@ -155,7 +155,7 @@ def tile_picked_hub_silu_e_kernel(tc, xT, w1, w2, w3_words, w3_scales, offs, src
                     start=True,
                     stop=True,
                 )
-            nc.scalar.copy(out=planes[w, t][:, first * PIECE : (first + count) * PIECE], in_=acc[:])
+            copy(out=planes[w, t][:, first * PIECE : (first + count) * PIECE], in_=acc[:])
 
         def whole_product(w, t, banks):
             for half, bank in enumerate(banks):
@@ -164,17 +164,17 @@ def tile_picked_hub_silu_e_kernel(tc, xT, w1, w2, w3_words, w3_scales, offs, src
         x_codes[0] = keep.tile([P, PIECE], U32, name="x_codes0", align_bytes=64)
         x_bytes[0] = keep.tile([P, PIECE], U8, name="x_bytes0", align_bytes=64)
         quantize_nodes(0)
-        w1_rounded = [keep.tile([P, 2, P, PACK], BF16, name=f"w1_rounded{h}", align_bytes=64) for h in range(2)]
+        w1_rounded = keep.tile([P, PACK, P, PACK], BF16, name="w1_rounded", align_bytes=64)
         for a, (lo, hi) in enumerate(w1_parts):
-            for h in range(2):
+            for t0, t1 in ((0, PACK),) if hi < H else ((0, 2), (2, PACK)):
                 nc.vector.tensor_copy(
-                    out=w1_rounded[h][:, :, lo // PACK : hi // PACK, :].rearrange("p u m j -> p m j u"),
-                    in_=w1_raw[a][:].rearrange("p j (m t) -> p j m t", t=PACK)[:, :, :, 2 * h : 2 * h + 2].rearrange("p j m u -> p m j u"),
+                    out=w1_rounded[:, t0:t1, lo // PACK : hi // PACK, :].rearrange("p t m j -> p m j t"),
+                    in_=w1_raw[a][:].rearrange("p j (m t) -> p m j t", t=PACK)[:, :, :, t0:t1],
                 )
 
         def quantize_w1_plane(t):
             nc.vector.quantize_mx(
-                out=w_codes[0, t].bitcast(FP8X4), scales=w_bytes[0, t], in_=w1_rounded[0][:, t].rearrange("p m j -> p (m j)")
+                out=w_codes[0, t].bitcast(FP8X4), scales=w_bytes[0, t], in_=w1_rounded[:, t].rearrange("p m j -> p (m j)")
             )
 
         quantize_w1_plane(0)
@@ -184,9 +184,9 @@ def tile_picked_hub_silu_e_kernel(tc, xT, w1, w2, w3_words, w3_scales, offs, src
             quantize_nodes(i)
         quantize_w1_plane(1)
         for i in range(pieces):
-            first_product(0, 0, i, 1, i)
+            first_product(0, 0, i, 1, i, nc.vector.tensor_copy if i == 0 else nc.scalar.copy)
         nc.vector.quantize_mx(
-            out=w1_codes23[:].bitcast(FP8X4), scales=w1_bytes23[:], in_=w1_rounded[1][:].rearrange("p u m j -> p (u m j)")
+            out=w1_codes23[:].bitcast(FP8X4), scales=w1_bytes23[:], in_=w1_rounded[:, 2:PACK].rearrange("p t m j -> p (t m j)")
         )
         whole_product(0, 1, (0, 1))
         w2_rounded = placed.tile([P, PACK, P, PACK], BF16, name="w2_rounded", offset=AT_PICKED, align_bytes=64)

@@ -19,23 +19,18 @@ K, T, S, H, N = 512, 2048, 1024, 512, 128
 P = 128
 PACK = 4
 GROUP = 16
+BANKS = 8
 FLOPS = 2 * K * H * S * 2 + 2 * H * N * S
 
 LOAD_CUTS = ((0, T), (0, T // 2, T), (0, T // 2, T), (0, 896, 1664, T))
 VECTOR_NODES = (416, 416, 352, 256)
 W1_CUTS = (0, 192, 384, H)
 PIECE = 256
-EDGE_RANGES = ((0, 256), (256, 384), (640, 256), (896, 128))
-SOURCE_WINDOW = 1408
-
-AT_W1_LAST = 0
-AT_W2_CODES = 8192
-AT_NODE_CODES = 16384
-AT_PICKED = 32768
-AT_SUMS = (AT_W2_CODES + 256 - 3072, AT_W2_CODES + 1792, AT_NODE_CODES + 3 * 4096, AT_W2_CODES + 256)
+HALF = S // 2
+EDGE_RANGES = ((0, 384), (384, 256), (640, 256), (896, 128))
 
 
-def powers_of_two(n):
+def pass_widths(n):
     parts = []
     start = 0
     for width in (256, 128):
@@ -54,6 +49,11 @@ def tile_picked_hub_silu_e_kernel(tc, xT, w1, w2, w3_words, w3_scales, offs, src
 
         def entries(list_tile, start, n):
             return list_tile[:, start // GROUP : (start + n) // GROUP]
+
+        warm_in = keep.tile([P, 1], F32, name="warm_in")
+        warm_out = keep.tile([P, 1], F32, name="warm_out")
+        nc.gpsimd.memset(warm_in[:], 0.0)
+        nc.scalar.activation(warm_out[:], warm_in[:], SILU)
 
         offs_t = keep.tile([P, S // GROUP], U16, name="offs_t")
         src_t = keep.tile([P, S // GROUP], U16, name="src_t")
@@ -76,11 +76,11 @@ def tile_picked_hub_silu_e_kernel(tc, xT, w1, w2, w3_words, w3_scales, offs, src
             if hi < H:
                 w1_raw.append(keep.tile([P, PACK, hi - lo], F32, name=f"w1_raw{a}", align_bytes=64))
             else:
-                w1_raw.append(placed.tile([P, PACK, hi - lo], F32, name=f"w1_raw{a}", offset=AT_W1_LAST, align_bytes=64))
+                w1_raw.append(placed.tile([P, PACK, hi - lo], F32, name=f"w1_raw{a}", offset=0, align_bytes=64))
             nc.sync.dma_start(out=w1_raw[a][:], in_=w1.rearrange("(p j) c -> p j c", j=PACK)[:, :, lo:hi])
-        nc.sync.dma_start(src_t[:], src)
         w2_raw = keep.tile([P, PACK, H], F32, name="w2_raw")
         nc.sync.dma_start(out=w2_raw[:], in_=w2.rearrange("(p j) c -> p j c", j=PACK))
+        nc.sync.dma_start(src_t[:], src)
         nc.sync.dma_start(dst_t[:], dst)
         nc.sync.dma_start(out=w3_codes[:].bitcast(I32), in_=w3_words[0].bitcast(I32))
         for q in range(4):
@@ -91,19 +91,10 @@ def tile_picked_hub_silu_e_kernel(tc, xT, w1, w2, w3_words, w3_scales, offs, src
 
         row_rounded = [keep.tile([P, T], BF16, name=f"row_rounded{j}", align_bytes=64) for j in range(PACK)]
         pieces = S // PIECE
-        picked = placed.tile([P, S, PACK], BF16, name="picked", offset=AT_PICKED, align_bytes=64)
-        x_codes = {}
-        x_bytes = {}
+        picked = keep.tile([P, S, PACK], BF16, name="picked", align_bytes=64)
 
         def gpsimd_round(out, in_):
             nc.gpsimd.tensor_scalar(out, in_, 1.0, 0.0, MULT, ADD)
-
-        def quantize_nodes(i):
-            nc.vector.quantize_mx(
-                out=x_codes[i][:].bitcast(FP8X4),
-                scales=x_bytes[i][:],
-                in_=picked[:, i * PIECE : (i + 1) * PIECE, :].rearrange("p c j -> p (c j)"),
-            )
 
         rounders = (
             (nc.scalar.copy, nc.vector.tensor_copy),
@@ -121,30 +112,50 @@ def tile_picked_hub_silu_e_kernel(tc, xT, w1, w2, w3_words, w3_scales, offs, src
             for lo, hi in zip(gather_cuts, gather_cuts[1:]):
                 nc.scalar.activation(picked[:, lo:hi, j], row_rounded[j][:].indirect(entries(offs_t, lo, hi - lo)), COPY)
 
-        w1_codes0 = keep.tile([P, P], U32, name="w1_codes0", align_bytes=64)
-        w1_codes1 = placed.tile([P, P], U32, name="w1_codes1", offset=AT_PICKED, align_bytes=64)
-        w1_codes23 = placed.tile([P, 2 * P], U32, name="w1_codes23", offset=AT_PICKED + 4096, align_bytes=64)
-        w1_bytes01 = keep.tile([P, 2 * P], U8, name="w1_bytes01", align_bytes=64)
-        w1_bytes23 = keep.tile([P, 2 * P], U8, name="w1_bytes23", align_bytes=64)
-        w2_codes = placed.tile([P, H], U32, name="w2_codes", offset=AT_W2_CODES, align_bytes=64)
-        w2_bytes = keep.tile([P, H], U8, name="w2_bytes", align_bytes=64)
-        w_codes = {(0, 0): w1_codes0[:], (0, 1): w1_codes1[:], (0, 2): w1_codes23[:, 0:P], (0, 3): w1_codes23[:, P : 2 * P]}
+        def quantize(codes, scale_bytes, values):
+            nc.vector.quantize_mx(out=codes.bitcast(FP8X4), scales=scale_bytes, in_=values)
+
+        x_codes = [keep.tile([P, PIECE], U32, name=f"x_codes{i}", align_bytes=64) for i in range(pieces)]
+        x_bytes = [keep.tile([P, PIECE], U8, name="x_bytes0", align_bytes=64)]
+
+        def quantize_nodes(i):
+            quantize(x_codes[i][:], x_bytes[i][:], picked[:, i * PIECE : (i + 1) * PIECE, :].rearrange("p c j -> p (c j)"))
+
+        quantize_nodes(0)
+
+        w_rounded = [keep.tile([P, PACK, P, PACK], BF16, name=f"w_rounded{w}", align_bytes=64) for w in range(2)]
+        w_codes = {}
         w_bytes = {}
-        for t in range(PACK):
-            w_bytes[0, t] = (w1_bytes01 if t < 2 else w1_bytes23)[:, (t % 2) * P : (t % 2 + 1) * P]
-            w_codes[1, t] = w2_codes[:, t * P : (t + 1) * P]
-            w_bytes[1, t] = w2_bytes[:, t * P : (t + 1) * P]
 
-        planes = {}
-        for w in range(2):
-            for t in range(PACK):
-                width = SOURCE_WINDOW if w == 0 else (S + GROUP if t == 0 else S)
-                planes[w, t] = keep.tile([P, width], F32, name=f"plane{w}_{t}", align_bytes=64)
-                if width > S:
-                    nc.gpsimd.memset(planes[w, t][:, S:width], 0.0)
+        def quantize_planes(w, t0, t1):
+            codes = keep.tile([P, (t1 - t0) * P], U32, name=f"w_codes{w}_{t0}", align_bytes=64)
+            scale_bytes = keep.tile([P, (t1 - t0) * P], U8, name=f"w_bytes{w}_{t0}", align_bytes=64)
+            quantize(codes[:], scale_bytes[:], w_rounded[w][:, t0:t1].rearrange("p t m j -> p (t m j)"))
+            for t in range(t0, t1):
+                w_codes[w, t] = codes[:, (t - t0) * P : (t - t0 + 1) * P]
+                w_bytes[w, t] = scale_bytes[:, (t - t0) * P : (t - t0 + 1) * P]
 
-        def first_product(w, t, first, count, bank, copy=nc.scalar.copy):
-            acc = psum.tile([P, count * PIECE], F32, name="acc", tag=f"bank{bank}")
+        for a, (lo, hi) in enumerate(w1_parts):
+            for t0, t1 in ((0, PACK),) if hi < H else ((0, 2), (2, PACK)):
+                nc.vector.tensor_copy(
+                    out=w_rounded[0][:, t0:t1, lo // PACK : hi // PACK, :].rearrange("p t m j -> p m j t"),
+                    in_=w1_raw[a][:].rearrange("p j (m t) -> p m j t", t=PACK)[:, :, :, t0:t1],
+                )
+        quantize_planes(0, 0, 1)
+        for i in range(1, pieces):
+            x_bytes.append(placed.tile([P, PIECE], U8, name=f"x_bytes{i}", offset=PIECE * i, align_bytes=64))
+            quantize_nodes(i)
+        quantize_planes(0, 1, PACK)
+
+        planes = {(w, t): keep.tile([P, S], F32, name=f"plane{w}_{t}", align_bytes=64) for w in range(2) for t in range(PACK)}
+        products = []
+
+        def next_bank(width):
+            products.append(width)
+            return psum.tile([P, width], F32, name="acc", tag=f"bank{(len(products) - 1) % BANKS}")
+
+        def first_product(w, t, first, count, copy=nc.scalar.copy):
+            acc = next_bank(count * PIECE)
             for i in range(count):
                 nc.tensor.matmul_mx(
                     out=acc[:, i * PIECE : (i + 1) * PIECE],
@@ -157,102 +168,65 @@ def tile_picked_hub_silu_e_kernel(tc, xT, w1, w2, w3_words, w3_scales, offs, src
                 )
             copy(out=planes[w, t][:, first * PIECE : (first + count) * PIECE], in_=acc[:])
 
-        def whole_product(w, t, banks):
-            for half, bank in enumerate(banks):
-                first_product(w, t, 2 * half, 2, bank)
-
-        x_codes[0] = keep.tile([P, PIECE], U32, name="x_codes0", align_bytes=64)
-        x_bytes[0] = keep.tile([P, PIECE], U8, name="x_bytes0", align_bytes=64)
-        quantize_nodes(0)
-        w1_rounded = keep.tile([P, PACK, P, PACK], BF16, name="w1_rounded", align_bytes=64)
-        for a, (lo, hi) in enumerate(w1_parts):
-            for t0, t1 in ((0, PACK),) if hi < H else ((0, 2), (2, PACK)):
-                nc.vector.tensor_copy(
-                    out=w1_rounded[:, t0:t1, lo // PACK : hi // PACK, :].rearrange("p t m j -> p m j t"),
-                    in_=w1_raw[a][:].rearrange("p j (m t) -> p m j t", t=PACK)[:, :, :, t0:t1],
-                )
-
-        def quantize_w1_plane(t):
-            nc.vector.quantize_mx(
-                out=w_codes[0, t].bitcast(FP8X4), scales=w_bytes[0, t], in_=w1_rounded[:, t].rearrange("p m j -> p (m j)")
-            )
-
-        quantize_w1_plane(0)
-        for i in range(1, pieces):
-            x_codes[i] = placed.tile([P, PIECE], U32, name=f"x_codes{i}", offset=AT_NODE_CODES + 4096 * i, align_bytes=64)
-            x_bytes[i] = placed.tile([P, PIECE], U8, name=f"x_bytes{i}", offset=AT_W1_LAST + PIECE * i, align_bytes=64)
-            quantize_nodes(i)
-        quantize_w1_plane(1)
         for i in range(pieces):
-            first_product(0, 0, i, 1, i, nc.vector.tensor_copy if i == 0 else nc.scalar.copy)
-        nc.vector.quantize_mx(
-            out=w1_codes23[:].bitcast(FP8X4), scales=w1_bytes23[:], in_=w1_rounded[:, 2:PACK].rearrange("p t m j -> p (t m j)")
+            first_product(0, 0, i, 1, nc.vector.tensor_copy if i == 0 else nc.scalar.copy)
+        for t in range(1, PACK):
+            for half in range(2):
+                first_product(0, t, 2 * half, 2)
+
+        sources = [keep.tile([P, S], F32, name=f"source{t}", align_bytes=64) for t in range(PACK)]
+
+        def vector_fetch(t, half):
+            r0 = half * HALF
+            nc.vector.tensor_copy(sources[t][:, r0 : r0 + HALF], planes[0, t][:].indirect(entries(src_t, r0, HALF)))
+
+        nc.vector.tensor_copy(
+            out=w_rounded[1][:].rearrange("p t m j -> p m j t"), in_=w2_raw[:].rearrange("p j (m t) -> p m j t", t=PACK)
         )
-        whole_product(0, 1, (0, 1))
-        w2_rounded = placed.tile([P, PACK, P, PACK], BF16, name="w2_rounded", offset=AT_PICKED, align_bytes=64)
-        nc.scalar.copy(out=w2_rounded[:].rearrange("p t m j -> p m j t"), in_=w2_raw[:].rearrange("p j (m t) -> p m j t", t=PACK))
-        whole_product(0, 2, (4, 1))
+        vector_fetch(0, 0)
+        quantize_planes(1, 0, PACK)
+        vector_fetch(0, 1)
+        for half in range(2):
+            vector_fetch(1, half)
+        for t in range(PACK):
+            for half in range(2):
+                first_product(1, t, 2 * half, 2)
+        for r0, n in EDGE_RANGES:
+            for t in range(2, PACK):
+                nc.scalar.activation(sources[t][:, r0 : r0 + n], planes[0, t][:].indirect(entries(src_t, r0, n)), COPY)
+
+        sums = [keep.tile([P, PACK, n], F32, name=f"sums{c}", align_bytes=64) for c, (r0, n) in enumerate(EDGE_RANGES)]
+
+        def add_targets(t, c):
+            r0, n = EDGE_RANGES[c]
+            nc.vector.tensor_tensor(sums[c][:, t, :], planes[1, t][:].indirect(entries(dst_t, r0, n)), sources[t][:, r0 : r0 + n], ADD)
+
+        for t in range(2):
+            for c in range(len(EDGE_RANGES)):
+                add_targets(t, c)
+        for c in range(len(EDGE_RANGES)):
+            for t in range(2, PACK):
+                add_targets(t, c)
 
         z = [keep.tile([P, n, PACK], BF16, name=f"z{c}", align_bytes=64) for c, (r0, n) in enumerate(EDGE_RANGES)]
-        z_codes = keep.tile([P, S], U32, name="z_codes", align_bytes=64)
-        z_bytes = keep.tile([P, S], U8, name="z_bytes", align_bytes=64)
-
-        def fetch_sources(t):
-            fetched = keep.tile([P, S], F32, name=f"source{t}", align_bytes=64)
-            nc.vector.tensor_copy(fetched[:], planes[0, t][:].indirect(src_t[:]))
-            return fetched
-
-        def second_product(c, copy):
-            r0, n = EDGE_RANGES[c]
-            for s0, width in powers_of_two(n):
-                cols = slice(r0 + s0, r0 + s0 + width)
-                nc.vector.quantize_mx(
-                    out=z_codes[:, cols].bitcast(FP8X4),
-                    scales=z_bytes[:, cols],
-                    in_=z[c][:, s0 : s0 + width, :].rearrange("p r t -> p (r t)"),
-                )
-            result = keep.tile([P, n], F32, name=f"result{c}")
-            acc_out = psum.tile([P, n], F32, name="acc_out", tag=f"bank{c}")
-            for s0, width in powers_of_two(n):
-                cols = slice(r0 + s0, r0 + s0 + width)
+        for c in range(len(EDGE_RANGES)):
+            nc.scalar.activation(z[c][:].rearrange("p (r i) t -> p r t i", i=2), sums[c][:].rearrange("p t (r i) -> p r t i", i=2), SILU)
+        for c, (r0, n) in enumerate(EDGE_RANGES):
+            z_codes = keep.tile([P, n], U32, name=f"z_codes{c}", align_bytes=64)
+            z_bytes = keep.tile([P, n], U8, name=f"z_bytes{c}", align_bytes=64)
+            quantize(z_codes[:], z_bytes[:], z[c][:].rearrange("p r t -> p (r t)"))
+            acc = next_bank(n)
+            for s0, width in pass_widths(n):
                 nc.tensor.matmul_mx(
-                    out=acc_out[:, s0 : s0 + width],
+                    out=acc[:, s0 : s0 + width],
                     lhsT=w3_codes[:].bitcast(FP4X4),
                     lhsT_scale=w3_bytes[:],
-                    rhs=z_codes[:, cols].bitcast(FP8X4),
-                    rhs_scale=z_bytes[:, cols],
+                    rhs=z_codes[:, s0 : s0 + width].bitcast(FP8X4),
+                    rhs_scale=z_bytes[:, s0 : s0 + width],
                     start=True,
                     stop=True,
                 )
-            copy(out=result[:], in_=acc_out[:])
+            result = keep.tile([P, n], F32, name=f"result{c}")
+            copy = nc.vector.tensor_copy if c == len(EDGE_RANGES) - 1 else nc.scalar.copy
+            copy(out=result[:], in_=acc[:])
             nc.sync.dma_start(out=out[:, r0 : r0 + n], in_=result[:])
-
-        sources = [fetch_sources(0), fetch_sources(1)]
-        nc.vector.quantize_mx(
-            out=w2_codes[:].bitcast(FP8X4), scales=w2_bytes[:], in_=w2_rounded[:].rearrange("p t m j -> p (t m j)")
-        )
-        whole_product(1, 0, (2, 3))
-        sources.append(fetch_sources(2))
-        whole_product(0, 3, (0, 5))
-        whole_product(1, 1, (2, 3))
-        whole_product(1, 2, (4, 5))
-        whole_product(1, 3, (4, 5))
-
-        sums0 = keep.tile([P, S], F32, name="sums0", align_bytes=64)
-        nc.vector.tensor_tensor(sums0[:], planes[1, 0][:].indirect(dst_t[:]), sources[0][:], ADD)
-        for c, (r0, n) in enumerate(EDGE_RANGES):
-            nc.scalar.activation(z[c][:, :, 0], sums0[:, r0 : r0 + n], SILU)
-        sources.append(fetch_sources(3))
-
-        for c, (r0, n) in enumerate(EDGE_RANGES):
-            if c == 2:
-                second_product(0, nc.scalar.copy)
-            sums = placed.tile([P, PACK - 1, n], F32, name=f"sums_range{c}", offset=AT_SUMS[c], align_bytes=64)
-            for t in range(1, PACK):
-                nc.vector.tensor_tensor(sums[:, t - 1, :], planes[1, t][:].indirect(entries(dst_t, r0, n)), sources[t][:, r0 : r0 + n], ADD)
-            nc.scalar.activation(
-                z[c][:, :, 1:PACK].rearrange("p (r i) t -> p r t i", i=2), sums[:].rearrange("p t (r i) -> p r t i", i=2), SILU
-            )
-        second_product(1, nc.scalar.copy)
-        for c in range(2, len(EDGE_RANGES)):
-            second_product(c, nc.vector.tensor_copy)

@@ -210,7 +210,7 @@ def tile_picked_hub_silu_e_kernel(tc, xT, w1, w2, w3_words, w3_scales, offs, src
 
         z = [keep.tile([P, n, PACK], BF16, name=f"z{c}", align_bytes=64) for c, (r0, n) in enumerate(EDGE_RANGES)]
         for c in range(len(EDGE_RANGES)):
-            nc.scalar.activation(z[c][:].rearrange("p (r i) t -> p r t i", i=2), sums[c][:].rearrange("p t (r i) -> p r t i", i=2), SILU)
+            nc.scalar.activation(z[c][:].rearrange("p (r i) t -> p r t i", i=4), sums[c][:].rearrange("p t (r i) -> p r t i", i=4), SILU)
         for c, (r0, n) in enumerate(EDGE_RANGES):
             z_codes = keep.tile([P, n], U32, name=f"z_codes{c}", align_bytes=64)
             z_bytes = keep.tile([P, n], U8, name=f"z_bytes{c}", align_bytes=64)

@@ -24,7 +24,7 @@ FLOPS = 2 * K * H * S * 2 + 2 * H * N * S
 
 LOAD_CUTS = ((0, T), (0, T // 2, T), (0, T // 2, T), (0, 896, 1664, T))
 VECTOR_NODES = (416, 416, 352, 256)
-W1_CUTS = (0, 192, 384, H)
+W1_CUTS = (0, 256, 384, H)
 PIECE = 256
 HALF = S // 2
 EDGE_RANGES = ((0, 384), (384, 256), (640, 256), (896, 128))

@@ -28,6 +28,10 @@ W1_CUTS = (0, 256, 384, H)
 PIECE = 256
 HALF = S // 2
 EDGE_RANGES = ((0, 384), (384, 256), (640, 256), (896, 128))
+AT_W2_ROUNDED = 2048
+AT_W2 = 12288
+AT_SUMS = (AT_W2 + 64 - 6144, AT_W2 + 64, AT_W2 + 64 + 6144, AT_W2 + 64 + 4096)
+AT_RANGE = (28672, 32768, 36864, 40960)
 
 
 def pass_widths(n):
@@ -78,7 +82,7 @@ def tile_picked_hub_silu_e_kernel(tc, xT, w1, w2, w3_words, w3_scales, offs, src
             else:
                 w1_raw.append(placed.tile([P, PACK, hi - lo], F32, name=f"w1_raw{a}", offset=0, align_bytes=64))
             nc.sync.dma_start(out=w1_raw[a][:], in_=w1.rearrange("(p j) c -> p j c", j=PACK)[:, :, lo:hi])
-        w2_raw = keep.tile([P, PACK, H], F32, name="w2_raw")
+        w2_raw = placed.tile([P, PACK, H], F32, name="w2_raw", offset=AT_W2, align_bytes=64)
         nc.sync.dma_start(out=w2_raw[:], in_=w2.rearrange("(p j) c -> p j c", j=PACK))
         nc.sync.dma_start(src_t[:], src)
         nc.sync.dma_start(dst_t[:], dst)
@@ -115,7 +119,9 @@ def tile_picked_hub_silu_e_kernel(tc, xT, w1, w2, w3_words, w3_scales, offs, src
         def quantize(codes, scale_bytes, values):
             nc.vector.quantize_mx(out=codes.bitcast(FP8X4), scales=scale_bytes, in_=values)
 
-        x_codes = [keep.tile([P, PIECE], U32, name=f"x_codes{i}", align_bytes=64) for i in range(pieces)]
+        x_codes = [keep.tile([P, PIECE], U32, name="x_codes0", align_bytes=64)]
+        for i in range(1, pieces):
+            x_codes.append(placed.tile([P, PIECE], U32, name=f"x_codes{i}", offset=AT_RANGE[i], align_bytes=64))
         x_bytes = [keep.tile([P, PIECE], U8, name="x_bytes0", align_bytes=64)]
 
         def quantize_nodes(i):
@@ -123,14 +129,14 @@ def tile_picked_hub_silu_e_kernel(tc, xT, w1, w2, w3_words, w3_scales, offs, src
 
         quantize_nodes(0)
 
-        w_rounded = [keep.tile([P, PACK, P, PACK], BF16, name=f"w_rounded{w}", align_bytes=64) for w in range(2)]
+        w1_rounded = keep.tile([P, PACK, P, PACK], BF16, name="w1_rounded", align_bytes=64)
         w_codes = {}
         w_bytes = {}
 
-        def quantize_planes(w, t0, t1):
+        def quantize_planes(w, t0, t1, rounded):
             codes = keep.tile([P, (t1 - t0) * P], U32, name=f"w_codes{w}_{t0}", align_bytes=64)
             scale_bytes = keep.tile([P, (t1 - t0) * P], U8, name=f"w_bytes{w}_{t0}", align_bytes=64)
-            quantize(codes[:], scale_bytes[:], w_rounded[w][:, t0:t1].rearrange("p t m j -> p (t m j)"))
+            quantize(codes[:], scale_bytes[:], rounded.rearrange("p t m j -> p (t m j)"))
             for t in range(t0, t1):
                 w_codes[w, t] = codes[:, (t - t0) * P : (t - t0 + 1) * P]
                 w_bytes[w, t] = scale_bytes[:, (t - t0) * P : (t - t0 + 1) * P]
@@ -138,14 +144,14 @@ def tile_picked_hub_silu_e_kernel(tc, xT, w1, w2, w3_words, w3_scales, offs, src
         for a, (lo, hi) in enumerate(w1_parts):
             for t0, t1 in ((0, PACK),) if hi < H else ((0, 2), (2, PACK)):
                 nc.vector.tensor_copy(
-                    out=w_rounded[0][:, t0:t1, lo // PACK : hi // PACK, :].rearrange("p t m j -> p m j t"),
+                    out=w1_rounded[:, t0:t1, lo // PACK : hi // PACK, :].rearrange("p t m j -> p m j t"),
                     in_=w1_raw[a][:].rearrange("p j (m t) -> p m j t", t=PACK)[:, :, :, t0:t1],
                 )
-        quantize_planes(0, 0, 1)
+        quantize_planes(0, 0, 1, w1_rounded[:, 0:1])
         for i in range(1, pieces):
             x_bytes.append(placed.tile([P, PIECE], U8, name=f"x_bytes{i}", offset=PIECE * i, align_bytes=64))
             quantize_nodes(i)
-        quantize_planes(0, 1, PACK)
+        quantize_planes(0, 1, PACK, w1_rounded[:, 1:PACK])
 
         planes = {(w, t): keep.tile([P, S], F32, name=f"plane{w}_{t}", align_bytes=64) for w in range(2) for t in range(PACK)}
         products = []
@@ -174,32 +180,50 @@ def tile_picked_hub_silu_e_kernel(tc, xT, w1, w2, w3_words, w3_scales, offs, src
             for half in range(2):
                 first_product(0, t, 2 * half, 2)
 
-        sources = [keep.tile([P, S], F32, name=f"source{t}", align_bytes=64) for t in range(PACK)]
+        whole_sources = [keep.tile([P, S], F32, name=f"source{t}", align_bytes=64) for t in range(2)]
+        sources = {(t, c): whole_sources[t][:, r0 : r0 + n] for t in range(2) for c, (r0, n) in enumerate(EDGE_RANGES)}
 
         def vector_fetch(t, half):
             r0 = half * HALF
-            nc.vector.tensor_copy(sources[t][:, r0 : r0 + HALF], planes[0, t][:].indirect(entries(src_t, r0, HALF)))
+            nc.vector.tensor_copy(whole_sources[t][:, r0 : r0 + HALF], planes[0, t][:].indirect(entries(src_t, r0, HALF)))
 
+        w2_early = placed.tile([P, 2, P, PACK], BF16, name="w2_early", offset=AT_W2_ROUNDED, align_bytes=64)
         nc.vector.tensor_copy(
-            out=w_rounded[1][:].rearrange("p t m j -> p m j t"), in_=w2_raw[:].rearrange("p j (m t) -> p m j t", t=PACK)
+            out=w2_early[:].rearrange("p t m j -> p m j t"), in_=w2_raw[:].rearrange("p j (m t) -> p m j t", t=PACK)[:, :, :, 0:2]
         )
         vector_fetch(0, 0)
-        quantize_planes(1, 0, PACK)
+        quantize_planes(1, 0, 2, w2_early[:])
+        w2_late = placed.tile([P, 2, P, PACK], BF16, name="w2_late", offset=AT_W2_ROUNDED, align_bytes=64)
+        gpsimd_round(out=w2_late[:], in_=w2_raw[:].rearrange("p j (m t) -> p t m j", t=PACK)[:, 2:PACK])
         vector_fetch(0, 1)
         for half in range(2):
             vector_fetch(1, half)
-        for t in range(PACK):
-            for half in range(2):
-                first_product(1, t, 2 * half, 2)
-        for r0, n in EDGE_RANGES:
-            for t in range(2, PACK):
-                nc.scalar.activation(sources[t][:, r0 : r0 + n], planes[0, t][:].indirect(entries(src_t, r0, n)), COPY)
+        quantize_planes(1, 2, PACK, w2_late[:])
 
-        sums = [keep.tile([P, PACK, n], F32, name=f"sums{c}", align_bytes=64) for c, (r0, n) in enumerate(EDGE_RANGES)]
+        def scalar_fetch(c):
+            r0, n = EDGE_RANGES[c]
+            for t in range(2, PACK):
+                at = AT_RANGE[c] + 512 - (4 * n if t == 2 else 0)
+                sources[t, c] = placed.tile([P, n], F32, name=f"source{t}_{c}", offset=at, align_bytes=64)[:]
+                nc.scalar.activation(sources[t, c], planes[0, t][:].indirect(entries(src_t, r0, n)), COPY)
+
+        for t in range(PACK):
+            if t == 2:
+                scalar_fetch(0)
+            first_product(1, t, 0, 2)
+            if t == 1:
+                first_product(1, t, 2, 1)
+                first_product(1, t, 3, 1, nc.vector.tensor_copy)
+            else:
+                first_product(1, t, 2, 2)
+        for c in range(1, len(EDGE_RANGES)):
+            scalar_fetch(c)
+
+        sums = [placed.tile([P, PACK, n], F32, name=f"sums{c}", offset=AT_SUMS[c], align_bytes=64) for c, (r0, n) in enumerate(EDGE_RANGES)]
 
         def add_targets(t, c):
             r0, n = EDGE_RANGES[c]
-            nc.vector.tensor_tensor(sums[c][:, t, :], planes[1, t][:].indirect(entries(dst_t, r0, n)), sources[t][:, r0 : r0 + n], ADD)
+            nc.vector.tensor_tensor(sums[c][:, t, :], planes[1, t][:].indirect(entries(dst_t, r0, n)), sources[t, c], ADD)
 
         for t in range(2):
             for c in range(len(EDGE_RANGES)):

@@ -27,6 +27,7 @@ VECTOR_NODES = (416, 416, 352, 256)
 W1_CUTS = (0, 256, 384, H)
 PIECE = 256
 HALF = S // 2
+VECTOR_TARGETS = 128
 EDGE_RANGES = ((0, 384), (384, 256), (640, 256), (896, 128))
 AT_W2_ROUNDED = 2048
 AT_W2 = 12288
@@ -151,7 +152,8 @@ def tile_picked_hub_silu_e_kernel(tc, xT, w1, w2, w3_words, w3_scales, offs, src
         for i in range(1, pieces):
             x_bytes.append(placed.tile([P, PIECE], U8, name=f"x_bytes{i}", offset=PIECE * i, align_bytes=64))
             quantize_nodes(i)
-        quantize_planes(0, 1, PACK, w1_rounded[:, 1:PACK])
+        quantize_planes(0, 1, 2, w1_rounded[:, 1:2])
+        quantize_planes(0, 2, PACK, w1_rounded[:, 2:PACK])
 
         planes = {(w, t): keep.tile([P, S], F32, name=f"plane{w}_{t}", align_bytes=64) for w in range(2) for t in range(PACK)}
         products = []
@@ -160,25 +162,26 @@ def tile_picked_hub_silu_e_kernel(tc, xT, w1, w2, w3_words, w3_scales, offs, src
             products.append(width)
             return psum.tile([P, width], F32, name="acc", tag=f"bank{(len(products) - 1) % BANKS}")
 
-        def first_product(w, t, first, count, copy=nc.scalar.copy):
-            acc = next_bank(count * PIECE)
-            for i in range(count):
+        def first_product(w, t, lo, hi, copy=nc.scalar.copy):
+            acc = next_bank(hi - lo)
+            for i in range(lo // PIECE, (hi - 1) // PIECE + 1):
+                a, b = max(lo, i * PIECE), min(hi, (i + 1) * PIECE)
                 nc.tensor.matmul_mx(
-                    out=acc[:, i * PIECE : (i + 1) * PIECE],
+                    out=acc[:, a - lo : b - lo],
                     lhsT=w_codes[w, t].bitcast(FP8X4),
                     lhsT_scale=w_bytes[w, t],
-                    rhs=x_codes[first + i][:].bitcast(FP8X4),
-                    rhs_scale=x_bytes[first + i][:],
+                    rhs=x_codes[i][:, a - i * PIECE : b - i * PIECE].bitcast(FP8X4),
+                    rhs_scale=x_bytes[i][:, a - i * PIECE : b - i * PIECE],
                     start=True,
                     stop=True,
                 )
-            copy(out=planes[w, t][:, first * PIECE : (first + count) * PIECE], in_=acc[:])
+            copy(out=planes[w, t][:, lo:hi], in_=acc[:])
 
         for i in range(pieces):
-            first_product(0, 0, i, 1, nc.vector.tensor_copy if i == 0 else nc.scalar.copy)
+            first_product(0, 0, i * PIECE, (i + 1) * PIECE, nc.vector.tensor_copy if i == 0 else nc.scalar.copy)
         for t in range(1, PACK):
             for half in range(2):
-                first_product(0, t, 2 * half, 2)
+                first_product(0, t, half * HALF, (half + 1) * HALF)
 
         whole_sources = [keep.tile([P, S], F32, name=f"source{t}", align_bytes=64) for t in range(2)]
         sources = {(t, c): whole_sources[t][:, r0 : r0 + n] for t in range(2) for c, (r0, n) in enumerate(EDGE_RANGES)}
@@ -210,12 +213,12 @@ def tile_picked_hub_silu_e_kernel(tc, xT, w1, w2, w3_words, w3_scales, offs, src
         for t in range(PACK):
             if t == 2:
                 scalar_fetch(0)
-            first_product(1, t, 0, 2)
+            first_product(1, t, 0, HALF)
             if t == 1:
-                first_product(1, t, 2, 1)
-                first_product(1, t, 3, 1, nc.vector.tensor_copy)
+                first_product(1, t, HALF, S - VECTOR_TARGETS)
+                first_product(1, t, S - VECTOR_TARGETS, S, nc.vector.tensor_copy)
             else:
-                first_product(1, t, 2, 2)
+                first_product(1, t, HALF, S)
         for c in range(1, len(EDGE_RANGES)):
             scalar_fetch(c)
 

@@ -23,7 +23,8 @@ BANKS = 8
 FLOPS = 2 * K * H * S * 2 + 2 * H * N * S
 
 LOAD_CUTS = ((0, T), (0, T // 2, T), (0, T // 2, T), (0, 896, 1664, T))
-VECTOR_NODES = (416, 416, 352, 256)
+VECTOR_NODES = (352, 352, 384, 256)
+ROW0_SCALAR = 704
 W1_CUTS = (0, 256, 384, H)
 PIECE = 256
 HALF = S // 2
@@ -108,7 +109,7 @@ def tile_picked_hub_silu_e_kernel(tc, xT, w1, w2, w3_words, w3_scales, offs, src
             (gpsimd_round, nc.vector.tensor_copy, gpsimd_round),
         )
         for j in range(PACK):
-            round_cuts = LOAD_CUTS[max(j, 1)]
+            round_cuts = LOAD_CUTS[j] if j > 0 else (0, ROW0_SCALAR, T)
             for lo, hi, copy in zip(round_cuts, round_cuts[1:], rounders[j]):
                 copy(out=row_rounded[j][:, lo:hi], in_=row_raw[j][:, lo:hi])
             n = VECTOR_NODES[j]

@@ -32,7 +32,7 @@ VECTOR_TARGETS = 128
 EDGE_RANGES = ((0, 384), (384, 256), (640, 256), (896, 128))
 AT_W2_ROUNDED = 2048
 AT_W2 = 12288
-AT_SUMS = (AT_W2 + 64 - 6144, AT_W2 + 64, AT_W2 + 64 + 6144, AT_W2 + 64 + 4096)
+AT_SUMS = (AT_W2 + 64 - 6144, AT_W2 + 64)
 AT_RANGE = (28672, 32768, 36864, 40960)
 
 
@@ -185,7 +185,7 @@ def tile_picked_hub_silu_e_kernel(tc, xT, w1, w2, w3_words, w3_scales, offs, src
                 first_product(0, t, half * HALF, (half + 1) * HALF)
 
         whole_sources = [keep.tile([P, S], F32, name=f"source{t}", align_bytes=64) for t in range(2)]
-        sources = {(t, c): whole_sources[t][:, r0 : r0 + n] for t in range(2) for c, (r0, n) in enumerate(EDGE_RANGES)}
+        sources = {}
 
         def vector_fetch(t, half):
             r0 = half * HALF
@@ -204,41 +204,47 @@ def tile_picked_hub_silu_e_kernel(tc, xT, w1, w2, w3_words, w3_scales, offs, src
             vector_fetch(1, half)
         quantize_planes(1, 2, PACK, w2_late[:])
 
-        def scalar_fetch(c):
-            r0, n = EDGE_RANGES[c]
+        def scalar_fetch(c0, c1):
+            r0 = EDGE_RANGES[c0][0]
+            n = sum(EDGE_RANGES[c1 - 1]) - r0
             for t in range(2, PACK):
-                at = AT_RANGE[c] + 512 - (4 * n if t == 2 else 0)
-                sources[t, c] = placed.tile([P, n], F32, name=f"source{t}_{c}", offset=at, align_bytes=64)[:]
-                nc.scalar.activation(sources[t, c], planes[0, t][:].indirect(entries(src_t, r0, n)), COPY)
+                at = AT_RANGE[c0 + min(c0, 1)] + 512 - (4 * n if t == 2 else 0)
+                fetched = placed.tile([P, n], F32, name=f"source{t}_{c0}", offset=at, align_bytes=64)
+                nc.scalar.activation(fetched[:], planes[0, t][:].indirect(entries(src_t, r0, n)), COPY)
+                for c in range(c0, c1):
+                    sources[t, c] = fetched[:, EDGE_RANGES[c][0] - r0 : sum(EDGE_RANGES[c]) - r0]
 
         for t in range(PACK):
             if t == 2:
-                scalar_fetch(0)
+                scalar_fetch(0, 1)
             first_product(1, t, 0, HALF)
             if t == 1:
                 first_product(1, t, HALF, S - VECTOR_TARGETS)
                 first_product(1, t, S - VECTOR_TARGETS, S, nc.vector.tensor_copy)
             else:
                 first_product(1, t, HALF, S)
-        for c in range(1, len(EDGE_RANGES)):
-            scalar_fetch(c)
+        scalar_fetch(1, 2)
+        scalar_fetch(2, len(EDGE_RANGES))
 
-        sums = [placed.tile([P, PACK, n], F32, name=f"sums{c}", offset=AT_SUMS[c], align_bytes=64) for c, (r0, n) in enumerate(EDGE_RANGES)]
+        first = EDGE_RANGES[0][1]
+        sum_tiles = [placed.tile([P, PACK, n], F32, name=f"sums{a}", offset=AT_SUMS[a], align_bytes=64) for a, n in enumerate((first, S - first))]
 
-        def add_targets(t, c):
-            r0, n = EDGE_RANGES[c]
-            nc.vector.tensor_tensor(sums[c][:, t, :], planes[1, t][:].indirect(entries(dst_t, r0, n)), sources[t, c], ADD)
+        def sums(r0, n):
+            return sum_tiles[0][:, :, r0 : r0 + n] if r0 < first else sum_tiles[1][:, :, r0 - first : r0 - first + n]
+
+        def add_targets(t, r0, n, source):
+            nc.vector.tensor_tensor(sums(r0, n)[:, t, :], planes[1, t][:].indirect(entries(dst_t, r0, n)), source, ADD)
 
         for t in range(2):
-            for c in range(len(EDGE_RANGES)):
-                add_targets(t, c)
-        for c in range(len(EDGE_RANGES)):
+            for r0, n in ((0, first), (first, S - first)):
+                add_targets(t, r0, n, whole_sources[t][:, r0 : r0 + n])
+        for c, (r0, n) in enumerate(EDGE_RANGES):
             for t in range(2, PACK):
-                add_targets(t, c)
+                add_targets(t, r0, n, sources[t, c])
 
         z = [keep.tile([P, n, PACK], BF16, name=f"z{c}", align_bytes=64) for c, (r0, n) in enumerate(EDGE_RANGES)]
-        for c in range(len(EDGE_RANGES)):
-            nc.scalar.activation(z[c][:].rearrange("p (r i) t -> p r t i", i=4), sums[c][:].rearrange("p t (r i) -> p r t i", i=4), SILU)
+        for c, (r0, n) in enumerate(EDGE_RANGES):
+            nc.scalar.activation(z[c][:].rearrange("p (r i) t -> p r t i", i=4), sums(r0, n).rearrange("p t (r i) -> p r t i", i=4), SILU)
         for c, (r0, n) in enumerate(EDGE_RANGES):
             z_codes = keep.tile([P, n], U32, name=f"z_codes{c}", align_bytes=64)
             z_bytes = keep.tile([P, n], U8, name=f"z_bytes{c}", align_bytes=64)

@@ -28,12 +28,13 @@ ROW0_SCALAR = 704
 W1_CUTS = (0, 256, 384, H)
 PIECE = 256
 HALF = S // 2
-VECTOR_TARGETS = 128
+VECTOR_TARGETS = 384
 EDGE_RANGES = ((0, 384), (384, 256), (640, 256), (896, 128))
 AT_W2_ROUNDED = 2048
 AT_W2 = 12288
-AT_SUMS = (AT_W2 + 64 - 6144, AT_W2 + 64)
+AT_SUMS = (AT_W2 + 64 - 6144, AT_W2 + 64, AT_W2 + 64 - 6144)
 AT_RANGE = (28672, 32768, 36864, 40960)
+AT_RESULT = (45056, 46592, 48128, 47616)
 
 
 def pass_widths(n):
@@ -226,33 +227,43 @@ def tile_picked_hub_silu_e_kernel(tc, xT, w1, w2, w3_words, w3_scales, offs, src
         scalar_fetch(1, 2)
         scalar_fetch(2, len(EDGE_RANGES))
 
-        first = EDGE_RANGES[0][1]
-        sum_tiles = [placed.tile([P, PACK, n], F32, name=f"sums{a}", offset=AT_SUMS[a], align_bytes=64) for a, n in enumerate((first, S - first))]
+        groups = ((0, 1), (1, 3), (3, 4))
+        spans = [(EDGE_RANGES[c0][0], sum(EDGE_RANGES[c1 - 1]) - EDGE_RANGES[c0][0]) for c0, c1 in groups]
+        sum_tiles = {}
 
         def sums(r0, n):
-            return sum_tiles[0][:, :, r0 : r0 + n] if r0 < first else sum_tiles[1][:, :, r0 - first : r0 - first + n]
+            a = max(a for a, span in enumerate(spans) if span[0] <= r0)
+            if a not in sum_tiles:
+                sum_tiles[a] = placed.tile([P, PACK, spans[a][1]], F32, name=f"sums{a}", offset=AT_SUMS[a], align_bytes=64)
+            return sum_tiles[a][:, :, r0 - spans[a][0] : r0 - spans[a][0] + n]
 
         def add_targets(t, r0, n, source):
             nc.vector.tensor_tensor(sums(r0, n)[:, t, :], planes[1, t][:].indirect(entries(dst_t, r0, n)), source, ADD)
 
-        for t in range(2):
-            for r0, n in ((0, first), (first, S - first)):
+        def add_low(r0, n):
+            for t in range(2):
                 add_targets(t, r0, n, whole_sources[t][:, r0 : r0 + n])
-        for c, (r0, n) in enumerate(EDGE_RANGES):
+
+        def add_high(c):
             for t in range(2, PACK):
-                add_targets(t, r0, n, sources[t, c])
+                add_targets(t, *EDGE_RANGES[c], sources[t, c])
 
         z = [keep.tile([P, n, PACK], BF16, name=f"z{c}", align_bytes=64) for c, (r0, n) in enumerate(EDGE_RANGES)]
-        for c, (r0, n) in enumerate(EDGE_RANGES):
-            nc.scalar.activation(z[c][:].rearrange("p (r i) t -> p r t i", i=4), sums(r0, n).rearrange("p t (r i) -> p r t i", i=4), SILU)
-        for c, (r0, n) in enumerate(EDGE_RANGES):
+
+        def silu(c):
+            nc.scalar.activation(z[c][:].rearrange("p (r i) t -> p r t i", i=4), sums(*EDGE_RANGES[c]).rearrange("p t (r i) -> p r t i", i=4), SILU)
+
+        banks = {}
+
+        def second_product(c):
+            r0, n = EDGE_RANGES[c]
             z_codes = keep.tile([P, n], U32, name=f"z_codes{c}", align_bytes=64)
             z_bytes = keep.tile([P, n], U8, name=f"z_bytes{c}", align_bytes=64)
             quantize(z_codes[:], z_bytes[:], z[c][:].rearrange("p r t -> p (r t)"))
-            acc = next_bank(n)
+            banks[c] = next_bank(n)
             for s0, width in pass_widths(n):
                 nc.tensor.matmul_mx(
-                    out=acc[:, s0 : s0 + width],
+                    out=banks[c][:, s0 : s0 + width],
                     lhsT=w3_codes[:].bitcast(FP4X4),
                     lhsT_scale=w3_bytes[:],
                     rhs=z_codes[:, s0 : s0 + width].bitcast(FP8X4),
@@ -260,7 +271,27 @@ def tile_picked_hub_silu_e_kernel(tc, xT, w1, w2, w3_words, w3_scales, offs, src
                     start=True,
                     stop=True,
                 )
-            result = keep.tile([P, n], F32, name=f"result{c}")
-            copy = nc.vector.tensor_copy if c == len(EDGE_RANGES) - 1 else nc.scalar.copy
-            copy(out=result[:], in_=acc[:])
+
+        def store(c, copy):
+            r0, n = EDGE_RANGES[c]
+            result = placed.tile([P, n], F32, name=f"result{c}", offset=AT_RESULT[c], align_bytes=64)
+            copy(out=result[:], in_=banks[c][:])
             nc.sync.dma_start(out=out[:, r0 : r0 + n], in_=result[:])
+
+        for t in range(2):
+            for r0, n in spans[:2]:
+                add_targets(t, r0, n, whole_sources[t][:, r0 : r0 + n])
+        for c in range(3):
+            add_high(c)
+        for c in range(3):
+            silu(c)
+        second_product(0)
+        add_low(*spans[2])
+        add_high(3)
+        store(0, nc.scalar.copy)
+        silu(3)
+        for c in range(1, 4):
+            second_product(c)
+        for c in (1, 2):
+            store(c, nc.scalar.copy)
+        store(3, nc.vector.tensor_copy)

from contextlib import ExitStack

import concourse.mybir as mybir

F32 = mybir.dt.float32
BF16 = mybir.dt.bfloat16
U32 = mybir.dt.uint32
I32 = mybir.dt.int32
U16 = mybir.dt.uint16
U8 = mybir.dt.uint8
FP8X4 = mybir.dt.float8_e4m3fn_x4
FP4X4 = mybir.dt.float4_e2m1fn_x4
ADD = mybir.AluOpType.add
MULT = mybir.AluOpType.mult
COPY = mybir.ActivationFunctionType.Copy
SILU = mybir.ActivationFunctionType.Silu

K, T, S, H, N = 512, 2048, 1024, 512, 128
P = 128
PACK = 4
GROUP = 16
BANKS = 8
FLOPS = 2 * K * H * S * 2 + 2 * H * N * S

LOAD_CUTS = ((0, T), (0, T // 2, T), (0, T // 2, T), (0, 896, 1664, T))
VECTOR_NODES = (352, 352, 384, 256)
ROW0_SCALAR = 704
W1_CUTS = (0, 256, 384, H)
PIECE = 256
HALF = S // 2
VECTOR_TARGETS = 384
EDGE_RANGES = ((0, 384), (384, 256), (640, 256), (896, 128))
AT_W2_ROUNDED = 2048
AT_W2 = 12288
AT_SUMS = (AT_W2 + 64 - 6144, AT_W2 + 64, AT_W2 + 64 - 6144)
AT_RANGE = (28672, 32768, 36864, 40960)
AT_RESULT = (45056, 46592, 48128, 47616)


def pass_widths(n):
    parts = []
    start = 0
    for width in (256, 128):
        if n - start >= width:
            parts.append((start, width))
            start = start + width
    return parts


def tile_picked_hub_silu_e_kernel(tc, xT, w1, w2, w3_words, w3_scales, offs, src, dst, out):
    nc = tc.nc
    with ExitStack() as ctx:
        keep = ctx.enter_context(tc.tile_pool(name="keep", bufs=1))
        placed = ctx.enter_context(tc.tile_pool(name="placed", bufs=1))
        psum = ctx.enter_context(tc.psum_pool(name="psum", bufs=1))

        def entries(list_tile, start, n):
            return list_tile[:, start // GROUP : (start + n) // GROUP]

        warm_in = keep.tile([P, 1], F32, name="warm_in")
        warm_out = keep.tile([P, 1], F32, name="warm_out")
        nc.gpsimd.memset(warm_in[:], 0.0)
        nc.scalar.activation(warm_out[:], warm_in[:], SILU)

        offs_t = keep.tile([P, S // GROUP], U16, name="offs_t")
        src_t = keep.tile([P, S // GROUP], U16, name="src_t")
        dst_t = keep.tile([P, S // GROUP], U16, name="dst_t")
        w3_codes = keep.tile([P, 2 * N], U8, name="w3_codes", align_bytes=64)
        w3_bytes = keep.tile([P, N], U8, name="w3_bytes", align_bytes=64)
        nc.gpsimd.memset(w3_bytes[:], 0)

        x_rows = xT.rearrange("(p j) c -> p j c", j=PACK)
        row_raw = []
        for j in range(PACK):
            row_raw.append(keep.tile([P, T], F32, name=f"row_raw{j}"))
            for lo, hi in zip(LOAD_CUTS[j], LOAD_CUTS[j][1:]):
                nc.sync.dma_start(out=row_raw[j][:, lo:hi], in_=x_rows[:, j, lo:hi])
            if j == 0:
                nc.sync.dma_start(offs_t[:], offs)
        w1_parts = list(zip(W1_CUTS, W1_CUTS[1:]))
        w1_raw = []
        for a, (lo, hi) in enumerate(w1_parts):
            if hi < H:
                w1_raw.append(keep.tile([P, PACK, hi - lo], F32, name=f"w1_raw{a}", align_bytes=64))
            else:
                w1_raw.append(placed.tile([P, PACK, hi - lo], F32, name=f"w1_raw{a}", offset=0, align_bytes=64))
            nc.sync.dma_start(out=w1_raw[a][:], in_=w1.rearrange("(p j) c -> p j c", j=PACK)[:, :, lo:hi])
        w2_raw = placed.tile([P, PACK, H], F32, name="w2_raw", offset=AT_W2, align_bytes=64)
        nc.sync.dma_start(out=w2_raw[:], in_=w2.rearrange("(p j) c -> p j c", j=PACK))
        nc.sync.dma_start(src_t[:], src)
        nc.sync.dma_start(dst_t[:], dst)
        nc.sync.dma_start(out=w3_codes[:].bitcast(I32), in_=w3_words[0].bitcast(I32))
        for q in range(4):
            nc.sync.dma_start(
                out=w3_bytes[32 * q : 32 * q + 4, :].bitcast(I32),
                in_=w3_scales[0, 4 * q : 4 * q + 4, :].bitcast(I32),
            )

        row_rounded = [keep.tile([P, T], BF16, name=f"row_rounded{j}", align_bytes=64) for j in range(PACK)]
        pieces = S // PIECE
        picked = keep.tile([P, S, PACK], BF16, name="picked", align_bytes=64)

        def gpsimd_round(out, in_):
            nc.gpsimd.tensor_scalar(out, in_, 1.0, 0.0, MULT, ADD)

        rounders = (
            (nc.scalar.copy, nc.vector.tensor_copy),
            (gpsimd_round, nc.vector.tensor_copy),
            (gpsimd_round, nc.vector.tensor_copy),
            (gpsimd_round, nc.vector.tensor_copy, gpsimd_round),
        )
        for j in range(PACK):
            round_cuts = LOAD_CUTS[j] if j > 0 else (0, ROW0_SCALAR, T)
            for lo, hi, copy in zip(round_cuts, round_cuts[1:], rounders[j]):
                copy(out=row_rounded[j][:, lo:hi], in_=row_raw[j][:, lo:hi])
            n = VECTOR_NODES[j]
            nc.vector.tensor_copy(picked[:, 0:n, j], row_raw[j][:].indirect(entries(offs_t, 0, n)))
            gather_cuts = range(n, S + 1, PIECE) if j == PACK - 1 else (n, S)
            for lo, hi in zip(gather_cuts, gather_cuts[1:]):
                nc.scalar.activation(picked[:, lo:hi, j], row_rounded[j][:].indirect(entries(offs_t, lo, hi - lo)), COPY)

        def quantize(codes, scale_bytes, values):
            nc.vector.quantize_mx(out=codes.bitcast(FP8X4), scales=scale_bytes, in_=values)

        x_codes = [keep.tile([P, PIECE], U32, name="x_codes0", align_bytes=64)]
        for i in range(1, pieces):
            x_codes.append(placed.tile([P, PIECE], U32, name=f"x_codes{i}", offset=AT_RANGE[i], align_bytes=64))
        x_bytes = [keep.tile([P, PIECE], U8, name="x_bytes0", align_bytes=64)]

        def quantize_nodes(i):
            quantize(x_codes[i][:], x_bytes[i][:], picked[:, i * PIECE : (i + 1) * PIECE, :].rearrange("p c j -> p (c j)"))

        quantize_nodes(0)

        w1_rounded = keep.tile([P, PACK, P, PACK], BF16, name="w1_rounded", align_bytes=64)
        w_codes = {}
        w_bytes = {}

        def quantize_planes(w, t0, t1, rounded):
            codes = keep.tile([P, (t1 - t0) * P], U32, name=f"w_codes{w}_{t0}", align_bytes=64)
            scale_bytes = keep.tile([P, (t1 - t0) * P], U8, name=f"w_bytes{w}_{t0}", align_bytes=64)
            quantize(codes[:], scale_bytes[:], rounded.rearrange("p t m j -> p (t m j)"))
            for t in range(t0, t1):
                w_codes[w, t] = codes[:, (t - t0) * P : (t - t0 + 1) * P]
                w_bytes[w, t] = scale_bytes[:, (t - t0) * P : (t - t0 + 1) * P]

        for a, (lo, hi) in enumerate(w1_parts):
            for t0, t1 in ((0, PACK),) if hi < H else ((0, 2), (2, PACK)):
                nc.vector.tensor_copy(
                    out=w1_rounded[:, t0:t1, lo // PACK : hi // PACK, :].rearrange("p t m j -> p m j t"),
                    in_=w1_raw[a][:].rearrange("p j (m t) -> p m j t", t=PACK)[:, :, :, t0:t1],
                )
        quantize_planes(0, 0, 1, w1_rounded[:, 0:1])
        for i in range(1, pieces):
            x_bytes.append(placed.tile([P, PIECE], U8, name=f"x_bytes{i}", offset=PIECE * i, align_bytes=64))
            quantize_nodes(i)
        quantize_planes(0, 1, 2, w1_rounded[:, 1:2])
        quantize_planes(0, 2, PACK, w1_rounded[:, 2:PACK])

        planes = {(w, t): keep.tile([P, S], F32, name=f"plane{w}_{t}", align_bytes=64) for w in range(2) for t in range(PACK)}
        products = []

        def next_bank(width):
            products.append(width)
            return psum.tile([P, width], F32, name="acc", tag=f"bank{(len(products) - 1) % BANKS}")

        def first_product(w, t, lo, hi, copy=nc.scalar.copy):
            acc = next_bank(hi - lo)
            for i in range(lo // PIECE, (hi - 1) // PIECE + 1):
                a, b = max(lo, i * PIECE), min(hi, (i + 1) * PIECE)
                nc.tensor.matmul_mx(
                    out=acc[:, a - lo : b - lo],
                    lhsT=w_codes[w, t].bitcast(FP8X4),
                    lhsT_scale=w_bytes[w, t],
                    rhs=x_codes[i][:, a - i * PIECE : b - i * PIECE].bitcast(FP8X4),
                    rhs_scale=x_bytes[i][:, a - i * PIECE : b - i * PIECE],
                    start=True,
                    stop=True,
                )
            copy(out=planes[w, t][:, lo:hi], in_=acc[:])

        for i in range(pieces):
            first_product(0, 0, i * PIECE, (i + 1) * PIECE, nc.vector.tensor_copy if i == 0 else nc.scalar.copy)
        for t in range(1, PACK):
            for half in range(2):
                first_product(0, t, half * HALF, (half + 1) * HALF)

        whole_sources = [keep.tile([P, S], F32, name=f"source{t}", align_bytes=64) for t in range(2)]
        sources = {}

        def vector_fetch(t, half):
            r0 = half * HALF
            nc.vector.tensor_copy(whole_sources[t][:, r0 : r0 + HALF], planes[0, t][:].indirect(entries(src_t, r0, HALF)))

        w2_early = placed.tile([P, 2, P, PACK], BF16, name="w2_early", offset=AT_W2_ROUNDED, align_bytes=64)
        nc.vector.tensor_copy(
            out=w2_early[:].rearrange("p t m j -> p m j t"), in_=w2_raw[:].rearrange("p j (m t) -> p m j t", t=PACK)[:, :, :, 0:2]
        )
        vector_fetch(0, 0)
        quantize_planes(1, 0, 2, w2_early[:])
        w2_late = placed.tile([P, 2, P, PACK], BF16, name="w2_late", offset=AT_W2_ROUNDED, align_bytes=64)
        gpsimd_round(out=w2_late[:], in_=w2_raw[:].rearrange("p j (m t) -> p t m j", t=PACK)[:, 2:PACK])
        vector_fetch(0, 1)
        for half in range(2):
            vector_fetch(1, half)
        quantize_planes(1, 2, PACK, w2_late[:])

        def scalar_fetch(c0, c1):
            r0 = EDGE_RANGES[c0][0]
            n = sum(EDGE_RANGES[c1 - 1]) - r0
            for t in range(2, PACK):
                at = AT_RANGE[c0 + min(c0, 1)] + 512 - (4 * n if t == 2 else 0)
                fetched = placed.tile([P, n], F32, name=f"source{t}_{c0}", offset=at, align_bytes=64)
                nc.scalar.activation(fetched[:], planes[0, t][:].indirect(entries(src_t, r0, n)), COPY)
                for c in range(c0, c1):
                    sources[t, c] = fetched[:, EDGE_RANGES[c][0] - r0 : sum(EDGE_RANGES[c]) - r0]

        for t in range(PACK):
            if t == 2:
                scalar_fetch(0, 1)
            first_product(1, t, 0, HALF)
            if t == 1:
                first_product(1, t, HALF, S - VECTOR_TARGETS)
                first_product(1, t, S - VECTOR_TARGETS, S, nc.vector.tensor_copy)
            else:
                first_product(1, t, HALF, S)
        scalar_fetch(1, 2)
        scalar_fetch(2, len(EDGE_RANGES))

        groups = ((0, 1), (1, 3), (3, 4))
        spans = [(EDGE_RANGES[c0][0], sum(EDGE_RANGES[c1 - 1]) - EDGE_RANGES[c0][0]) for c0, c1 in groups]
        sum_tiles = {}

        def sums(r0, n):
            a = max(a for a, span in enumerate(spans) if span[0] <= r0)
            if a not in sum_tiles:
                sum_tiles[a] = placed.tile([P, PACK, spans[a][1]], F32, name=f"sums{a}", offset=AT_SUMS[a], align_bytes=64)
            return sum_tiles[a][:, :, r0 - spans[a][0] : r0 - spans[a][0] + n]

        def add_targets(t, r0, n, source):
            nc.vector.tensor_tensor(sums(r0, n)[:, t, :], planes[1, t][:].indirect(entries(dst_t, r0, n)), source, ADD)

        def add_low(r0, n):
            for t in range(2):
                add_targets(t, r0, n, whole_sources[t][:, r0 : r0 + n])

        def add_high(c):
            for t in range(2, PACK):
                add_targets(t, *EDGE_RANGES[c], sources[t, c])

        z = [keep.tile([P, n, PACK], BF16, name=f"z{c}", align_bytes=64) for c, (r0, n) in enumerate(EDGE_RANGES)]

        def silu(c):
            nc.scalar.activation(z[c][:].rearrange("p (r i) t -> p r t i", i=4), sums(*EDGE_RANGES[c]).rearrange("p t (r i) -> p r t i", i=4), SILU)

        banks = {}

        def second_product(c):
            r0, n = EDGE_RANGES[c]
            z_codes = keep.tile([P, n], U32, name=f"z_codes{c}", align_bytes=64)
            z_bytes = keep.tile([P, n], U8, name=f"z_bytes{c}", align_bytes=64)
            quantize(z_codes[:], z_bytes[:], z[c][:].rearrange("p r t -> p (r t)"))
            banks[c] = next_bank(n)
            for s0, width in pass_widths(n):
                nc.tensor.matmul_mx(
                    out=banks[c][:, s0 : s0 + width],
                    lhsT=w3_codes[:].bitcast(FP4X4),
                    lhsT_scale=w3_bytes[:],
                    rhs=z_codes[:, s0 : s0 + width].bitcast(FP8X4),
                    rhs_scale=z_bytes[:, s0 : s0 + width],
                    start=True,
                    stop=True,
                )

        def store(c, copy):
            r0, n = EDGE_RANGES[c]
            result = placed.tile([P, n], F32, name=f"result{c}", offset=AT_RESULT[c], align_bytes=64)
            copy(out=result[:], in_=banks[c][:])
            nc.sync.dma_start(out=out[:, r0 : r0 + n], in_=result[:])

        for t in range(2):
            for r0, n in spans[:2]:
                add_targets(t, r0, n, whole_sources[t][:, r0 : r0 + n])
        for c in range(3):
            add_high(c)
        for c in range(3):
            silu(c)
        second_product(0)
        add_low(*spans[2])
        add_high(3)
        store(0, nc.scalar.copy)
        silu(3)
        for c in range(1, 4):
            second_product(c)
        for c in (1, 2):
            store(c, nc.scalar.copy)
        store(3, nc.vector.tensor_copy)
